import numpy as np
import ml_dtypes


def mxq(x, axis, fmt="e4m3"):
    dtype, down = {"e4m3": (ml_dtypes.float8_e4m3fn, 7), "e5m2": (ml_dtypes.float8_e5m2, 14)}[fmt]
    v = np.moveaxis(np.asarray(x, np.float32).astype(ml_dtypes.bfloat16).astype(np.float64), axis, -1)
    blocks = v.reshape(v.shape[:-1] + (-1, 32))
    amax = np.abs(blocks).max(-1, keepdims=True)
    byte = np.maximum(np.where(amax > 0, np.frexp(amax)[1] - 1 + 127, 0) - down, 1)
    scale = np.exp2(byte - 127.0)
    codes = (blocks / scale).astype(np.float32).astype(dtype).astype(np.float64)
    return np.moveaxis((codes * scale).reshape(v.shape), -1, axis)


WIDE = False


def mx_kscale(k):
    if not WIDE:
        return np.ones(k)
    levels = np.array([10, -10, 5, -5, 0])
    if k % 512:
        return np.exp2(np.random.permutation(np.resize(levels, k // 32))).repeat(32)
    a = np.empty((k // 512, 16))
    for p in range(k // 512):
        a[p, :8] = np.random.permutation(np.resize(levels, 8))
        for g in range(8):
            far = levels[np.abs(levels - a[p, g]) >= 10]
            a[p, g + 8] = far[np.random.randint(len(far))]
    return np.exp2(a.ravel()).repeat(32)


def f64(x):
    return np.asarray(x).astype(np.float64)


def striped(idx):
    return np.tile(idx.reshape(-1, 16).T, (8, 1)).astype(np.uint16)


def unstriped(offs):
    return offs[:16].T.reshape(-1).astype(np.int64)


E2M1 = np.array([0.0, 0.5, 1.0, 1.5, 2.0, 3.0, 4.0, 6.0, -0.0, -0.5, -1.0, -1.5, -2.0, -3.0, -4.0, -6.0])


def pack_weight(w, fmt):
    k, n = w.shape
    w = f64(np.asarray(w, np.float32).astype(ml_dtypes.bfloat16)).reshape(k // 32, 32, n)
    amax = np.abs(w).max(1)
    if fmt == "e4m3":
        byte = np.frexp(amax)[1] - 1 + 127 - 7
    else:
        mant, ex = np.frexp(amax / 6.0)
        byte = np.where(mant > 0.5, ex, ex - 1) + 127
    byte = np.clip(np.where(amax > 0, byte, 1), 1, 254)
    scaled = (w * np.exp2(127.0 - byte)[:, None, :]).reshape(k, n).astype(np.float32)
    by_word = np.ascontiguousarray(scaled.reshape(k // 512, 128, 4, n).transpose(0, 1, 3, 2))
    if fmt == "e4m3":
        words = by_word.astype(ml_dtypes.float8_e4m3fn).view(np.uint8)
    else:
        c = by_word.astype(ml_dtypes.float4_e2m1fn).view(np.uint8) & 0xF
        words = (c[..., 0::2] | (c[..., 1::2] << 4)).reshape(k // 512, 128, 2 * n)
    return np.ascontiguousarray(words), np.ascontiguousarray(byte.astype(np.uint8).reshape(k // 512, 16, n))


def unpack_weight(words, scales, fmt):
    g, _, n = scales.shape
    words = np.ascontiguousarray(words).reshape(g, 128, n, -1)
    if fmt == "e4m3":
        vals = words.view(ml_dtypes.float8_e4m3fn).astype(np.float64)
    else:
        nib = np.empty((g, 128, n, 4), np.uint8)
        nib[..., 0::2] = words & 0xF
        nib[..., 1::2] = words >> 4
        vals = E2M1[nib]
    vals = vals * np.repeat(np.exp2(scales.astype(np.float64) - 127.0), 8, axis=1)[..., None]
    return vals.transpose(0, 1, 3, 2).reshape(g * 512, n)


def silu(v):
    return v / (1.0 + np.exp(-np.maximum(v, -700.0)))


K, T, E, C, H, N = 1024, 768, 6, 256, 512, 128


def by_expert(wq, xq):
    return np.concatenate([wq[e].T @ xq[:, e * C:(e + 1) * C] for e in range(E)], axis=1)


def setup_inputs():
    n = np.random.standard_normal
    s = mx_kscale(K)[:, None]
    u = mx_kscale(H)
    first = np.random.permutation(np.repeat(np.arange(E), T // E))
    second = (first + 1 + np.random.permutation(np.repeat(np.arange(E - 1), -(-T // (E - 1)))[:T])) % E
    while np.bincount(second, minlength=E).max() != T // E:
        load = np.bincount(second, minlength=E); hi, lo = int(load.argmax()), int(load.argmin())
        t = np.flatnonzero((second == hi) & (first != lo))[0]; second[t] = lo
    slot_token = np.empty(E * C, np.int64); pos = np.empty((2, T), np.int64); fill = np.zeros(E, np.int64)
    place = np.stack([np.random.permutation(C) for _ in range(E)])
    for r, deal in enumerate((first, second)):
        for t in np.random.permutation(T):
            e = deal[t]; j = e * C + place[e, fill[e]]; fill[e] += 1; slot_token[j] = t; pos[r, t] = j
    g = np.random.uniform(0.2, 0.8, T)
    x = pack_weight(n((K, T)) * s, "e4m3")
    return {
        "x_words": x[0],
        "x_scales": x[1],
        "w1": (n((E + 1, K, H)) / np.sqrt(K) / s[None]).astype(np.float32),
        "w3": (n((E + 1, K, H)) / np.sqrt(K) / s[None] * u[None, None, :]).astype(np.float32),
        "w2": (n((E + 1, H, N)) / np.sqrt(H) / u[None, :, None]).astype(np.float32),
        "gate": np.stack([np.tile(g, (N, 1)), np.tile(1.0 - g, (N, 1))]).astype(np.float32),
        "offs": striped(slot_token),
        "pos1": striped(pos[0]),
        "pos2": striped(pos[1]),
    }


def reference(x_words, x_scales, w1, w3, w2, gate, offs, pos1, pos2):
    idx = unstriped(offs)
    w1q, w3q, w2q = mxq(f64(w1), 1, "e4m3"), mxq(f64(w3), 1, "e4m3"), mxq(f64(w2), 1, "e4m3")
    xs = unpack_weight(x_words, x_scales, "e4m3")
    hs = silu(w1q[E].T @ xs) * (w3q[E].T @ xs)
    ys = w2q[E].T @ mxq(hs, 0, "e4m3")
    xq = unpack_weight(x_words, x_scales, "e4m3")[:, idx]
    h = silu(by_expert(w1q, xq))
    h = h * by_expert(w3q, xq)
    y = by_expert(w2q, mxq(h, 0, "e4m3"))
    return ys + f64(gate[0]) * y[:, unstriped(pos1)] + f64(gate[1]) * y[:, unstriped(pos2)]

@@ -1,0 +1,257 @@
+from contextlib import ExitStack
+
+import concourse.mybir as mybir
+
+K, T, E, C, H, N = 1024, 768, 6, 256, 512, 128
+FLOPS = 2 * (E * C + T) * (2 * K * H + H * N)
+
+F32 = mybir.dt.float32
+BF16 = mybir.dt.bfloat16
+I32 = mybir.dt.int32
+U32 = mybir.dt.uint32
+U16 = mybir.dt.uint16
+U8 = mybir.dt.uint8
+FP8X4 = mybir.dt.float8_e4m3fn_x4
+MULT = mybir.AluOpType.mult
+ADD = mybir.AluOpType.add
+SILU = mybir.ActivationFunctionType.Silu
+
+P = 128
+PACK = 4
+K_PASS = P * PACK
+PASSES = K // K_PASS
+SUB = 128
+LIST_COLS = C // 16
+A1_BANKS = 4
+
+FIRST_ENGINES = ("ss", "ss", "ss", "ss")
+ROUTED_ENGINES = ("sv", "sv", "sv", "sv")
+SHARED_ENGINES = ("ss", "sv", "ss", "sv")
+
+
+def tile_moe_shr_glu_silu_kernel(
+    tc, x_words, x_scales, w1, w3, w2, gate, offs, pos1, pos2, out
+):
+    nc = tc.nc
+
+    with ExitStack() as ctx:
+        keep = ctx.enter_context(tc.tile_pool(name="keep", bufs=1))
+        raw_pool = ctx.enter_context(tc.tile_pool(name="raw", bufs=14))
+        raw2_pool = ctx.enter_context(tc.tile_pool(name="raw2", bufs=3))
+        rounded_pool = ctx.enter_context(tc.tile_pool(name="rounded", bufs=5))
+        codes_pool = ctx.enter_context(tc.tile_pool(name="codes", bufs=8))
+        small_pool = ctx.enter_context(tc.tile_pool(name="small", bufs=3))
+        silu_pool = ctx.enter_context(tc.tile_pool(name="silu", bufs=2))
+        psum_a1 = ctx.enter_context(tc.psum_pool(name="psum_a1", bufs=A1_BANKS))
+        psum_a3 = ctx.enter_context(tc.psum_pool(name="psum_a3", bufs=3))
+        psum_y = ctx.enter_context(tc.psum_pool(name="psum_y", bufs=1))
+
+        token_scales = keep.tile([P, T], U8, name="token_scales", align_bytes=64)
+        nc.vector.memset(token_scales[:].bitcast(I32), 0)
+        token_words = [
+            keep.tile([P, T], U32, name=f"token_words{o}", align_bytes=64) for o in range(PASSES)
+        ]
+
+        def load_words(o):
+            nc.sync.dma_start(
+                token_words[o][:].bitcast(I32),
+                x_words[o].rearrange("p t r -> p (t r)").bitcast(I32),
+            )
+
+        load_words(0)
+        offs_sb = keep.tile([P, E * LIST_COLS], U16, name="offs_sb")
+        nc.sync.dma_start(offs_sb[:], offs)
+        for q in range(4):
+            nc.sync.dma_start(
+                token_scales[32 * q : 32 * q + 4 * PASSES, :].bitcast(I32),
+                x_scales[:, 4 * q : 4 * q + 4, :].bitcast(I32),
+            )
+        load_words(1)
+
+        def copy_on(letter, dst, src):
+            if letter == "s":
+                nc.scalar.copy(dst, src)
+            else:
+                nc.vector.tensor_copy(dst, src)
+
+        def load_pass(w, e, o):
+            raw = raw_pool.tile([P, PACK, H], F32, name="raw")
+            nc.sync.dma_start(
+                raw[:], w[e, o * K_PASS : (o + 1) * K_PASS, :].rearrange("(p j) c -> p j c", j=PACK)
+            )
+            return raw
+
+        def rounded_tile():
+            return rounded_pool.tile([P, PACK, P, PACK], BF16, name="rounded", align_bytes=64)
+
+        def quantize_pass(raw, letters, rounded=None):
+            if rounded is None:
+                rounded = rounded_tile()
+            src = raw[:].rearrange("p j (m t) -> p m j t", t=PACK)
+            dst = rounded[:].rearrange("p t m j -> p m j t")
+            for half, letter in enumerate(letters):
+                pair = slice(2 * half, 2 * half + 2)
+                copy_on(letter, dst[:, :, :, pair], src[:, :, :, pair])
+            codes = codes_pool.tile([P, H], U32, name="codes", align_bytes=64)
+            scales = codes_pool.tile([P, H], U8, name="scales", align_bytes=64)
+            nc.vector.quantize_mx(
+                out=codes[:].bitcast(FP8X4),
+                scales=scales[:],
+                in_=rounded[:].rearrange("p t m j -> p (t m j)"),
+            )
+            return codes, scales
+
+        def load_w2(e):
+            raw2 = raw2_pool.tile([P, PACK, N], F32, name="raw2")
+            nc.sync.dma_start(raw2[:], w2[e].rearrange("(p j) n -> p j n", j=PACK))
+            return raw2
+
+        def quantize_w2(raw2):
+            rounded2 = small_pool.tile([P, N, PACK], BF16, name="rounded2", align_bytes=64)
+            nc.vector.tensor_copy(
+                rounded2[:].rearrange("p (c i) j -> p c j i", i=4),
+                raw2[:].rearrange("p j (c i) -> p c j i", i=4),
+            )
+            codes2 = small_pool.tile([P, N], U32, name="codes2", align_bytes=64)
+            scales2 = small_pool.tile([P, N], U8, name="scales2", align_bytes=64)
+            nc.vector.quantize_mx(
+                out=codes2[:].bitcast(FP8X4),
+                scales=scales2[:],
+                in_=rounded2[:].rearrange("p n j -> p (n j)"),
+            )
+            return codes2, scales2
+
+        def first_layer(weights, words, scales, cols, pool):
+            acc = pool.tile([P, PACK, SUB], F32, name="acc")
+            for t in range(PACK):
+                for o in range(PASSES):
+                    w_codes, w_scales = weights[o]
+                    nc.tensor.matmul_mx(
+                        out=acc[:, t, :],
+                        lhsT=w_codes[:, t * P : (t + 1) * P].bitcast(FP8X4),
+                        lhsT_scale=w_scales[:, t * P : (t + 1) * P],
+                        rhs=words[o][:, cols].bitcast(FP8X4),
+                        rhs_scale=scales[4 * o : P, cols],
+                        start=(o == 0),
+                        stop=(o == PASSES - 1),
+                    )
+            return acc
+
+        def second_layer(weights3, weights2, words, scales, first_col, silus):
+            h = small_pool.tile([P, C, PACK], BF16, name="h", align_bytes=64)
+            for b, s in enumerate(silus):
+                cols = slice(first_col + b * SUB, first_col + (b + 1) * SUB)
+                acc = first_layer(weights3, words, scales, cols, psum_a3)
+                nc.vector.tensor_tensor(
+                    h[:, b * SUB : (b + 1) * SUB, :], acc[:].rearrange("p t n -> p n t"), s, MULT
+                )
+            h_codes = small_pool.tile([P, C], U32, name="h_codes", align_bytes=64)
+            h_scales = small_pool.tile([P, C], U8, name="h_scales", align_bytes=64)
+            nc.vector.quantize_mx(
+                out=h_codes[:].bitcast(FP8X4),
+                scales=h_scales[:],
+                in_=h[:].rearrange("p n t -> p (n t)"),
+            )
+            y_acc = psum_y.tile([P, C], F32, name="y_acc")
+            codes2, scales2 = weights2
+            nc.tensor.matmul_mx(
+                out=y_acc[:],
+                lhsT=codes2[:].bitcast(FP8X4),
+                lhsT_scale=scales2[:],
+                rhs=h_codes[:].bitcast(FP8X4),
+                rhs_scale=h_scales[:],
+                start=True,
+                stop=True,
+            )
+            return y_acc
+
+        y_slots = keep.tile([P, E * C], F32, name="y_slots")
+
+        for e in range(E):
+            mine = offs_sb[:, e * LIST_COLS : (e + 1) * LIST_COLS]
+            slot_words = []
+            for o in range(PASSES):
+                gathered = keep.tile([P, C], U32, name=f"slot_words{e}_{o}", align_bytes=64)
+                nc.vector.tensor_copy(gathered[:], token_words[o][:].indirect(mine))
+                slot_words.append(gathered)
+            slot_scales = keep.tile([P, C], U8, name=f"slot_scales{e}", align_bytes=64)
+            nc.vector.tensor_copy(slot_scales[:], token_scales[:].indirect(mine))
+
+            letters = FIRST_ENGINES if e == 0 else ROUTED_ENGINES
+            weights1 = [quantize_pass(load_pass(w1, e, o), letters[o]) for o in range(PASSES)]
+            accs = [
+                first_layer(weights1, slot_words, slot_scales, slice(b * SUB, (b + 1) * SUB), psum_a1)
+                for b in range(C // SUB)
+            ]
+            weights3 = [quantize_pass(load_pass(w3, e, 0), letters[2])]
+            weights2 = quantize_w2(load_w2(e))
+            last_raw = load_pass(w3, e, 1)
+            weights3.append(quantize_pass(last_raw, letters[3]))
+            silus = []
+            for b, acc in enumerate(accs):
+                s = last_raw[:, b, :].rearrange("p (n t) -> p n t", t=PACK)
+                nc.scalar.activation(s, acc[:].rearrange("p t n -> p n t"), SILU)
+                silus.append(s)
+            y_acc = second_layer(weights3, weights2, slot_words, slot_scales, 0, silus)
+            nc.scalar.copy(y_slots[:, e * C : (e + 1) * C], y_acc[:])
+
+        pos_sb = []
+        gate_sb = []
+        for r, pos in enumerate((pos1, pos2)):
+            lst = keep.tile([P, T // 16], U16, name=f"pos_sb{r}")
+            nc.sync.dma_start(lst[:], pos)
+            pos_sb.append(lst)
+        weights1 = [quantize_pass(load_pass(w1, E, o), SHARED_ENGINES[o]) for o in range(PASSES)]
+        for r in range(2):
+            g = keep.tile([P, T], F32, name=f"gate_sb{r}")
+            nc.sync.dma_start(g[:], gate[r])
+            gate_sb.append(g)
+
+        def shared_a1(b):
+            return first_layer(
+                weights1, token_words, token_scales, slice(b * SUB, (b + 1) * SUB), psum_a1
+            )
+
+        accs = [shared_a1(b) for b in range(A1_BANKS)]
+        weights3 = [quantize_pass(load_pass(w3, E, 0), SHARED_ENGINES[2])]
+        last_raw = load_pass(w3, E, 1)
+        last_rounded = rounded_tile()
+        weights3.append(quantize_pass(last_raw, SHARED_ENGINES[3], last_rounded))
+        silus = []
+        for b in range(T // SUB):
+            if b < A1_BANKS:
+                acc = accs[b]
+                s = last_raw[:, b, :].rearrange("p (n t) -> p n t", t=PACK)
+            else:
+                acc = shared_a1(b)
+                s = silu_pool.tile([P, SUB, PACK], F32, name="s")[:]
+            nc.scalar.activation(s, acc[:].rearrange("p t n -> p n t"), SILU)
+            silus.append(s)
+        weights2 = quantize_w2(load_w2(E))
+
+        routed = []
+        for c in range(T // C):
+            cols = slice(c * C, (c + 1) * C)
+            picks = []
+            for r in range(2):
+                if c == T // C - 1:
+                    pick = last_rounded[:, r, :, :].rearrange("p m j -> p (m j)").bitcast(F32)
+                else:
+                    pick = small_pool.tile([P, C], F32, name=f"pick{r}")[:]
+                nc.vector.tensor_tensor(
+                    pick,
+                    y_slots[:].indirect(pos_sb[r][:, c * LIST_COLS : (c + 1) * LIST_COLS]),
+                    gate_sb[r][:, cols],
+                    MULT,
+                )
+                picks.append(pick)
+            both = small_pool.tile([P, C], F32, name="both")
+            nc.vector.tensor_tensor(both[:], picks[0], picks[1], ADD)
+            routed.append(both)
+
+        for c in range(T // C):
+            pair = silus[c * (C // SUB) : (c + 1) * (C // SUB)]
+            y_acc = second_layer(weights3, weights2, token_words, token_scales, c * C, pair)
+            result = small_pool.tile([P, C], F32, name="result")
+            nc.vector.tensor_tensor(result[:], y_acc[:], routed[c][:], ADD)
+            nc.sync.dma_start(out[:, c * C : (c + 1) * C], result[:])

@@ -26,7 +26,8 @@ A1_BANKS = 4
 
 FIRST_ENGINES = ("ss", "ss", "ss", "ss")
 ROUTED_ENGINES = ("sv", "sv", "sv", "sv")
-SHARED_ENGINES = ("ss", "sv", "ss", "sv")
+SHARED_ENGINES = ("ss", "ss", "sv")
+WHOLE_LOADS = 4
 
 
 def tile_moe_shr_glu_silu_kernel(
@@ -36,8 +37,7 @@ def tile_moe_shr_glu_silu_kernel(
 
     with ExitStack() as ctx:
         keep = ctx.enter_context(tc.tile_pool(name="keep", bufs=1))
-        raw_pool = ctx.enter_context(tc.tile_pool(name="raw", bufs=14))
-        raw2_pool = ctx.enter_context(tc.tile_pool(name="raw2", bufs=3))
+        raw_pool = ctx.enter_context(tc.tile_pool(name="raw", bufs=7))
         rounded_pool = ctx.enter_context(tc.tile_pool(name="rounded", bufs=5))
         codes_pool = ctx.enter_context(tc.tile_pool(name="codes", bufs=8))
         small_pool = ctx.enter_context(tc.tile_pool(name="small", bufs=3))
@@ -74,26 +74,31 @@ def tile_moe_shr_glu_silu_kernel(
             else:
                 nc.vector.tensor_copy(dst, src)
 
-        def load_pass(w, e, o):
-            raw = raw_pool.tile([P, PACK, H], F32, name="raw")
-            nc.sync.dma_start(
-                raw[:], w[e, o * K_PASS : (o + 1) * K_PASS, :].rearrange("(p j) c -> p j c", j=PACK)
-            )
-            return raw
+        def raw_tile():
+            return raw_pool.tile([P, PASSES, PACK, H], F32, name="raw")
+
+        def by_pass(matrix):
+            return matrix.rearrange("(o p j) c -> p o j c", o=PASSES, j=PACK)
 
         def rounded_tile():
             return rounded_pool.tile([P, PACK, P, PACK], BF16, name="rounded", align_bytes=64)
 
-        def quantize_pass(raw, letters, rounded=None):
-            if rounded is None:
-                rounded = rounded_tile()
-            src = raw[:].rearrange("p j (m t) -> p m j t", t=PACK)
+        def code_tiles():
+            codes = codes_pool.tile([P, H], U32, name="codes", align_bytes=64)
+            scales = codes_pool.tile([P, H], U8, name="scales", align_bytes=64)
+            return codes, scales
+
+        def round_columns(rounded, raw_pass, letters, ms):
+            src = raw_pass.rearrange("p j (m t) -> p m j t", t=PACK)
             dst = rounded[:].rearrange("p t m j -> p m j t")
             for half, letter in enumerate(letters):
                 pair = slice(2 * half, 2 * half + 2)
-                copy_on(letter, dst[:, :, :, pair], src[:, :, :, pair])
-            codes = codes_pool.tile([P, H], U32, name="codes", align_bytes=64)
-            scales = codes_pool.tile([P, H], U8, name="scales", align_bytes=64)
+                copy_on(letter, dst[:, ms, :, pair], src[:, ms, :, pair])
+
+        def quantize_pass(raw_pass, letters):
+            rounded = rounded_tile()
+            round_columns(rounded, raw_pass, letters, slice(0, P))
+            codes, scales = code_tiles()
             nc.vector.quantize_mx(
                 out=codes[:].bitcast(FP8X4),
                 scales=scales[:],
@@ -101,16 +106,43 @@ def tile_moe_shr_glu_silu_kernel(
             )
             return codes, scales
 
-        def load_w2(e):
-            raw2 = raw2_pool.tile([P, PACK, N], F32, name="raw2")
-            nc.sync.dma_start(raw2[:], w2[e].rearrange("(p j) n -> p j n", j=PACK))
-            return raw2
+        def load_and_quantize(matrix, letters, whole):
+            raw = raw_tile()
+            if whole:
+                nc.sync.dma_start(raw[:], by_pass(matrix))
+            quantized = []
+            for o in range(PASSES):
+                if not whole:
+                    nc.sync.dma_start(raw[:, o], by_pass(matrix)[:, o])
+                quantized.append(quantize_pass(raw[:, o], letters[o]))
+            return raw, quantized
 
-        def quantize_w2(raw2):
+        def load_and_quantize_finely(matrix, letters):
+            raw = raw_tile()
+            nc.sync.dma_start(raw[:, 0], by_pass(matrix)[:, 0])
+            quantized = [quantize_pass(raw[:, 0], letters)]
+            rounded = rounded_tile()
+            for half in range(2):
+                cols = slice(half * H // 2, (half + 1) * H // 2)
+                nc.sync.dma_start(raw[:, 1, :, cols], by_pass(matrix)[:, 1, :, cols])
+                round_columns(rounded, raw[:, 1], "vs", slice(half * P // 2, (half + 1) * P // 2))
+            codes, scales = code_tiles()
+            for half in range(2):
+                cols = slice(half * H // 2, (half + 1) * H // 2)
+                nc.vector.quantize_mx(
+                    out=codes[:, cols].bitcast(FP8X4),
+                    scales=scales[:, cols],
+                    in_=rounded[:, 2 * half : 2 * half + 2].rearrange("p t m j -> p (t m j)"),
+                )
+            quantized.append((codes, scales))
+            return raw, quantized, rounded
+
+        def quantize_w2(raw2, letter):
             rounded2 = small_pool.tile([P, N, PACK], BF16, name="rounded2", align_bytes=64)
-            nc.vector.tensor_copy(
+            copy_on(
+                letter,
                 rounded2[:].rearrange("p (c i) j -> p c j i", i=4),
-                raw2[:].rearrange("p j (c i) -> p c j i", i=4),
+                raw2.rearrange("p j (c i) -> p c j i", i=4),
             )
             codes2 = small_pool.tile([P, N], U32, name="codes2", align_bytes=64)
             scales2 = small_pool.tile([P, N], U8, name="scales2", align_bytes=64)
@@ -166,6 +198,9 @@ def tile_moe_shr_glu_silu_kernel(
             return y_acc
 
         y_slots = keep.tile([P, E * C], F32, name="y_slots")
+        w2_raw = keep.tile([P, E + 1, PACK, N], F32, name="w2_raw")
+        w2_rows = w2.rearrange("e (p j) n -> p e j n", j=PACK)
+        pos_sb = [keep.tile([P, T // 16], U16, name=f"pos_sb{r}") for r in range(2)]
 
         for e in range(E):
             mine = offs_sb[:, e * LIST_COLS : (e + 1) * LIST_COLS]
@@ -178,30 +213,30 @@ def tile_moe_shr_glu_silu_kernel(
             nc.vector.tensor_copy(slot_scales[:], token_scales[:].indirect(mine))
 
             letters = FIRST_ENGINES if e == 0 else ROUTED_ENGINES
-            weights1 = [quantize_pass(load_pass(w1, e, o), letters[o]) for o in range(PASSES)]
+            weights1 = load_and_quantize(w1[e], letters[:2], 0 < e < WHOLE_LOADS)[1]
             accs = [
                 first_layer(weights1, slot_words, slot_scales, slice(b * SUB, (b + 1) * SUB), psum_a1)
                 for b in range(C // SUB)
             ]
-            weights3 = [quantize_pass(load_pass(w3, e, 0), letters[2])]
-            weights2 = quantize_w2(load_w2(e))
-            last_raw = load_pass(w3, e, 1)
-            weights3.append(quantize_pass(last_raw, letters[3]))
+            if e < E - 1:
+                raw3, weights3 = load_and_quantize(w3[e], letters[2:], e < WHOLE_LOADS)
+            else:
+                raw3, weights3 = load_and_quantize_finely(w3[e], letters[2])[:2]
+            if e == 0:
+                nc.sync.dma_start(w2_raw[:, :E], w2_rows[:, :E])
+                nc.sync.dma_start(pos_sb[0][:], pos1)
+                nc.sync.dma_start(pos_sb[1][:], pos2)
+            weights2 = quantize_w2(w2_raw[:, e], "v")
             silus = []
             for b, acc in enumerate(accs):
-                s = last_raw[:, b, :].rearrange("p (n t) -> p n t", t=PACK)
+                s = raw3[:, 1, b, :].rearrange("p (n t) -> p n t", t=PACK)
                 nc.scalar.activation(s, acc[:].rearrange("p t n -> p n t"), SILU)
                 silus.append(s)
             y_acc = second_layer(weights3, weights2, slot_words, slot_scales, 0, silus)
-            nc.scalar.copy(y_slots[:, e * C : (e + 1) * C], y_acc[:])
+            copy_on("v" if e < E - 1 else "s", y_slots[:, e * C : (e + 1) * C], y_acc[:])
 
-        pos_sb = []
         gate_sb = []
-        for r, pos in enumerate((pos1, pos2)):
-            lst = keep.tile([P, T // 16], U16, name=f"pos_sb{r}")
-            nc.sync.dma_start(lst[:], pos)
-            pos_sb.append(lst)
-        weights1 = [quantize_pass(load_pass(w1, E, o), SHARED_ENGINES[o]) for o in range(PASSES)]
+        weights1 = load_and_quantize(w1[E], SHARED_ENGINES[:2], False)[1]
         for r in range(2):
             g = keep.tile([P, T], F32, name=f"gate_sb{r}")
             nc.sync.dma_start(g[:], gate[r])
@@ -213,21 +248,19 @@ def tile_moe_shr_glu_silu_kernel(
             )
 
         accs = [shared_a1(b) for b in range(A1_BANKS)]
-        weights3 = [quantize_pass(load_pass(w3, E, 0), SHARED_ENGINES[2])]
-        last_raw = load_pass(w3, E, 1)
-        last_rounded = rounded_tile()
-        weights3.append(quantize_pass(last_raw, SHARED_ENGINES[3], last_rounded))
+        raw3, weights3, last_rounded = load_and_quantize_finely(w3[E], SHARED_ENGINES[2])
         silus = []
         for b in range(T // SUB):
             if b < A1_BANKS:
                 acc = accs[b]
-                s = last_raw[:, b, :].rearrange("p (n t) -> p n t", t=PACK)
+                s = raw3[:, 1, b, :].rearrange("p (n t) -> p n t", t=PACK)
             else:
                 acc = shared_a1(b)
                 s = silu_pool.tile([P, SUB, PACK], F32, name="s")[:]
             nc.scalar.activation(s, acc[:].rearrange("p t n -> p n t"), SILU)
             silus.append(s)
-        weights2 = quantize_w2(load_w2(E))
+        nc.sync.dma_start(w2_raw[:, E], w2_rows[:, E])
+        weights2 = quantize_w2(w2_raw[:, E], "s")
 
         routed = []
         for c in range(T // C):
@@ -235,7 +268,7 @@ def tile_moe_shr_glu_silu_kernel(
             picks = []
             for r in range(2):
                 if c == T // C - 1:
-                    pick = last_rounded[:, r, :, :].rearrange("p m j -> p (m j)").bitcast(F32)
+                    pick = last_rounded[:, 2 + r, :, :].rearrange("p m j -> p (m j)").bitcast(F32)
                 else:
                     pick = small_pool.tile([P, C], F32, name=f"pick{r}")[:]
                 nc.vector.tensor_tensor(

@@ -46,27 +46,21 @@ def tile_moe_shr_glu_silu_kernel(
         psum_a3 = ctx.enter_context(tc.psum_pool(name="psum_a3", bufs=3))
         psum_y = ctx.enter_context(tc.psum_pool(name="psum_y", bufs=1))
 
-        token_scales = keep.tile([P, T], U8, name="token_scales", align_bytes=64)
+        token_scales = keep.tile([P, T], U8, name="token_scales", align_bytes=256)
         nc.vector.memset(token_scales[:].bitcast(I32), 0)
-        token_words = [
-            keep.tile([P, T], U32, name=f"token_words{o}", align_bytes=64) for o in range(PASSES)
-        ]
-
-        def load_words(o):
-            nc.sync.dma_start(
-                token_words[o][:].bitcast(I32),
-                x_words[o].rearrange("p t r -> p (t r)").bitcast(I32),
-            )
-
-        load_words(0)
-        offs_sb = keep.tile([P, E * LIST_COLS], U16, name="offs_sb")
+        all_words = keep.tile([P, PASSES, T], U32, name="all_words", align_bytes=256)
+        nc.sync.dma_start(
+            all_words[:].bitcast(I32),
+            x_words.rearrange("o p t r -> p o (t r)").bitcast(I32),
+        )
+        token_words = [all_words[:, o, :] for o in range(PASSES)]
+        offs_sb = keep.tile([P, E * LIST_COLS], U16, name="offs_sb", align_bytes=256)
         nc.sync.dma_start(offs_sb[:], offs)
         for q in range(4):
             nc.sync.dma_start(
                 token_scales[32 * q : 32 * q + 4 * PASSES, :].bitcast(I32),
                 x_scales[:, 4 * q : 4 * q + 4, :].bitcast(I32),
             )
-        load_words(1)
 
         def copy_on(letter, dst, src):
             if letter == "s":
@@ -75,7 +69,7 @@ def tile_moe_shr_glu_silu_kernel(
                 nc.vector.tensor_copy(dst, src)
 
         def raw_tile():
-            return raw_pool.tile([P, PASSES, PACK, H], F32, name="raw")
+            return raw_pool.tile([P, PASSES, PACK, H], F32, name="raw", align_bytes=256)
 
         def by_pass(matrix):
             return matrix.rearrange("(o p j) c -> p o j c", o=PASSES, j=PACK)
@@ -198,22 +192,22 @@ def tile_moe_shr_glu_silu_kernel(
             return y_acc
 
         y_slots = keep.tile([P, E * C], F32, name="y_slots")
-        w2_raw = keep.tile([P, E + 1, PACK, N], F32, name="w2_raw")
+        w2_raw = keep.tile([P, E + 1, PACK, N], F32, name="w2_raw", align_bytes=256)
         w2_rows = w2.rearrange("e (p j) n -> p e j n", j=PACK)
-        pos_sb = [keep.tile([P, T // 16], U16, name=f"pos_sb{r}") for r in range(2)]
+        pos_sb = [keep.tile([P, T // 16], U16, name=f"pos_sb{r}", align_bytes=256) for r in range(2)]
 
         for e in range(E):
             mine = offs_sb[:, e * LIST_COLS : (e + 1) * LIST_COLS]
             slot_words = []
             for o in range(PASSES):
                 gathered = keep.tile([P, C], U32, name=f"slot_words{e}_{o}", align_bytes=64)
-                nc.vector.tensor_copy(gathered[:], token_words[o][:].indirect(mine))
+                nc.vector.tensor_copy(gathered[:], token_words[o].indirect(mine))
                 slot_words.append(gathered)
             slot_scales = keep.tile([P, C], U8, name=f"slot_scales{e}", align_bytes=64)
             nc.vector.tensor_copy(slot_scales[:], token_scales[:].indirect(mine))
 
             letters = FIRST_ENGINES if e == 0 else ROUTED_ENGINES
-            weights1 = load_and_quantize(w1[e], letters[:2], 0 < e < WHOLE_LOADS)[1]
+            weights1 = load_and_quantize(w1[e], letters[:2], e < WHOLE_LOADS)[1]
             accs = [
                 first_layer(weights1, slot_words, slot_scales, slice(b * SUB, (b + 1) * SUB), psum_a1)
                 for b in range(C // SUB)
@@ -238,7 +232,7 @@ def tile_moe_shr_glu_silu_kernel(
         gate_sb = []
         weights1 = load_and_quantize(w1[E], SHARED_ENGINES[:2], False)[1]
         for r in range(2):
-            g = keep.tile([P, T], F32, name=f"gate_sb{r}")
+            g = keep.tile([P, T], F32, name=f"gate_sb{r}", align_bytes=256)
             nc.sync.dma_start(g[:], gate[r])
             gate_sb.append(g)
 
@@ -285,6 +279,6 @@ def tile_moe_shr_glu_silu_kernel(
         for c in range(T // C):
             pair = silus[c * (C // SUB) : (c + 1) * (C // SUB)]
             y_acc = second_layer(weights3, weights2, token_words, token_scales, c * C, pair)
-            result = small_pool.tile([P, C], F32, name="result")
+            result = small_pool.tile([P, C], F32, name="result", align_bytes=256)
             nc.vector.tensor_tensor(result[:], y_acc[:], routed[c][:], ADD)
             nc.sync.dma_start(out[:, c * C : (c + 1) * C], result[:])

@@ -18,80 +18,74 @@ SILU = mybir.ActivationFunctionType.Silu
 
 P = 128
 PACK = 4
-K_PASS = P * PACK
-PASSES = K // K_PASS
-SUB = 128
+PASSES = K // (P * PACK)
+GROUP = 128
 LIST_COLS = C // 16
-A1_BANKS = 4
+SHARED = E
+LAST_ROUTED = E - 1
 
-FIRST_ENGINES = ("ss", "ss", "ss", "ss")
-ROUTED_ENGINES = ("sv", "sv", "sv", "sv")
-SHARED_ENGINES = ("ss", "ss", "sv")
+MX_ALIGN = 64
+DMA_ALIGN = 256
+
+A1_BANKS, A3_BANKS, Y_BANKS = 4, 3, 1
+
 WHOLE_LOADS = 4
+
+SHARED_RANGES = ((0, 2), (2, 4), (4, 5), (5, 6))
 
 
 def tile_moe_shr_glu_silu_kernel(
     tc, x_words, x_scales, w1, w3, w2, gate, offs, pos1, pos2, out
 ):
     nc = tc.nc
+    on_scalar, on_vector = nc.scalar.copy, nc.vector.tensor_copy
 
     with ExitStack() as ctx:
         keep = ctx.enter_context(tc.tile_pool(name="keep", bufs=1))
         raw_pool = ctx.enter_context(tc.tile_pool(name="raw", bufs=7))
         rounded_pool = ctx.enter_context(tc.tile_pool(name="rounded", bufs=5))
         codes_pool = ctx.enter_context(tc.tile_pool(name="codes", bufs=8))
-        small_pool = ctx.enter_context(tc.tile_pool(name="small", bufs=3))
-        silu_pool = ctx.enter_context(tc.tile_pool(name="silu", bufs=2))
+        small_pool = ctx.enter_context(tc.tile_pool(name="small", bufs=T // C))
+        silu_pool = ctx.enter_context(tc.tile_pool(name="silu", bufs=T // GROUP - A1_BANKS))
         psum_a1 = ctx.enter_context(tc.psum_pool(name="psum_a1", bufs=A1_BANKS))
-        psum_a3 = ctx.enter_context(tc.psum_pool(name="psum_a3", bufs=3))
-        psum_y = ctx.enter_context(tc.psum_pool(name="psum_y", bufs=1))
+        psum_a3 = ctx.enter_context(tc.psum_pool(name="psum_a3", bufs=A3_BANKS))
+        psum_y = ctx.enter_context(tc.psum_pool(name="psum_y", bufs=Y_BANKS))
 
-        token_scales = keep.tile([P, T], U8, name="token_scales", align_bytes=256)
+        token_scales = keep.tile([P, T], U8, name="token_scales", align_bytes=DMA_ALIGN)
         nc.vector.memset(token_scales[:].bitcast(I32), 0)
-        all_words = keep.tile([P, PASSES, T], U32, name="all_words", align_bytes=256)
+        all_words = keep.tile([P, PASSES, T], U32, name="all_words", align_bytes=DMA_ALIGN)
         nc.sync.dma_start(
             all_words[:].bitcast(I32),
             x_words.rearrange("o p t r -> p o (t r)").bitcast(I32),
         )
         token_words = [all_words[:, o, :] for o in range(PASSES)]
-        offs_sb = keep.tile([P, E * LIST_COLS], U16, name="offs_sb", align_bytes=256)
+        offs_sb = keep.tile([P, E * LIST_COLS], U16, name="offs_sb", align_bytes=DMA_ALIGN)
         nc.sync.dma_start(offs_sb[:], offs)
-        for q in range(4):
-            nc.sync.dma_start(
-                token_scales[32 * q : 32 * q + 4 * PASSES, :].bitcast(I32),
-                x_scales[:, 4 * q : 4 * q + 4, :].bitcast(I32),
-            )
-
-        def copy_on(letter, dst, src):
-            if letter == "s":
-                nc.scalar.copy(dst, src)
-            else:
-                nc.vector.tensor_copy(dst, src)
 
         def raw_tile():
-            return raw_pool.tile([P, PASSES, PACK, H], F32, name="raw", align_bytes=256)
+            return raw_pool.tile([P, PASSES, PACK, H], F32, name="raw", align_bytes=DMA_ALIGN)
 
         def by_pass(matrix):
-            return matrix.rearrange("(o p j) c -> p o j c", o=PASSES, j=PACK)
+            return matrix.rearrange("(o p j) i -> p o j i", o=PASSES, j=PACK)
 
         def rounded_tile():
-            return rounded_pool.tile([P, PACK, P, PACK], BF16, name="rounded", align_bytes=64)
+            return rounded_pool.tile([P, PACK, P, PACK], BF16, name="rounded", align_bytes=MX_ALIGN)
 
         def code_tiles():
-            codes = codes_pool.tile([P, H], U32, name="codes", align_bytes=64)
-            scales = codes_pool.tile([P, H], U8, name="scales", align_bytes=64)
+            codes = codes_pool.tile([P, H], U32, name="codes", align_bytes=MX_ALIGN)
+            scales = codes_pool.tile([P, H], U8, name="scales", align_bytes=MX_ALIGN)
             return codes, scales
 
-        def round_columns(rounded, raw_pass, letters, ms):
+        def round_columns(rounded, raw_pass, copies, m_range):
             src = raw_pass.rearrange("p j (m t) -> p m j t", t=PACK)
             dst = rounded[:].rearrange("p t m j -> p m j t")
-            for half, letter in enumerate(letters):
+            for half, copy in enumerate(copies):
                 pair = slice(2 * half, 2 * half + 2)
-                copy_on(letter, dst[:, ms, :, pair], src[:, ms, :, pair])
+                copy(dst[:, m_range, :, pair], src[:, m_range, :, pair])
 
-        def quantize_pass(raw_pass, letters):
+        def quantize_pass(raw_pass, copies):
             rounded = rounded_tile()
-            round_columns(rounded, raw_pass, letters, slice(0, P))
+            round_columns(rounded, raw_pass, copies, slice(0, P))
             codes, scales = code_tiles()
             nc.vector.quantize_mx(
                 out=codes[:].bitcast(FP8X4),
@@ -100,26 +94,35 @@ def tile_moe_shr_glu_silu_kernel(
             )
             return codes, scales
 
-        def load_and_quantize(matrix, letters, whole):
+        def load_whole(matrix):
             raw = raw_tile()
+            nc.sync.dma_start(raw[:], by_pass(matrix))
+            return raw
+
+        def quantize_loaded(raw, copies):
+            return [quantize_pass(raw[:, o], copies) for o in range(PASSES)]
+
+        def load_and_quantize(matrix, copies, whole):
             if whole:
-                nc.sync.dma_start(raw[:], by_pass(matrix))
+                raw = load_whole(matrix)
+                return raw, quantize_loaded(raw, copies)
+            raw = raw_tile()
             quantized = []
             for o in range(PASSES):
-                if not whole:
-                    nc.sync.dma_start(raw[:, o], by_pass(matrix)[:, o])
-                quantized.append(quantize_pass(raw[:, o], letters[o]))
+                nc.sync.dma_start(raw[:, o], by_pass(matrix)[:, o])
+                quantized.append(quantize_pass(raw[:, o], copies))
             return raw, quantized
 
-        def load_and_quantize_finely(matrix, letters):
+        def load_and_quantize_finely(matrix, copies):
             raw = raw_tile()
             nc.sync.dma_start(raw[:, 0], by_pass(matrix)[:, 0])
-            quantized = [quantize_pass(raw[:, 0], letters)]
+            quantized = [quantize_pass(raw[:, 0], copies)]
             rounded = rounded_tile()
             for half in range(2):
                 cols = slice(half * H // 2, (half + 1) * H // 2)
                 nc.sync.dma_start(raw[:, 1, :, cols], by_pass(matrix)[:, 1, :, cols])
-                round_columns(rounded, raw[:, 1], "vs", slice(half * P // 2, (half + 1) * P // 2))
+                m_range = slice(half * P // 2, (half + 1) * P // 2)
+                round_columns(rounded, raw[:, 1], (on_vector, on_scalar), m_range)
             codes, scales = code_tiles()
             for half in range(2):
                 cols = slice(half * H // 2, (half + 1) * H // 2)
@@ -131,15 +134,14 @@ def tile_moe_shr_glu_silu_kernel(
             quantized.append((codes, scales))
             return raw, quantized, rounded
 
-        def quantize_w2(raw2, letter):
-            rounded2 = small_pool.tile([P, N, PACK], BF16, name="rounded2", align_bytes=64)
-            copy_on(
-                letter,
-                rounded2[:].rearrange("p (c i) j -> p c j i", i=4),
-                raw2.rearrange("p j (c i) -> p c j i", i=4),
+        def quantize_w2(raw2, copy):
+            rounded2 = small_pool.tile([P, N, PACK], BF16, name="rounded2", align_bytes=MX_ALIGN)
+            copy(
+                rounded2[:].rearrange("p (c u) j -> p c j u", u=4),
+                raw2.rearrange("p j (c u) -> p c j u", u=4),
             )
-            codes2 = small_pool.tile([P, N], U32, name="codes2", align_bytes=64)
-            scales2 = small_pool.tile([P, N], U8, name="scales2", align_bytes=64)
+            codes2 = small_pool.tile([P, N], U32, name="codes2", align_bytes=MX_ALIGN)
+            scales2 = small_pool.tile([P, N], U8, name="scales2", align_bytes=MX_ALIGN)
             nc.vector.quantize_mx(
                 out=codes2[:].bitcast(FP8X4),
                 scales=scales2[:],
@@ -147,8 +149,9 @@ def tile_moe_shr_glu_silu_kernel(
             )
             return codes2, scales2
 
-        def first_layer(weights, words, scales, cols, pool):
-            acc = pool.tile([P, PACK, SUB], F32, name="acc")
+        def first_layer(weights, words, scales, group, pool):
+            cols = slice(group * GROUP, (group + 1) * GROUP)
+            acc = pool.tile([P, PACK, GROUP], F32, name="acc")
             for t in range(PACK):
                 for o in range(PASSES):
                     w_codes, w_scales = weights[o]
@@ -163,22 +166,32 @@ def tile_moe_shr_glu_silu_kernel(
                     )
             return acc
 
-        def second_layer(weights3, weights2, words, scales, first_col, silus):
-            h = small_pool.tile([P, C, PACK], BF16, name="h", align_bytes=64)
-            for b, s in enumerate(silus):
-                cols = slice(first_col + b * SUB, first_col + (b + 1) * SUB)
-                acc = first_layer(weights3, words, scales, cols, psum_a3)
+        def silu_into(dst, acc):
+            nc.scalar.activation(dst, acc[:].rearrange("p t n -> p n t"), SILU)
+            return dst
+
+        def spent_row(raw, row):
+            return raw[:, 1, row, :].rearrange("p (n t) -> p n t", t=PACK)
+
+        def second_layer(weights3, weights2, words, scales, first_group, silus):
+            width = len(silus) * GROUP
+            h = small_pool.tile([P, width, PACK], BF16, name="h", align_bytes=MX_ALIGN)
+            for b, silu in enumerate(silus):
+                acc = first_layer(weights3, words, scales, first_group + b, psum_a3)
                 nc.vector.tensor_tensor(
-                    h[:, b * SUB : (b + 1) * SUB, :], acc[:].rearrange("p t n -> p n t"), s, MULT
+                    h[:, b * GROUP : (b + 1) * GROUP, :],
+                    acc[:].rearrange("p t n -> p n t"),
+                    silu,
+                    MULT,
                 )
-            h_codes = small_pool.tile([P, C], U32, name="h_codes", align_bytes=64)
-            h_scales = small_pool.tile([P, C], U8, name="h_scales", align_bytes=64)
+            h_codes = small_pool.tile([P, width], U32, name="h_codes", align_bytes=MX_ALIGN)
+            h_scales = small_pool.tile([P, width], U8, name="h_scales", align_bytes=MX_ALIGN)
             nc.vector.quantize_mx(
                 out=h_codes[:].bitcast(FP8X4),
                 scales=h_scales[:],
                 in_=h[:].rearrange("p n t -> p (n t)"),
             )
-            y_acc = psum_y.tile([P, C], F32, name="y_acc")
+            y_acc = psum_y.tile([P, width], F32, name="y_acc")
             codes2, scales2 = weights2
             nc.tensor.matmul_mx(
                 out=y_acc[:],
@@ -192,73 +205,76 @@ def tile_moe_shr_glu_silu_kernel(
             return y_acc
 
         y_slots = keep.tile([P, E * C], F32, name="y_slots")
-        w2_raw = keep.tile([P, E + 1, PACK, N], F32, name="w2_raw", align_bytes=256)
+        w2_raw = keep.tile([P, E + 1, PACK, N], F32, name="w2_raw", align_bytes=DMA_ALIGN)
         w2_rows = w2.rearrange("e (p j) n -> p e j n", j=PACK)
-        pos_sb = [keep.tile([P, T // 16], U16, name=f"pos_sb{r}", align_bytes=256) for r in range(2)]
+        pos_sb = [
+            keep.tile([P, T // 16], U16, name=f"pos_sb{r}", align_bytes=DMA_ALIGN) for r in range(2)
+        ]
+
+        first_raw = load_whole(w1[0])
+        for q in range(4):
+            nc.sync.dma_start(
+                token_scales[32 * q : 32 * q + 4 * PASSES, :].bitcast(I32),
+                x_scales[:, 4 * q : 4 * q + 4, :].bitcast(I32),
+            )
+
+        both_engines = (on_scalar, on_vector)
+        scalar_alone = (on_scalar, on_scalar)
 
         for e in range(E):
-            mine = offs_sb[:, e * LIST_COLS : (e + 1) * LIST_COLS]
+            expert_offs = offs_sb[:, e * LIST_COLS : (e + 1) * LIST_COLS]
             slot_words = []
             for o in range(PASSES):
-                gathered = keep.tile([P, C], U32, name=f"slot_words{e}_{o}", align_bytes=64)
-                nc.vector.tensor_copy(gathered[:], token_words[o].indirect(mine))
+                gathered = keep.tile([P, C], U32, name=f"slot_words{e}_{o}", align_bytes=MX_ALIGN)
+                nc.vector.tensor_copy(gathered[:], token_words[o].indirect(expert_offs))
                 slot_words.append(gathered)
-            slot_scales = keep.tile([P, C], U8, name=f"slot_scales{e}", align_bytes=64)
-            nc.vector.tensor_copy(slot_scales[:], token_scales[:].indirect(mine))
+            slot_scales = keep.tile([P, C], U8, name=f"slot_scales{e}", align_bytes=MX_ALIGN)
+            nc.vector.tensor_copy(slot_scales[:], token_scales[:].indirect(expert_offs))
 
-            letters = FIRST_ENGINES if e == 0 else ROUTED_ENGINES
-            weights1 = load_and_quantize(w1[e], letters[:2], e < WHOLE_LOADS)[1]
-            accs = [
-                first_layer(weights1, slot_words, slot_scales, slice(b * SUB, (b + 1) * SUB), psum_a1)
-                for b in range(C // SUB)
-            ]
-            if e < E - 1:
-                raw3, weights3 = load_and_quantize(w3[e], letters[2:], e < WHOLE_LOADS)
+            if e == 0:
+                copies = scalar_alone
+                weights1 = quantize_loaded(first_raw, copies)
             else:
-                raw3, weights3 = load_and_quantize_finely(w3[e], letters[2])[:2]
+                copies = both_engines
+                weights1 = load_and_quantize(w1[e], copies, e < WHOLE_LOADS)[1]
+            accs = [
+                first_layer(weights1, slot_words, slot_scales, b, psum_a1) for b in range(C // GROUP)
+            ]
+            if e < LAST_ROUTED:
+                raw3, weights3 = load_and_quantize(w3[e], copies, e < WHOLE_LOADS)
+            else:
+                raw3, weights3 = load_and_quantize_finely(w3[e], copies)[:2]
             if e == 0:
                 nc.sync.dma_start(w2_raw[:, :E], w2_rows[:, :E])
                 nc.sync.dma_start(pos_sb[0][:], pos1)
                 nc.sync.dma_start(pos_sb[1][:], pos2)
-            weights2 = quantize_w2(w2_raw[:, e], "v")
-            silus = []
-            for b, acc in enumerate(accs):
-                s = raw3[:, 1, b, :].rearrange("p (n t) -> p n t", t=PACK)
-                nc.scalar.activation(s, acc[:].rearrange("p t n -> p n t"), SILU)
-                silus.append(s)
+            weights2 = quantize_w2(w2_raw[:, e], on_vector)
+            silus = [silu_into(spent_row(raw3, b), acc) for b, acc in enumerate(accs)]
             y_acc = second_layer(weights3, weights2, slot_words, slot_scales, 0, silus)
-            copy_on("v" if e < E - 1 else "s", y_slots[:, e * C : (e + 1) * C], y_acc[:])
+            copy_out = on_vector if e < LAST_ROUTED else on_scalar
+            copy_out(y_slots[:, e * C : (e + 1) * C], y_acc[:])
 
+        weights1 = load_and_quantize(w1[SHARED], both_engines, False)[1]
         gate_sb = []
-        weights1 = load_and_quantize(w1[E], SHARED_ENGINES[:2], False)[1]
         for r in range(2):
-            g = keep.tile([P, T], F32, name=f"gate_sb{r}", align_bytes=256)
-            nc.sync.dma_start(g[:], gate[r])
-            gate_sb.append(g)
+            gate_tile = keep.tile([P, T], F32, name=f"gate_sb{r}", align_bytes=DMA_ALIGN)
+            nc.sync.dma_start(gate_tile[:], gate[r])
+            gate_sb.append(gate_tile)
 
-        def shared_a1(b):
-            return first_layer(
-                weights1, token_words, token_scales, slice(b * SUB, (b + 1) * SUB), psum_a1
-            )
-
-        accs = [shared_a1(b) for b in range(A1_BANKS)]
-        raw3, weights3, last_rounded = load_and_quantize_finely(w3[E], SHARED_ENGINES[2])
-        silus = []
-        for b in range(T // SUB):
-            if b < A1_BANKS:
-                acc = accs[b]
-                s = raw3[:, 1, b, :].rearrange("p (n t) -> p n t", t=PACK)
-            else:
-                acc = shared_a1(b)
-                s = silu_pool.tile([P, SUB, PACK], F32, name="s")[:]
-            nc.scalar.activation(s, acc[:].rearrange("p t n -> p n t"), SILU)
-            silus.append(s)
-        nc.sync.dma_start(w2_raw[:, E], w2_rows[:, E])
-        weights2 = quantize_w2(w2_raw[:, E], "s")
+        accs = [
+            first_layer(weights1, token_words, token_scales, b, psum_a1) for b in range(A1_BANKS)
+        ]
+        raw3, weights3, last_rounded = load_and_quantize_finely(w3[SHARED], both_engines)
+        silus = [silu_into(spent_row(raw3, b), acc) for b, acc in enumerate(accs)]
+        for b in range(A1_BANKS, T // GROUP):
+            acc = first_layer(weights1, token_words, token_scales, b, psum_a1)
+            silu_tile = silu_pool.tile([P, GROUP, PACK], F32, name="silu_tile")
+            silus.append(silu_into(silu_tile[:], acc))
+        nc.sync.dma_start(w2_raw[:, SHARED], w2_rows[:, SHARED])
+        weights2 = quantize_w2(w2_raw[:, SHARED], on_scalar)
 
         routed = []
         for c in range(T // C):
-            cols = slice(c * C, (c + 1) * C)
             picks = []
             for r in range(2):
                 if c == T // C - 1:
@@ -268,17 +284,20 @@ def tile_moe_shr_glu_silu_kernel(
                 nc.vector.tensor_tensor(
                     pick,
                     y_slots[:].indirect(pos_sb[r][:, c * LIST_COLS : (c + 1) * LIST_COLS]),
-                    gate_sb[r][:, cols],
+                    gate_sb[r][:, c * C : (c + 1) * C],
                     MULT,
                 )
                 picks.append(pick)
-            both = small_pool.tile([P, C], F32, name="both")
-            nc.vector.tensor_tensor(both[:], picks[0], picks[1], ADD)
-            routed.append(both)
+            combined = small_pool.tile([P, C], F32, name="combined")
+            nc.vector.tensor_tensor(combined[:], picks[0], picks[1], ADD)
+            routed.append(combined)
 
-        for c in range(T // C):
-            pair = silus[c * (C // SUB) : (c + 1) * (C // SUB)]
-            y_acc = second_layer(weights3, weights2, token_words, token_scales, c * C, pair)
-            result = small_pool.tile([P, C], F32, name="result", align_bytes=256)
-            nc.vector.tensor_tensor(result[:], y_acc[:], routed[c][:], ADD)
-            nc.sync.dma_start(out[:, c * C : (c + 1) * C], result[:])
+        for first, last in SHARED_RANGES:
+            width = (last - first) * GROUP
+            y_acc = second_layer(
+                weights3, weights2, token_words, token_scales, first, silus[first:last]
+            )
+            result = small_pool.tile([P, width], F32, name="result", align_bytes=DMA_ALIGN)
+            c, offset = divmod(first * GROUP, C)
+            nc.vector.tensor_tensor(result[:], y_acc[:], routed[c][:, offset : offset + width], ADD)
+            nc.sync.dma_start(out[:, first * GROUP : last * GROUP], result[:])

@@ -1,6 +1,7 @@
 from contextlib import ExitStack
 
 import concourse.mybir as mybir
+from concourse.masks import make_identity
 
 K, T, E, C, H, N = 1024, 768, 6, 256, 512, 128
 FLOPS = 2 * (E * C + T) * (2 * K * H + H * N)
@@ -23,14 +24,14 @@ GROUP = 128
 LIST_COLS = C // 16
 SHARED = E
 LAST_ROUTED = E - 1
-
 MX_ALIGN = 64
 DMA_ALIGN = 256
-
-A1_BANKS, A3_BANKS, Y_BANKS = 4, 3, 1
-
+A1_BANKS = 4
 WHOLE_LOADS = 4
-
+EARLY_W2 = 5
+FINE_D = 2
+FINE_H = 1
+GATHER = 512
 SHARED_RANGES = ((0, 2), (2, 4), (4, 5), (5, 6))
 
 
@@ -44,12 +45,12 @@ def tile_moe_shr_glu_silu_kernel(
         keep = ctx.enter_context(tc.tile_pool(name="keep", bufs=1))
         raw_pool = ctx.enter_context(tc.tile_pool(name="raw", bufs=7))
         rounded_pool = ctx.enter_context(tc.tile_pool(name="rounded", bufs=5))
-        codes_pool = ctx.enter_context(tc.tile_pool(name="codes", bufs=8))
+        codes_pool = ctx.enter_context(tc.tile_pool(name="codes", bufs=9))
         small_pool = ctx.enter_context(tc.tile_pool(name="small", bufs=T // C))
-        silu_pool = ctx.enter_context(tc.tile_pool(name="silu", bufs=T // GROUP - A1_BANKS))
-        psum_a1 = ctx.enter_context(tc.psum_pool(name="psum_a1", bufs=A1_BANKS))
-        psum_a3 = ctx.enter_context(tc.psum_pool(name="psum_a3", bufs=A3_BANKS))
-        psum_y = ctx.enter_context(tc.psum_pool(name="psum_y", bufs=Y_BANKS))
+        tail_pool = ctx.enter_context(tc.tile_pool(name="tail", bufs=6))
+        psum_a1 = ctx.enter_context(tc.psum_pool(name="psum", bufs=8))
+        psum_a3 = psum_a1
+        psum_y = psum_a1
 
         token_scales = keep.tile([P, T], U8, name="token_scales", align_bytes=DMA_ALIGN)
         nc.vector.memset(token_scales[:].bitcast(I32), 0)
@@ -62,6 +63,26 @@ def tile_moe_shr_glu_silu_kernel(
         offs_sb = keep.tile([P, E * LIST_COLS], U16, name="offs_sb", align_bytes=DMA_ALIGN)
         nc.sync.dma_start(offs_sb[:], offs)
 
+        identity = keep.tile([P, P], F32, name="identity", align_bytes=MX_ALIGN)
+        make_identity(nc, identity[:])
+        gate_sb = [keep.tile([P, T], F32, name=f"gate_sb{r}") for r in range(2)]
+        for first, per in ((0, 4), (512, 2)):
+            column = keep.tile([P, 2, 8], F32, name=f"gate_column{per}")
+            nc.scalar.dma_start(
+                column[:, :, :per],
+                gate[:, 0, first : first + P * per].rearrange("r (p c) -> p r c", c=per),
+            )
+            for r in range(2):
+                spread = psum_a1.tile([P, PACK, GROUP], F32, name="acc")
+                for c in range(per):
+                    nc.tensor.transpose(
+                        spread[:, c, :], column[:, r, c : c + 1].to_broadcast([P, P]), identity[:]
+                    )
+                nc.scalar.copy(
+                    gate_sb[r][:, first : first + P * per].rearrange("p (n c) -> p n c", c=per),
+                    spread[:, :per, :].rearrange("p c n -> p n c"),
+                )
+
         def raw_tile():
             return raw_pool.tile([P, PASSES, PACK, H], F32, name="raw", align_bytes=DMA_ALIGN)
 
@@ -71,9 +92,12 @@ def tile_moe_shr_glu_silu_kernel(
         def rounded_tile():
             return rounded_pool.tile([P, PACK, P, PACK], BF16, name="rounded", align_bytes=MX_ALIGN)
 
-        def code_tiles():
-            codes = codes_pool.tile([P, H], U32, name="codes", align_bytes=MX_ALIGN)
-            scales = codes_pool.tile([P, H], U8, name="scales", align_bytes=MX_ALIGN)
+        def by_t(codes, scales, count):
+            return [(codes[:, t * P : (t + 1) * P], scales[:, t * P : (t + 1) * P]) for t in range(count)]
+
+        def code_tiles(width):
+            codes = codes_pool.tile([P, width], U32, name="codes", align_bytes=MX_ALIGN)
+            scales = codes_pool.tile([P, width], U8, name="scales", align_bytes=MX_ALIGN)
             return codes, scales
 
         def round_columns(rounded, raw_pass, copies, m_range):
@@ -86,13 +110,13 @@ def tile_moe_shr_glu_silu_kernel(
         def quantize_pass(raw_pass, copies):
             rounded = rounded_tile()
             round_columns(rounded, raw_pass, copies, slice(0, P))
-            codes, scales = code_tiles()
+            codes, scales = code_tiles(H)
             nc.vector.quantize_mx(
                 out=codes[:].bitcast(FP8X4),
                 scales=scales[:],
                 in_=rounded[:].rearrange("p t m j -> p (t m j)"),
             )
-            return codes, scales
+            return by_t(codes, scales, PACK)
 
         def load_whole(matrix):
             raw = raw_tile()
@@ -105,39 +129,39 @@ def tile_moe_shr_glu_silu_kernel(
         def load_and_quantize(matrix, copies, whole):
             if whole:
                 raw = load_whole(matrix)
-                return raw, quantize_loaded(raw, copies)
+                return raw, [quantize_pass(raw[:, o], copies[o]) for o in range(PASSES)]
             raw = raw_tile()
             quantized = []
             for o in range(PASSES):
                 nc.sync.dma_start(raw[:, o], by_pass(matrix)[:, o])
-                quantized.append(quantize_pass(raw[:, o], copies))
+                quantized.append(quantize_pass(raw[:, o], copies[o]))
             return raw, quantized
 
-        def load_and_quantize_finely(matrix, copies):
+        def load_and_quantize_finely(matrix, copies, pieces, last_copies):
             raw = raw_tile()
             nc.sync.dma_start(raw[:, 0], by_pass(matrix)[:, 0])
             quantized = [quantize_pass(raw[:, 0], copies)]
             rounded = rounded_tile()
-            for half in range(2):
-                cols = slice(half * H // 2, (half + 1) * H // 2)
+            for piece in range(pieces):
+                cols = slice(piece * H // pieces, (piece + 1) * H // pieces)
                 nc.sync.dma_start(raw[:, 1, :, cols], by_pass(matrix)[:, 1, :, cols])
-                m_range = slice(half * P // 2, (half + 1) * P // 2)
-                round_columns(rounded, raw[:, 1], (on_vector, on_scalar), m_range)
-            codes, scales = code_tiles()
+                m_range = slice(piece * P // pieces, (piece + 1) * P // pieces)
+                round_columns(rounded, raw[:, 1], last_copies, m_range)
+            halves = []
             for half in range(2):
-                cols = slice(half * H // 2, (half + 1) * H // 2)
+                codes, scales = code_tiles(H // 2)
                 nc.vector.quantize_mx(
-                    out=codes[:, cols].bitcast(FP8X4),
-                    scales=scales[:, cols],
+                    out=codes[:].bitcast(FP8X4),
+                    scales=scales[:],
                     in_=rounded[:, 2 * half : 2 * half + 2].rearrange("p t m j -> p (t m j)"),
                 )
-            quantized.append((codes, scales))
+                halves.extend(by_t(codes, scales, 2))
+            quantized.append(halves)
             return raw, quantized, rounded
 
-        def quantize_w2(raw2, copy):
-            rounded2 = small_pool.tile([P, N, PACK], BF16, name="rounded2", align_bytes=MX_ALIGN)
+        def quantize_w2(raw2, copy, rounded2):
             copy(
-                rounded2[:].rearrange("p (c u) j -> p c j u", u=4),
+                rounded2.rearrange("p (c u) j -> p c j u", u=4),
                 raw2.rearrange("p j (c u) -> p c j u", u=4),
             )
             codes2 = small_pool.tile([P, N], U32, name="codes2", align_bytes=MX_ALIGN)
@@ -145,24 +169,26 @@ def tile_moe_shr_glu_silu_kernel(
             nc.vector.quantize_mx(
                 out=codes2[:].bitcast(FP8X4),
                 scales=scales2[:],
-                in_=rounded2[:].rearrange("p n j -> p (n j)"),
+                in_=rounded2.rearrange("p n j -> p (n j)"),
             )
-            return codes2, scales2
+            return codes2[:], scales2[:]
 
-        def first_layer(weights, words, scales, group, pool):
-            cols = slice(group * GROUP, (group + 1) * GROUP)
+        def w2_tile(pool, name):
+            return pool.tile([P, N, PACK], BF16, name=name, align_bytes=MX_ALIGN)[:]
+
+        def first_layer(weights, words, scales, cols, pool):
             acc = pool.tile([P, PACK, GROUP], F32, name="acc")
-            for t in range(PACK):
-                for o in range(PASSES):
-                    w_codes, w_scales = weights[o]
+            for o in range(PASSES):
+                for t in range(PACK):
+                    w_codes, w_scales = weights[o][t]
                     nc.tensor.matmul_mx(
                         out=acc[:, t, :],
-                        lhsT=w_codes[:, t * P : (t + 1) * P].bitcast(FP8X4),
-                        lhsT_scale=w_scales[:, t * P : (t + 1) * P],
+                        lhsT=w_codes.bitcast(FP8X4),
+                        lhsT_scale=w_scales,
                         rhs=words[o][:, cols].bitcast(FP8X4),
                         rhs_scale=scales[4 * o : P, cols],
-                        start=(o == 0),
-                        stop=(o == PASSES - 1),
+                        start=(o == 0 and t == 0),
+                        stop=(o == PASSES - 1 and t == PACK - 1),
                     )
             return acc
 
@@ -170,14 +196,17 @@ def tile_moe_shr_glu_silu_kernel(
             nc.scalar.activation(dst, acc[:].rearrange("p t n -> p n t"), SILU)
             return dst
 
-        def spent_row(raw, row):
-            return raw[:, 1, row, :].rearrange("p (n t) -> p n t", t=PACK)
+        def spent_row(raw, row, o=1):
+            return raw[:, o, row, :].rearrange("p (n t) -> p n t", t=PACK)
 
-        def second_layer(weights3, weights2, words, scales, first_group, silus):
+        def group_cols(first, b):
+            return slice(first + b * GROUP, first + (b + 1) * GROUP)
+
+        def hidden(accs3, silus):
             width = len(silus) * GROUP
             h = small_pool.tile([P, width, PACK], BF16, name="h", align_bytes=MX_ALIGN)
             for b, silu in enumerate(silus):
-                acc = first_layer(weights3, words, scales, first_group + b, psum_a3)
+                acc = accs3[b]
                 nc.vector.tensor_tensor(
                     h[:, b * GROUP : (b + 1) * GROUP, :],
                     acc[:].rearrange("p t n -> p n t"),
@@ -191,18 +220,20 @@ def tile_moe_shr_glu_silu_kernel(
                 scales=h_scales[:],
                 in_=h[:].rearrange("p n t -> p (n t)"),
             )
-            y_acc = psum_y.tile([P, width], F32, name="y_acc")
+            return h_codes, h_scales
+
+        def second_layer(y_acc, weights2, h_quantized):
             codes2, scales2 = weights2
+            h_codes, h_scales = h_quantized
             nc.tensor.matmul_mx(
-                out=y_acc[:],
-                lhsT=codes2[:].bitcast(FP8X4),
-                lhsT_scale=scales2[:],
+                out=y_acc,
+                lhsT=codes2.bitcast(FP8X4),
+                lhsT_scale=scales2,
                 rhs=h_codes[:].bitcast(FP8X4),
                 rhs_scale=h_scales[:],
                 start=True,
                 stop=True,
             )
-            return y_acc
 
         y_slots = keep.tile([P, E * C], F32, name="y_slots")
         w2_raw = keep.tile([P, E + 1, PACK, N], F32, name="w2_raw", align_bytes=DMA_ALIGN)
@@ -220,67 +251,111 @@ def tile_moe_shr_glu_silu_kernel(
 
         both_engines = (on_scalar, on_vector)
         scalar_alone = (on_scalar, on_scalar)
+        vector_alone = (on_vector, on_vector)
 
-        for e in range(E):
-            expert_offs = offs_sb[:, e * LIST_COLS : (e + 1) * LIST_COLS]
+        gathered = []
+        for g in range(E * C // GATHER):
+            piece = offs_sb[:, g * GATHER // 16 : (g + 1) * GATHER // 16]
             slot_words = []
             for o in range(PASSES):
-                gathered = keep.tile([P, C], U32, name=f"slot_words{e}_{o}", align_bytes=MX_ALIGN)
-                nc.vector.tensor_copy(gathered[:], token_words[o].indirect(expert_offs))
-                slot_words.append(gathered)
-            slot_scales = keep.tile([P, C], U8, name=f"slot_scales{e}", align_bytes=MX_ALIGN)
-            nc.vector.tensor_copy(slot_scales[:], token_scales[:].indirect(expert_offs))
+                words = keep.tile([P, GATHER], U32, name=f"slot_words{g}_{o}", align_bytes=MX_ALIGN)
+                nc.vector.tensor_copy(words[:], token_words[o].indirect(piece))
+                slot_words.append(words)
+            slot_scales = keep.tile([P, GATHER], U8, name=f"slot_scales{g}", align_bytes=MX_ALIGN)
+            nc.vector.tensor_copy(slot_scales[:], token_scales[:].indirect(piece))
+            gathered.append((slot_words, slot_scales))
 
+        waiting = []
+        for e in range(E):
+            slot_words, slot_scales = gathered[e * C // GATHER]
+            first = e * C % GATHER
             if e == 0:
                 copies = scalar_alone
-                weights1 = quantize_loaded(first_raw, copies)
+                raw1, weights1 = first_raw, quantize_loaded(first_raw, copies)
             else:
                 copies = both_engines
-                weights1 = load_and_quantize(w1[e], copies, e < WHOLE_LOADS)[1]
+                raw1, weights1 = load_and_quantize(w1[e], (copies,copies), e < WHOLE_LOADS)
             accs = [
-                first_layer(weights1, slot_words, slot_scales, b, psum_a1) for b in range(C // GROUP)
+                first_layer(weights1, slot_words, slot_scales, group_cols(first, b), psum_a1)
+                for b in range(C // GROUP)
             ]
             if e < LAST_ROUTED:
-                raw3, weights3 = load_and_quantize(w3[e], copies, e < WHOLE_LOADS)
+                raw3, weights3 = load_and_quantize(w3[e], (copies,copies), e < WHOLE_LOADS)
             else:
-                raw3, weights3 = load_and_quantize_finely(w3[e], copies)[:2]
+                raw3, weights3 = load_and_quantize_finely(w3[e], copies, FINE_D, (on_vector, on_scalar))[:2]
+                if EARLY_W2 < E:
+                    nc.sync.dma_start(w2_raw[:, EARLY_W2:E], w2_rows[:, EARLY_W2:E])
             if e == 0:
-                nc.sync.dma_start(w2_raw[:, :E], w2_rows[:, :E])
+                nc.sync.dma_start(w2_raw[:, :EARLY_W2], w2_rows[:, :EARLY_W2])
                 nc.sync.dma_start(pos_sb[0][:], pos1)
                 nc.sync.dma_start(pos_sb[1][:], pos2)
-            weights2 = quantize_w2(w2_raw[:, e], on_vector)
-            silus = [silu_into(spent_row(raw3, b), acc) for b, acc in enumerate(accs)]
-            y_acc = second_layer(weights3, weights2, slot_words, slot_scales, 0, silus)
-            copy_out = on_vector if e < LAST_ROUTED else on_scalar
-            copy_out(y_slots[:, e * C : (e + 1) * C], y_acc[:])
-
-        weights1 = load_and_quantize(w1[SHARED], both_engines, False)[1]
-        gate_sb = []
-        for r in range(2):
-            gate_tile = keep.tile([P, T], F32, name=f"gate_sb{r}", align_bytes=DMA_ALIGN)
-            nc.sync.dma_start(gate_tile[:], gate[r])
-            gate_sb.append(gate_tile)
-
-        accs = [
-            first_layer(weights1, token_words, token_scales, b, psum_a1) for b in range(A1_BANKS)
+            silus = [
+                silu_into(spent_row(raw3, b, 1), acc)
+                for b, acc in enumerate(accs)
+            ]
+            accs3 = [
+                first_layer(weights3, slot_words, slot_scales, group_cols(first, b), psum_a3)
+                for b in range(C // GROUP)
+            ]
+            if e < EARLY_W2:
+                weights2 = quantize_w2(w2_raw[:, e], on_vector, w2_tile(small_pool, "rounded2"))
+                h_quantized = hidden(accs3, silus)
+                y_acc = psum_y.tile([P, C], F32, name="acc")
+                second_layer(y_acc[:], weights2, h_quantized)
+                copy_out = on_vector if e < LAST_ROUTED else on_scalar
+                copy_out(y_slots[:, e * C : (e + 1) * C], y_acc[:])
+            else:
+                waiting.append(hidden(accs3, silus))
+        late = [
+            quantize_w2(
+                w2_raw[:, e],
+                on_scalar,
+                raw3[:, 1, 2, 2 * N :].bitcast(BF16).rearrange("p (n j) -> p n j", j=PACK),
+            )
+            for e in range(EARLY_W2, E)
         ]
-        raw3, weights3, last_rounded = load_and_quantize_finely(w3[SHARED], both_engines)
-        silus = [silu_into(spent_row(raw3, b), acc) for b, acc in enumerate(accs)]
-        for b in range(A1_BANKS, T // GROUP):
-            acc = first_layer(weights1, token_words, token_scales, b, psum_a1)
-            silu_tile = silu_pool.tile([P, GROUP, PACK], F32, name="silu_tile")
-            silus.append(silu_into(silu_tile[:], acc))
-        nc.sync.dma_start(w2_raw[:, SHARED], w2_rows[:, SHARED])
-        weights2 = quantize_w2(w2_raw[:, SHARED], on_scalar)
+        for b, h_quantized in enumerate(waiting):
+            e = EARLY_W2 + b
+            y_acc = psum_y.tile([P, C], F32, name="acc")
+            second_layer(y_acc[:], late[b], h_quantized)
+            on_vector(y_slots[:, e * C : (e + 1) * C], y_acc[:])
 
+
+        raw1, weights1 = load_and_quantize(w1[SHARED], (scalar_alone, scalar_alone), False)
+        accs = [
+            first_layer(weights1, token_words, token_scales, group_cols(0, b), psum_a1)
+            for b in range(T // GROUP)
+        ]
+        raw3, weights3, last_rounded = load_and_quantize_finely(w3[SHARED], scalar_alone, FINE_H, scalar_alone)
+
+        nc.sync.dma_start(w2_raw[:, SHARED], w2_rows[:, SHARED])
+        silus = []
+        for b in range(T // GROUP):
+            if b % 2 == 0:
+                pair = rounded_pool.tile([P, 2, GROUP, PACK], F32, name="rounded", align_bytes=MX_ALIGN)
+            silus.append(silu_into(pair[:, b % 2], accs[b]))
+            if b == 2:
+                weights2 = quantize_w2(w2_raw[:, SHARED], on_scalar, w2_tile(rounded_pool, "rounded"))
+
+        accs3 = [
+            first_layer(weights3, token_words, token_scales, group_cols(0, b), psum_a3)
+            for b in range(T // GROUP)
+        ]
+
+        def spent_part(raw, o, index):
+            return raw[:, o, index // 2, index % 2 * C : (index % 2 + 1) * C]
+
+        pick_places = [None, None, spent_part(raw1, 0, 0), spent_part(raw1, 0, 1), spent_part(raw1, 1, 0), spent_part(raw1, 1, 1)]
+        sum_places = [spent_part(raw1, 0, 2), spent_part(raw1, 1, 2), codes_pool.tile([P, C], F32, name="codes", align_bytes=MX_ALIGN)[:]]
         routed = []
         for c in range(T // C):
             picks = []
             for r in range(2):
-                if c == T // C - 1:
-                    pick = last_rounded[:, 2 + r, :, :].rearrange("p m j -> p (m j)").bitcast(F32)
+                place = pick_places[2 * c + r]
+                if place is None:
+                    pick = small_pool.tile([P, C], F32, name=f"pick{r}", bufs=1)[:]
                 else:
-                    pick = small_pool.tile([P, C], F32, name=f"pick{r}")[:]
+                    pick = place
                 nc.vector.tensor_tensor(
                     pick,
                     y_slots[:].indirect(pos_sb[r][:, c * LIST_COLS : (c + 1) * LIST_COLS]),
@@ -288,16 +363,51 @@ def tile_moe_shr_glu_silu_kernel(
                     MULT,
                 )
                 picks.append(pick)
-            combined = small_pool.tile([P, C], F32, name="combined")
-            nc.vector.tensor_tensor(combined[:], picks[0], picks[1], ADD)
+            combined = sum_places[c]
+            nc.vector.tensor_tensor(combined, picks[0], picks[1], ADD)
             routed.append(combined)
 
-        for first, last in SHARED_RANGES:
-            width = (last - first) * GROUP
-            y_acc = second_layer(
-                weights3, weights2, token_words, token_scales, first, silus[first:last]
+        def tail_tile(shape, dtype):
+            return tail_pool.tile(shape, dtype, name="tail", align_bytes=DMA_ALIGN)
+
+        h_tiles, quantized = {}, {}
+
+        def multiply(b):
+            if b % 2 == 0:
+                h_tiles[b // 2] = tail_tile([P, C, PACK], BF16)
+            nc.vector.tensor_tensor(
+                h_tiles[b // 2][:, b % 2 * GROUP : (b % 2 + 1) * GROUP, :],
+                accs3[b][:].rearrange("p t n -> p n t"),
+                silus[b],
+                MULT,
             )
-            result = small_pool.tile([P, width], F32, name="result", align_bytes=DMA_ALIGN)
-            c, offset = divmod(first * GROUP, C)
-            nc.vector.tensor_tensor(result[:], y_acc[:], routed[c][:, offset : offset + width], ADD)
-            nc.sync.dma_start(out[:, first * GROUP : last * GROUP], result[:])
+
+        def quantize_h(c):
+            h_codes = tail_tile([P, C], U32)
+            h_scales = small_pool.tile([P, C], U8, name="h_scales", align_bytes=MX_ALIGN)
+            nc.vector.quantize_mx(
+                out=h_codes[:].bitcast(FP8X4),
+                scales=h_scales[:],
+                in_=h_tiles[c][:].rearrange("p n t -> p (n t)"),
+            )
+            y_acc = psum_y.tile([P, C], F32, name="acc")
+            second_layer(y_acc[:], weights2, (h_codes, h_scales))
+            quantized[c] = y_acc
+
+        def finish(c):
+            result = tail_tile([P, C], F32)
+            nc.vector.tensor_tensor(result[:], quantized[c][:], routed[c], ADD)
+            nc.sync.dma_start(out[:, c * C : (c + 1) * C], result[:])
+
+        multiply(0)
+        multiply(1)
+        multiply(2)
+        quantize_h(0)
+        multiply(3)
+        multiply(4)
+        quantize_h(1)
+        multiply(5)
+        finish(0)
+        quantize_h(2)
+        finish(1)
+        finish(2)

@@ -44,10 +44,10 @@ def tile_moe_shr_glu_silu_kernel(
     with ExitStack() as ctx:
         keep = ctx.enter_context(tc.tile_pool(name="keep", bufs=1))
         raw_pool = ctx.enter_context(tc.tile_pool(name="raw", bufs=7))
-        rounded_pool = ctx.enter_context(tc.tile_pool(name="rounded", bufs=5))
+        rounded_pool = ctx.enter_context(tc.tile_pool(name="rounded", bufs=6))
         codes_pool = ctx.enter_context(tc.tile_pool(name="codes", bufs=9))
         small_pool = ctx.enter_context(tc.tile_pool(name="small", bufs=T // C))
-        tail_pool = ctx.enter_context(tc.tile_pool(name="tail", bufs=6))
+        tail_pool = ctx.enter_context(tc.tile_pool(name="tail", bufs=7))
         psum_a1 = ctx.enter_context(tc.psum_pool(name="psum", bufs=8))
         psum_a3 = psum_a1
         psum_y = psum_a1
@@ -103,8 +103,9 @@ def tile_moe_shr_glu_silu_kernel(
         def round_columns(rounded, raw_pass, copies, m_range):
             src = raw_pass.rearrange("p j (m t) -> p m j t", t=PACK)
             dst = rounded[:].rearrange("p t m j -> p m j t")
-            for half, copy in enumerate(copies):
-                pair = slice(2 * half, 2 * half + 2)
+            width = PACK // len(copies)
+            for part, copy in enumerate(copies):
+                pair = slice(width * part, width * (part + 1))
                 copy(dst[:, m_range, :, pair], src[:, m_range, :, pair])
 
         def quantize_pass(raw_pass, copies):
@@ -137,16 +138,29 @@ def tile_moe_shr_glu_silu_kernel(
                 quantized.append(quantize_pass(raw[:, o], copies[o]))
             return raw, quantized
 
-        def load_and_quantize_finely(matrix, copies, pieces, last_copies):
+        def load_and_quantize_finely(matrix, copies, pieces, last_copies, hold=False):
             raw = raw_tile()
             nc.sync.dma_start(raw[:, 0], by_pass(matrix)[:, 0])
-            quantized = [quantize_pass(raw[:, 0], copies)]
+            if hold:
+                first_rounded = rounded_tile()
+                round_columns(first_rounded, raw[:, 0], copies, slice(0, P))
+            else:
+                quantized = [quantize_pass(raw[:, 0], copies)]
             rounded = rounded_tile()
             for piece in range(pieces):
                 cols = slice(piece * H // pieces, (piece + 1) * H // pieces)
                 nc.sync.dma_start(raw[:, 1, :, cols], by_pass(matrix)[:, 1, :, cols])
                 m_range = slice(piece * P // pieces, (piece + 1) * P // pieces)
                 round_columns(rounded, raw[:, 1], last_copies, m_range)
+            if hold:
+                codes = rounded_pool.tile([P, H], U32, name="rounded", align_bytes=MX_ALIGN)
+                scales = codes_pool.tile([P, H], U8, name="scales", align_bytes=MX_ALIGN)
+                nc.vector.quantize_mx(
+                    out=codes[:].bitcast(FP8X4),
+                    scales=scales[:],
+                    in_=first_rounded[:].rearrange("p t m j -> p (t m j)"),
+                )
+                quantized = [by_t(codes, scales, PACK)]
             halves = []
             for half in range(2):
                 codes, scales = code_tiles(H // 2)
@@ -159,12 +173,15 @@ def tile_moe_shr_glu_silu_kernel(
             quantized.append(halves)
             return raw, quantized, rounded
 
-        def quantize_w2(raw2, copy, rounded2):
+        def round_w2(rounded2, raw2, copy):
             copy(
                 rounded2.rearrange("p (c u) j -> p c j u", u=4),
                 raw2.rearrange("p j (c u) -> p c j u", u=4),
             )
-            codes2 = small_pool.tile([P, N], U32, name="codes2", align_bytes=MX_ALIGN)
+
+        def quantize_rounded_w2(rounded2, codes2=None):
+            if codes2 is None:
+                codes2 = small_pool.tile([P, N], U32, name="codes2", align_bytes=MX_ALIGN)
             scales2 = small_pool.tile([P, N], U8, name="scales2", align_bytes=MX_ALIGN)
             nc.vector.quantize_mx(
                 out=codes2[:].bitcast(FP8X4),
@@ -172,6 +189,25 @@ def tile_moe_shr_glu_silu_kernel(
                 in_=rounded2.rearrange("p n j -> p (n j)"),
             )
             return codes2[:], scales2[:]
+
+        def quantize_w2(raw2, copy, rounded2):
+            round_w2(rounded2, raw2, copy)
+            return quantize_rounded_w2(rounded2)
+
+        def multiply_group(acc, silu):
+            h = small_pool.tile([P, GROUP, PACK], BF16, name="h", align_bytes=MX_ALIGN)
+            nc.vector.tensor_tensor(h[:], acc[:].rearrange("p t n -> p n t"), silu, MULT)
+            return h
+
+        def quantize_group(h):
+            h_codes = small_pool.tile([P, GROUP], U32, name="h_codes", align_bytes=MX_ALIGN)
+            h_scales = small_pool.tile([P, GROUP], U8, name="h_scales", align_bytes=MX_ALIGN)
+            nc.vector.quantize_mx(
+                out=h_codes[:].bitcast(FP8X4),
+                scales=h_scales[:],
+                in_=h[:].rearrange("p n t -> p (n t)"),
+            )
+            return h_codes, h_scales
 
         def w2_tile(pool, name):
             return pool.tile([P, N, PACK], BF16, name=name, align_bytes=MX_ALIGN)[:]
@@ -283,12 +319,12 @@ def tile_moe_shr_glu_silu_kernel(
                 raw3, weights3 = load_and_quantize(w3[e], (copies,copies), e < WHOLE_LOADS)
             else:
                 raw3, weights3 = load_and_quantize_finely(w3[e], copies, FINE_D, (on_vector, on_scalar))[:2]
-                if EARLY_W2 < E:
-                    nc.sync.dma_start(w2_raw[:, EARLY_W2:E], w2_rows[:, EARLY_W2:E])
-            if e == 0:
-                nc.sync.dma_start(w2_raw[:, :EARLY_W2], w2_rows[:, :EARLY_W2])
+                nc.sync.dma_start(w2_raw[:, EARLY_W2:E], w2_rows[:, EARLY_W2:E])
                 nc.sync.dma_start(pos_sb[0][:], pos1)
                 nc.sync.dma_start(pos_sb[1][:], pos2)
+            if e == 0:
+                nc.sync.dma_start(w2_raw[:, :EARLY_W2], w2_rows[:, :EARLY_W2])
+
             silus = [
                 silu_into(spent_row(raw3, b, 1), acc)
                 for b, acc in enumerate(accs)
@@ -304,29 +340,24 @@ def tile_moe_shr_glu_silu_kernel(
                 second_layer(y_acc[:], weights2, h_quantized)
                 copy_out = on_vector if e < LAST_ROUTED else on_scalar
                 copy_out(y_slots[:, e * C : (e + 1) * C], y_acc[:])
-            else:
-                waiting.append(hidden(accs3, silus))
-        late = [
-            quantize_w2(
-                w2_raw[:, e],
-                on_scalar,
-                raw3[:, 1, 2, 2 * N :].bitcast(BF16).rearrange("p (n j) -> p n j", j=PACK),
-            )
-            for e in range(EARLY_W2, E)
-        ]
-        for b, h_quantized in enumerate(waiting):
-            e = EARLY_W2 + b
-            y_acc = psum_y.tile([P, C], F32, name="acc")
-            second_layer(y_acc[:], late[b], h_quantized)
-            on_vector(y_slots[:, e * C : (e + 1) * C], y_acc[:])
+        e = LAST_ROUTED
+        rounded2 = w2_tile(small_pool, "rounded2")
+        round_w2(rounded2, w2_raw[:, e], on_vector)
+        h_groups = [multiply_group(accs3[b], silus[b]) for b in range(C // GROUP)]
+        weights2 = quantize_rounded_w2(rounded2)
+        h_quantized = [quantize_group(h) for h in h_groups]
+        for b in range(C // GROUP):
+            y_acc = psum_y.tile([P, GROUP], F32, name="acc")
+            second_layer(y_acc[:], weights2, h_quantized[b])
+            on_vector(y_slots[:, group_cols(e * C, b)], y_acc[:])
 
 
-        raw1, weights1 = load_and_quantize(w1[SHARED], (scalar_alone, scalar_alone), False)
+        raw1, weights1 = load_and_quantize(w1[SHARED], ((on_scalar,), (on_scalar,)), False)
         accs = [
             first_layer(weights1, token_words, token_scales, group_cols(0, b), psum_a1)
             for b in range(T // GROUP)
         ]
-        raw3, weights3, last_rounded = load_and_quantize_finely(w3[SHARED], scalar_alone, FINE_H, scalar_alone)
+        raw3, weights3, last_rounded = load_and_quantize_finely(w3[SHARED], (on_scalar,), FINE_H, (on_vector, on_scalar), True)
 
         nc.sync.dma_start(w2_raw[:, SHARED], w2_rows[:, SHARED])
         silus = []
@@ -335,7 +366,8 @@ def tile_moe_shr_glu_silu_kernel(
                 pair = rounded_pool.tile([P, 2, GROUP, PACK], F32, name="rounded", align_bytes=MX_ALIGN)
             silus.append(silu_into(pair[:, b % 2], accs[b]))
             if b == 2:
-                weights2 = quantize_w2(w2_raw[:, SHARED], on_scalar, w2_tile(rounded_pool, "rounded"))
+                shared_rounded2 = w2_tile(rounded_pool, "rounded")
+                round_w2(shared_rounded2, w2_raw[:, SHARED], on_scalar)
 
         accs3 = [
             first_layer(weights3, token_words, token_scales, group_cols(0, b), psum_a3)
@@ -345,8 +377,8 @@ def tile_moe_shr_glu_silu_kernel(
         def spent_part(raw, o, index):
             return raw[:, o, index // 2, index % 2 * C : (index % 2 + 1) * C]
 
-        pick_places = [None, None, spent_part(raw1, 0, 0), spent_part(raw1, 0, 1), spent_part(raw1, 1, 0), spent_part(raw1, 1, 1)]
-        sum_places = [spent_part(raw1, 0, 2), spent_part(raw1, 1, 2), codes_pool.tile([P, C], F32, name="codes", align_bytes=MX_ALIGN)[:]]
+        pick_places = [None, None, spent_part(raw1, 0, 0), spent_part(raw1, 0, 1), spent_part(raw1, 1, 0), codes_pool.tile([P, C], F32, name="codes", align_bytes=MX_ALIGN)[:]]
+        sum_places = [last_rounded[:, 2].rearrange("p m j -> p (m j)").bitcast(F32), last_rounded[:, 3].rearrange("p m j -> p (m j)").bitcast(F32), last_rounded[:, 1].rearrange("p m j -> p (m j)").bitcast(F32)]
         routed = []
         for c in range(T // C):
             picks = []
@@ -364,7 +396,7 @@ def tile_moe_shr_glu_silu_kernel(
                 )
                 picks.append(pick)
             combined = sum_places[c]
-            nc.vector.tensor_tensor(combined, picks[0], picks[1], ADD)
+            nc.gpsimd.tensor_tensor(combined, picks[0], picks[1], ADD)
             routed.append(combined)
 
         def tail_tile(shape, dtype):
@@ -382,6 +414,11 @@ def tile_moe_shr_glu_silu_kernel(
                 MULT,
             )
 
+        shared_w2 = []
+
+        def quantize_shared_w2(c):
+            shared_w2.append(quantize_rounded_w2(shared_rounded2, tail_tile([P, N], U32)))
+
         def quantize_h(c):
             h_codes = tail_tile([P, C], U32)
             h_scales = small_pool.tile([P, C], U8, name="h_scales", align_bytes=MX_ALIGN)
@@ -391,7 +428,7 @@ def tile_moe_shr_glu_silu_kernel(
                 in_=h_tiles[c][:].rearrange("p n t -> p (n t)"),
             )
             y_acc = psum_y.tile([P, C], F32, name="acc")
-            second_layer(y_acc[:], weights2, (h_codes, h_scales))
+            second_layer(y_acc[:], shared_w2[0], (h_codes, h_scales))
             quantized[c] = y_acc
 
         def finish(c):
@@ -402,12 +439,13 @@ def tile_moe_shr_glu_silu_kernel(
         multiply(0)
         multiply(1)
         multiply(2)
-        quantize_h(0)
         multiply(3)
+        quantize_shared_w2(0)
         multiply(4)
-        quantize_h(1)
+        quantize_h(0)
         multiply(5)
-        finish(0)
+        quantize_h(1)
         quantize_h(2)
+        finish(0)
         finish(1)
         finish(2)

@@ -28,7 +28,7 @@ MX_ALIGN = 64
 DMA_ALIGN = 256
 A1_BANKS = 4
 WHOLE_LOADS = 4
-EARLY_W2 = 5
+EARLY_W2 = 4
 FINE_D = 2
 FINE_H = 1
 GATHER = 512
@@ -127,7 +127,7 @@ def tile_moe_shr_glu_silu_kernel(
         def quantize_loaded(raw, copies):
             return [quantize_pass(raw[:, o], copies) for o in range(PASSES)]
 
-        def load_and_quantize(matrix, copies, whole):
+        def load_and_quantize(matrix, copies, whole, between=None):
             if whole:
                 raw = load_whole(matrix)
                 return raw, [quantize_pass(raw[:, o], copies[o]) for o in range(PASSES)]
@@ -135,6 +135,8 @@ def tile_moe_shr_glu_silu_kernel(
             quantized = []
             for o in range(PASSES):
                 nc.sync.dma_start(raw[:, o], by_pass(matrix)[:, o])
+                if o == 0 and between is not None:
+                    between()
                 quantized.append(quantize_pass(raw[:, o], copies[o]))
             return raw, quantized
 
@@ -200,8 +202,8 @@ def tile_moe_shr_glu_silu_kernel(
             return h
 
         def quantize_group(h):
-            h_codes = small_pool.tile([P, GROUP], U32, name="h_codes", align_bytes=MX_ALIGN)
-            h_scales = small_pool.tile([P, GROUP], U8, name="h_scales", align_bytes=MX_ALIGN)
+            h_codes = small_pool.tile([P, GROUP], U32, name="h_codes", align_bytes=MX_ALIGN, bufs=4)
+            h_scales = small_pool.tile([P, GROUP], U8, name="h_scales", align_bytes=MX_ALIGN, bufs=4)
             nc.vector.quantize_mx(
                 out=h_codes[:].bitcast(FP8X4),
                 scales=h_scales[:],
@@ -209,8 +211,8 @@ def tile_moe_shr_glu_silu_kernel(
             )
             return h_codes, h_scales
 
-        def w2_tile(pool, name):
-            return pool.tile([P, N, PACK], BF16, name=name, align_bytes=MX_ALIGN)[:]
+        def w2_tile(pool, name, bufs=None):
+            return pool.tile([P, N, PACK], BF16, name=name, align_bytes=MX_ALIGN, bufs=bufs)[:]
 
         def first_layer(weights, words, scales, cols, pool):
             acc = pool.tile([P, PACK, GROUP], F32, name="acc")
@@ -249,8 +251,8 @@ def tile_moe_shr_glu_silu_kernel(
                     silu,
                     MULT,
                 )
-            h_codes = small_pool.tile([P, width], U32, name="h_codes", align_bytes=MX_ALIGN)
-            h_scales = small_pool.tile([P, width], U8, name="h_scales", align_bytes=MX_ALIGN)
+            h_codes = small_pool.tile([P, width], U32, name="h_codes", align_bytes=MX_ALIGN, bufs=4)
+            h_scales = small_pool.tile([P, width], U8, name="h_scales", align_bytes=MX_ALIGN, bufs=4)
             nc.vector.quantize_mx(
                 out=h_codes[:].bitcast(FP8X4),
                 scales=h_scales[:],
@@ -277,6 +279,10 @@ def tile_moe_shr_glu_silu_kernel(
         pos_sb = [
             keep.tile([P, T // 16], U16, name=f"pos_sb{r}", align_bytes=DMA_ALIGN) for r in range(2)
         ]
+
+        def load_pos():
+            nc.sync.dma_start(pos_sb[0][:], pos1)
+            nc.sync.dma_start(pos_sb[1][:], pos2)
 
         first_raw = load_whole(w1[0])
         for q in range(4):
@@ -320,8 +326,7 @@ def tile_moe_shr_glu_silu_kernel(
             else:
                 raw3, weights3 = load_and_quantize_finely(w3[e], copies, FINE_D, (on_vector, on_scalar))[:2]
                 nc.sync.dma_start(w2_raw[:, EARLY_W2:E], w2_rows[:, EARLY_W2:E])
-                nc.sync.dma_start(pos_sb[0][:], pos1)
-                nc.sync.dma_start(pos_sb[1][:], pos2)
+
             if e == 0:
                 nc.sync.dma_start(w2_raw[:, :EARLY_W2], w2_rows[:, :EARLY_W2])
 
@@ -334,25 +339,38 @@ def tile_moe_shr_glu_silu_kernel(
                 for b in range(C // GROUP)
             ]
             if e < EARLY_W2:
-                weights2 = quantize_w2(w2_raw[:, e], on_vector, w2_tile(small_pool, "rounded2"))
+                weights2 = quantize_w2(w2_raw[:, e], on_vector, w2_tile(small_pool, "rounded2", 1))
                 h_quantized = hidden(accs3, silus)
                 y_acc = psum_y.tile([P, C], F32, name="acc")
                 second_layer(y_acc[:], weights2, h_quantized)
                 copy_out = on_vector if e < LAST_ROUTED else on_scalar
                 copy_out(y_slots[:, e * C : (e + 1) * C], y_acc[:])
-        e = LAST_ROUTED
-        rounded2 = w2_tile(small_pool, "rounded2")
-        round_w2(rounded2, w2_raw[:, e], on_vector)
+            elif e < LAST_ROUTED:
+                waiting.append(hidden(accs3, silus))
+        late = E - EARLY_W2
+        rounded2 = raw3[:, 1, 2, H - late * 2 * N :].bitcast(BF16).rearrange("p (e n j) -> p e n j", e=late, j=PACK)
+        for b in range(late):
+            round_w2(rounded2[:, b], w2_raw[:, EARLY_W2 + b], on_vector)
         h_groups = [multiply_group(accs3[b], silus[b]) for b in range(C // GROUP)]
-        weights2 = quantize_rounded_w2(rounded2)
+        codes2 = small_pool.tile([P, late, N], U32, name="h", align_bytes=MX_ALIGN)
+        scales2 = small_pool.tile([P, late, N], U8, name="scales2", align_bytes=MX_ALIGN)
+        nc.vector.quantize_mx(
+            out=codes2[:].rearrange("p e n -> p (e n)").bitcast(FP8X4),
+            scales=scales2[:].rearrange("p e n -> p (e n)"),
+            in_=rounded2.rearrange("p e n j -> p (e n j)"),
+        )
         h_quantized = [quantize_group(h) for h in h_groups]
+        for b, held in enumerate(waiting):
+            y_acc = psum_y.tile([P, C], F32, name="acc")
+            second_layer(y_acc[:], (codes2[:, b], scales2[:, b]), held)
+            on_scalar(y_slots[:, (EARLY_W2 + b) * C : (EARLY_W2 + b + 1) * C], y_acc[:])
         for b in range(C // GROUP):
             y_acc = psum_y.tile([P, GROUP], F32, name="acc")
-            second_layer(y_acc[:], weights2, h_quantized[b])
-            on_vector(y_slots[:, group_cols(e * C, b)], y_acc[:])
+            second_layer(y_acc[:], (codes2[:, late - 1], scales2[:, late - 1]), h_quantized[b])
+            on_scalar(y_slots[:, group_cols(LAST_ROUTED * C, b)], y_acc[:])
 
 
-        raw1, weights1 = load_and_quantize(w1[SHARED], ((on_scalar,), (on_scalar,)), False)
+        raw1, weights1 = load_and_quantize(w1[SHARED], (both_engines, (on_scalar,)), False, load_pos)
         accs = [
             first_layer(weights1, token_words, token_scales, group_cols(0, b), psum_a1)
             for b in range(T // GROUP)
@@ -421,7 +439,7 @@ def tile_moe_shr_glu_silu_kernel(
 
         def quantize_h(c):
             h_codes = tail_tile([P, C], U32)
-            h_scales = small_pool.tile([P, C], U8, name="h_scales", align_bytes=MX_ALIGN)
+            h_scales = small_pool.tile([P, C], U8, name="h_scales", align_bytes=MX_ALIGN, bufs=4)
             nc.vector.quantize_mx(
                 out=h_codes[:].bitcast(FP8X4),
                 scales=h_scales[:],

@@ -108,9 +108,15 @@ def tile_moe_shr_glu_silu_kernel(
                 pair = slice(width * part, width * (part + 1))
                 copy(dst[:, m_range, :, pair], src[:, m_range, :, pair])
 
-        def quantize_pass(raw_pass, copies):
+        def round_pass(raw_pass, copies):
             rounded = rounded_tile()
             round_columns(rounded, raw_pass, copies, slice(0, P))
+            return rounded
+
+        def quantize_pass(raw_pass, copies):
+            return quantize_rounded(round_pass(raw_pass, copies))
+
+        def quantize_rounded(rounded):
             codes, scales = code_tiles(H)
             nc.vector.quantize_mx(
                 out=codes[:].bitcast(FP8X4),
@@ -240,9 +246,9 @@ def tile_moe_shr_glu_silu_kernel(
         def group_cols(first, b):
             return slice(first + b * GROUP, first + (b + 1) * GROUP)
 
-        def hidden(accs3, silus):
+        def hidden(accs3, silus, pool, name):
             width = len(silus) * GROUP
-            h = small_pool.tile([P, width, PACK], BF16, name="h", align_bytes=MX_ALIGN)
+            h = pool.tile([P, width, PACK], BF16, name=name, align_bytes=MX_ALIGN)
             for b, silu in enumerate(silus):
                 acc = accs3[b]
                 nc.vector.tensor_tensor(
@@ -308,15 +314,22 @@ def tile_moe_shr_glu_silu_kernel(
             gathered.append((slot_words, slot_scales))
 
         waiting = []
+        ahead = None
+        copies = both_engines
         for e in range(E):
             slot_words, slot_scales = gathered[e * C // GATHER]
             first = e * C % GATHER
             if e == 0:
                 copies = scalar_alone
                 raw1, weights1 = first_raw, quantize_loaded(first_raw, copies)
-            else:
+            elif ahead is None:
                 copies = both_engines
                 raw1, weights1 = load_and_quantize(w1[e], (copies,copies), e < WHOLE_LOADS)
+            else:
+                copies = both_engines
+                raw1, weights1 = ahead
+                nc.sync.dma_start(raw1[:, 1], by_pass(w1[e])[:, 1])
+                weights1.append(quantize_pass(raw1[:, 1], copies))
             accs = [
                 first_layer(weights1, slot_words, slot_scales, group_cols(first, b), psum_a1)
                 for b in range(C // GROUP)
@@ -338,32 +351,47 @@ def tile_moe_shr_glu_silu_kernel(
                 first_layer(weights3, slot_words, slot_scales, group_cols(first, b), psum_a3)
                 for b in range(C // GROUP)
             ]
+            h_place = (small_pool, "h")
+            if WHOLE_LOADS <= e + 1 < E:
+                next_raw = raw_tile()
+                nc.sync.dma_start(next_raw[:, 0], by_pass(w1[e + 1])[:, 0])
+                next_rounded = round_pass(next_raw[:, 0], both_engines)
+                h_place = (rounded_pool, "rounded")
+            if e < LAST_ROUTED:
+                h_quantized = hidden(accs3, silus, *h_place)
+            if WHOLE_LOADS <= e + 1 < E:
+                ahead = (next_raw, [quantize_rounded(next_rounded)])
             if e < EARLY_W2:
                 weights2 = quantize_w2(w2_raw[:, e], on_vector, w2_tile(small_pool, "rounded2", 1))
-                h_quantized = hidden(accs3, silus)
                 y_acc = psum_y.tile([P, C], F32, name="acc")
                 second_layer(y_acc[:], weights2, h_quantized)
                 copy_out = on_vector if e < LAST_ROUTED else on_scalar
                 copy_out(y_slots[:, e * C : (e + 1) * C], y_acc[:])
             elif e < LAST_ROUTED:
-                waiting.append(hidden(accs3, silus))
+                waiting.append(h_quantized)
         late = E - EARLY_W2
-        rounded2 = raw3[:, 1, 2, H - late * 2 * N :].bitcast(BF16).rearrange("p (e n j) -> p e n j", e=late, j=PACK)
-        for b in range(late):
-            round_w2(rounded2[:, b], w2_raw[:, EARLY_W2 + b], on_vector)
+        rounded2 = (
+            raw3[:, 1, 2:]
+            .rearrange("p j i -> p (j i)")[:, 2 * H - late * 2 * N :]
+            .bitcast(BF16)
+            .rearrange("p (e n j) -> p e n j", e=late, j=PACK)
+        )
+        for b, copy in zip(reversed(range(late)), (on_vector, on_vector)):
+            round_w2(rounded2[:, b], w2_raw[:, EARLY_W2 + b], copy)
         h_groups = [multiply_group(accs3[b], silus[b]) for b in range(C // GROUP)]
         codes2 = small_pool.tile([P, late, N], U32, name="h", align_bytes=MX_ALIGN)
         scales2 = small_pool.tile([P, late, N], U8, name="scales2", align_bytes=MX_ALIGN)
-        nc.vector.quantize_mx(
-            out=codes2[:].rearrange("p e n -> p (e n)").bitcast(FP8X4),
-            scales=scales2[:].rearrange("p e n -> p (e n)"),
-            in_=rounded2.rearrange("p e n j -> p (e n j)"),
-        )
+        for a, z in ((0, 2),):
+            nc.vector.quantize_mx(
+                out=codes2[:, a:z].rearrange("p e n -> p (e n)").bitcast(FP8X4),
+                scales=scales2[:, a:z].rearrange("p e n -> p (e n)"),
+                in_=rounded2[:, a:z].rearrange("p e n j -> p (e n j)"),
+            )
         h_quantized = [quantize_group(h) for h in h_groups]
+        y_acc = psum_y.tile([P, len(waiting) * C], F32, name="acc")
         for b, held in enumerate(waiting):
-            y_acc = psum_y.tile([P, C], F32, name="acc")
-            second_layer(y_acc[:], (codes2[:, b], scales2[:, b]), held)
-            on_scalar(y_slots[:, (EARLY_W2 + b) * C : (EARLY_W2 + b + 1) * C], y_acc[:])
+            second_layer(y_acc[:, b * C : (b + 1) * C], (codes2[:, b], scales2[:, b]), held)
+        on_scalar(y_slots[:, EARLY_W2 * C : LAST_ROUTED * C], y_acc[:])
         for b in range(C // GROUP):
             y_acc = psum_y.tile([P, GROUP], F32, name="acc")
             second_layer(y_acc[:], (codes2[:, late - 1], scales2[:, late - 1]), h_quantized[b])
@@ -406,12 +434,15 @@ def tile_moe_shr_glu_silu_kernel(
                     pick = small_pool.tile([P, C], F32, name=f"pick{r}", bufs=1)[:]
                 else:
                     pick = place
-                nc.vector.tensor_tensor(
-                    pick,
-                    y_slots[:].indirect(pos_sb[r][:, c * LIST_COLS : (c + 1) * LIST_COLS]),
-                    gate_sb[r][:, c * C : (c + 1) * C],
-                    MULT,
-                )
+                looked_up = y_slots[:].indirect(pos_sb[r][:, c * LIST_COLS : (c + 1) * LIST_COLS])
+                gate_part = gate_sb[r][:, c * C : (c + 1) * C]
+                if 2 * c + r in ():
+                    nc.vector.tensor_copy(pick, looked_up)
+                    product = (last_rounded[:, 0].rearrange("p m j -> p (m j)").bitcast(F32) if r == 0 else spent_part(raw1, 1, 2 + r))
+                    nc.gpsimd.tensor_tensor(product, pick, gate_part, MULT)
+                    pick = product
+                else:
+                    nc.vector.tensor_tensor(pick, looked_up, gate_part, MULT)
                 picks.append(pick)
             combined = sum_places[c]
             nc.gpsimd.tensor_tensor(combined, picks[0], picks[1], ADD)

@@ -43,9 +43,9 @@ def tile_moe_shr_glu_silu_kernel(
 
     with ExitStack() as ctx:
         keep = ctx.enter_context(tc.tile_pool(name="keep", bufs=1))
-        raw_pool = ctx.enter_context(tc.tile_pool(name="raw", bufs=7))
-        rounded_pool = ctx.enter_context(tc.tile_pool(name="rounded", bufs=6))
-        codes_pool = ctx.enter_context(tc.tile_pool(name="codes", bufs=9))
+        raw_pool = ctx.enter_context(tc.tile_pool(name="raw", bufs=6))
+        rounded_pool = ctx.enter_context(tc.tile_pool(name="rounded", bufs=10))
+        codes_pool = ctx.enter_context(tc.tile_pool(name="codes", bufs=8))
         small_pool = ctx.enter_context(tc.tile_pool(name="small", bufs=T // C))
         tail_pool = ctx.enter_context(tc.tile_pool(name="tail", bufs=7))
         psum_a1 = ctx.enter_context(tc.psum_pool(name="psum", bufs=8))
@@ -103,6 +103,10 @@ def tile_moe_shr_glu_silu_kernel(
         def round_columns(rounded, raw_pass, copies, m_range):
             src = raw_pass.rearrange("p j (m t) -> p m j t", t=PACK)
             dst = rounded[:].rearrange("p t m j -> p m j t")
+            if isinstance(copies, int):
+                on_vector(dst[:, :copies], src[:, :copies])
+                on_scalar(dst[:, copies:], src[:, copies:])
+                return
             width = PACK // len(copies)
             for part, copy in enumerate(copies):
                 pair = slice(width * part, width * (part + 1))
@@ -313,62 +317,112 @@ def tile_moe_shr_glu_silu_kernel(
             nc.vector.tensor_copy(slot_scales[:], token_scales[:].indirect(piece))
             gathered.append((slot_words, slot_scales))
 
-        waiting = []
-        ahead = None
-        copies = both_engines
-        for e in range(E):
-            slot_words, slot_scales = gathered[e * C // GATHER]
-            first = e * C % GATHER
-            if e == 0:
-                copies = scalar_alone
-                raw1, weights1 = first_raw, quantize_loaded(first_raw, copies)
-            elif ahead is None:
-                copies = both_engines
-                raw1, weights1 = load_and_quantize(w1[e], (copies,copies), e < WHOLE_LOADS)
-            else:
-                copies = both_engines
-                raw1, weights1 = ahead
-                nc.sync.dma_start(raw1[:, 1], by_pass(w1[e])[:, 1])
-                weights1.append(quantize_pass(raw1[:, 1], copies))
-            accs = [
-                first_layer(weights1, slot_words, slot_scales, group_cols(first, b), psum_a1)
-                for b in range(C // GROUP)
-            ]
-            if e < LAST_ROUTED:
-                raw3, weights3 = load_and_quantize(w3[e], (copies,copies), e < WHOLE_LOADS)
-            else:
-                raw3, weights3 = load_and_quantize_finely(w3[e], copies, FINE_D, (on_vector, on_scalar))[:2]
-                nc.sync.dma_start(w2_raw[:, EARLY_W2:E], w2_rows[:, EARLY_W2:E])
+        def chained(shape, dtype):
+            return rounded_pool.tile(shape, dtype, name="rounded", align_bytes=MX_ALIGN)
 
+        def quantize_chained(rounded):
+            codes = codes_pool.tile([P, H], U32, name="codes", align_bytes=MX_ALIGN)
+            scales = chained([P, H], U8)
+            nc.vector.quantize_mx(
+                out=codes[:].bitcast(FP8X4),
+                scales=scales[:],
+                in_=rounded[:].rearrange("p t m j -> p (t m j)"),
+            )
+            return by_t(codes, scales, PACK)
+
+        def add_pass(accs, weights, e, o):
+            slot_words, slot_scales = gathered[e * C // GATHER]
+            for b, acc in enumerate(accs):
+                cols = group_cols(e * C % GATHER, b)
+                for t in range(PACK):
+                    nc.tensor.matmul_mx(
+                        out=acc[:, t, :],
+                        lhsT=weights[t][0].bitcast(FP8X4),
+                        lhsT_scale=weights[t][1],
+                        rhs=slot_words[o][:, cols].bitcast(FP8X4),
+                        rhs_scale=slot_scales[4 * o : P, cols],
+                        start=(o == 0 and t == 0),
+                        stop=(o == PASSES - 1 and t == PACK - 1),
+                    )
+
+        def new_banks():
+            return [psum_a1.tile([P, PACK, GROUP], F32, name="acc") for b in range(C // GROUP)]
+
+        def load_and_round(raw, matrix, o, whole, copies):
+            if not whole:
+                nc.sync.dma_start(raw[:, o], by_pass(matrix)[:, o])
+            elif o == 0 and matrix is not None:
+                nc.sync.dma_start(raw[:], by_pass(matrix))
+            return round_pass(raw[:, o], copies)
+
+        waiting = []
+        for e in range(E):
+            copies = scalar_alone if e == 0 else 56
+            whole1, whole3 = e < 4, e < WHOLE_LOADS
+            raw1 = first_raw if e == 0 else raw_tile()
+            rounded_a = load_and_round(raw1, None if e == 0 else w1[e], 0, whole1, copies)
+            if e > 0:
+                add_pass(accs3, quantize_chained(rounded_d), e - 1, 1)
+            rounded_b = load_and_round(raw1, w1[e], 1, whole1, copies)
+            if e > 0:
+                h = chained([P, C, PACK], BF16)
+                for b in range(C // GROUP):
+                    nc.vector.tensor_tensor(
+                        h[:, group_cols(0, b)], accs3[b][:].rearrange("p t n -> p n t"), silus[b], MULT
+                    )
+            accs = new_banks()
+            add_pass(accs, quantize_chained(rounded_a), e, 0)
+            raw3 = raw_tile()
+            rounded_c = load_and_round(raw3, w3[e], 0, whole3, copies)
             if e == 0:
                 nc.sync.dma_start(w2_raw[:, :EARLY_W2], w2_rows[:, :EARLY_W2])
-
-            silus = [
-                silu_into(spent_row(raw3, b, 1), acc)
-                for b, acc in enumerate(accs)
-            ]
-            accs3 = [
-                first_layer(weights3, slot_words, slot_scales, group_cols(first, b), psum_a3)
-                for b in range(C // GROUP)
-            ]
-            h_place = (small_pool, "h")
-            if WHOLE_LOADS <= e + 1 < E:
-                next_raw = raw_tile()
-                nc.sync.dma_start(next_raw[:, 0], by_pass(w1[e + 1])[:, 0])
-                next_rounded = round_pass(next_raw[:, 0], both_engines)
-                h_place = (rounded_pool, "rounded")
+            if e > 0:
+                h_codes = small_pool.tile([P, C], U32, name="h_codes", align_bytes=MX_ALIGN, bufs=4)
+                h_scales = chained([P, C], U8)
+                nc.vector.quantize_mx(
+                    out=h_codes[:].bitcast(FP8X4),
+                    scales=h_scales[:],
+                    in_=h[:].rearrange("p n t -> p (n t)"),
+                )
+                if e - 1 < EARLY_W2:
+                    y_acc = psum_y.tile([P, C], F32, name="acc")
+                    second_layer(y_acc[:], weights2, (h_codes, h_scales))
+                else:
+                    waiting.append((h_codes, h_scales))
+            add_pass(accs, quantize_chained(rounded_b), e, 1)
             if e < LAST_ROUTED:
-                h_quantized = hidden(accs3, silus, *h_place)
-            if WHOLE_LOADS <= e + 1 < E:
-                ahead = (next_raw, [quantize_rounded(next_rounded)])
-            if e < EARLY_W2:
-                weights2 = quantize_w2(w2_raw[:, e], on_vector, w2_tile(small_pool, "rounded2", 1))
-                y_acc = psum_y.tile([P, C], F32, name="acc")
-                second_layer(y_acc[:], weights2, h_quantized)
-                copy_out = on_vector if e < LAST_ROUTED else on_scalar
-                copy_out(y_slots[:, e * C : (e + 1) * C], y_acc[:])
-            elif e < LAST_ROUTED:
-                waiting.append(h_quantized)
+                rounded_d = load_and_round(raw3, w3[e], 1, whole3, copies)
+                if 0 < e <= EARLY_W2:
+                    on_vector(y_slots[:, (e - 1) * C : e * C], y_acc[:])
+                if e < EARLY_W2:
+                    rounded2 = chained([P, N, PACK], BF16)[:]
+                    round_w2(rounded2, w2_raw[:, e], on_vector)
+                accs3 = new_banks()
+                add_pass(accs3, quantize_chained(rounded_c), e, 0)
+                if e < EARLY_W2:
+                    weights2 = quantize_rounded_w2(rounded2)
+            else:
+                rounded_d = rounded_tile()
+                accs3 = new_banks()
+                for piece in range(FINE_D):
+                    cols = slice(piece * H // FINE_D, (piece + 1) * H // FINE_D)
+                    nc.sync.dma_start(raw3[:, 1, :, cols], by_pass(w3[e])[:, 1, :, cols])
+                    m_range = slice(piece * P // FINE_D, (piece + 1) * P // FINE_D)
+                    round_columns(rounded_d, raw3[:, 1], (on_vector, on_scalar), m_range)
+                    if piece == 0:
+                        add_pass(accs3, quantize_chained(rounded_c), e, 0)
+                nc.sync.dma_start(w2_raw[:, EARLY_W2:E], w2_rows[:, EARLY_W2:E])
+                halves = []
+                for half in range(2):
+                    codes, scales = code_tiles(H // 2)
+                    nc.vector.quantize_mx(
+                        out=codes[:].bitcast(FP8X4),
+                        scales=scales[:],
+                        in_=rounded_d[:, 2 * half : 2 * half + 2].rearrange("p t m j -> p (t m j)"),
+                    )
+                    halves.extend(by_t(codes, scales, 2))
+                add_pass(accs3, halves, e, 1)
+            silus = [silu_into(spent_row(raw3, b, 1), acc) for b, acc in enumerate(accs)]
         late = E - EARLY_W2
         rounded2 = (
             raw3[:, 1, 2:]
@@ -391,14 +445,14 @@ def tile_moe_shr_glu_silu_kernel(
         y_acc = psum_y.tile([P, len(waiting) * C], F32, name="acc")
         for b, held in enumerate(waiting):
             second_layer(y_acc[:, b * C : (b + 1) * C], (codes2[:, b], scales2[:, b]), held)
-        on_scalar(y_slots[:, EARLY_W2 * C : LAST_ROUTED * C], y_acc[:])
+        on_vector(y_slots[:, EARLY_W2 * C : LAST_ROUTED * C], y_acc[:])
         for b in range(C // GROUP):
             y_acc = psum_y.tile([P, GROUP], F32, name="acc")
             second_layer(y_acc[:], (codes2[:, late - 1], scales2[:, late - 1]), h_quantized[b])
-            on_scalar(y_slots[:, group_cols(LAST_ROUTED * C, b)], y_acc[:])
+            on_vector(y_slots[:, group_cols(LAST_ROUTED * C, b)], y_acc[:])
 
 
-        raw1, weights1 = load_and_quantize(w1[SHARED], (both_engines, (on_scalar,)), False, load_pos)
+        raw1, weights1 = load_and_quantize(w1[SHARED], ((on_scalar,), (on_scalar,)), False, load_pos)
         accs = [
             first_layer(weights1, token_words, token_scales, group_cols(0, b), psum_a1)
             for b in range(T // GROUP)

@@ -21,36 +21,147 @@ P = 128
 PACK = 4
 PASSES = K // (P * PACK)
 GROUP = 128
+LINE = 4
 LIST_COLS = C // 16
+GATHER = 2 * C
 SHARED = E
-LAST_ROUTED = E - 1
+LAST = E - 1
 MX_ALIGN = 64
 DMA_ALIGN = 256
-A1_BANKS = 4
+
 WHOLE_LOADS = 4
-EARLY_W2 = 4
-FINE_D = 2
-FINE_H = 1
-GATHER = 512
-SHARED_RANGES = ((0, 2), (2, 4), (4, 5), (5, 6))
+EARLY_W2 = E - 2
+ROUTED_SHARE = 56
+SHARED_W1_SHARE = 32
+SHARED_W3_SHARE = 16
 
 
 def tile_moe_shr_glu_silu_kernel(
     tc, x_words, x_scales, w1, w3, w2, gate, offs, pos1, pos2, out
 ):
     nc = tc.nc
-    on_scalar, on_vector = nc.scalar.copy, nc.vector.tensor_copy
 
     with ExitStack() as ctx:
         keep = ctx.enter_context(tc.tile_pool(name="keep", bufs=1))
         raw_pool = ctx.enter_context(tc.tile_pool(name="raw", bufs=6))
-        rounded_pool = ctx.enter_context(tc.tile_pool(name="rounded", bufs=10))
-        codes_pool = ctx.enter_context(tc.tile_pool(name="codes", bufs=8))
+        chain_pool = ctx.enter_context(tc.tile_pool(name="chain", bufs=10))
+        codes_pool = ctx.enter_context(tc.tile_pool(name="codes", bufs=9))
         small_pool = ctx.enter_context(tc.tile_pool(name="small", bufs=T // C))
         tail_pool = ctx.enter_context(tc.tile_pool(name="tail", bufs=7))
-        psum_a1 = ctx.enter_context(tc.psum_pool(name="psum", bufs=8))
-        psum_a3 = psum_a1
-        psum_y = psum_a1
+        psum = ctx.enter_context(tc.psum_pool(name="psum", bufs=8))
+
+        def chained(shape, dtype):
+            return chain_pool.tile(shape, dtype, name="chained", align_bytes=MX_ALIGN)
+
+        def codes_tile(shape, dtype):
+            return codes_pool.tile(shape, dtype, name="codes", align_bytes=MX_ALIGN)
+
+        def scales_tile(width):
+            return codes_pool.tile([P, width], U8, name="scales", align_bytes=MX_ALIGN)
+
+        def small(shape, dtype, name):
+            return small_pool.tile(shape, dtype, name=name, align_bytes=MX_ALIGN)
+
+        def hidden_tile(width, dtype, name):
+            return small_pool.tile([P, width], dtype, name=name, align_bytes=MX_ALIGN, bufs=4)
+
+        def tail_tile(shape, dtype):
+            return tail_pool.tile(shape, dtype, name="tail", align_bytes=DMA_ALIGN)
+
+        def bank(shape):
+            return psum.tile(shape, F32, name="bank")
+
+        def raw_tile():
+            return raw_pool.tile([P, PASSES, PACK, H], F32, name="raw", align_bytes=DMA_ALIGN)
+
+        def by_pass(matrix):
+            return matrix.rearrange("(o p j) i -> p o j i", o=PASSES, j=PACK)
+
+        def group_cols(first, b):
+            return slice(first + b * GROUP, first + (b + 1) * GROUP)
+
+        def walks(rounded, rows):
+            return (
+                rounded[:].rearrange("p t m j -> p m j t"),
+                rows.rearrange("p j (m t) -> p m j t", t=PACK),
+            )
+
+        def round_pass(rows, vector_share):
+            rounded = chained([P, PACK, P, PACK], BF16)
+            dst, src = walks(rounded, rows)
+            if vector_share:
+                nc.vector.tensor_copy(dst[:, :vector_share], src[:, :vector_share])
+            nc.scalar.copy(dst[:, vector_share:], src[:, vector_share:])
+            return rounded
+
+        def round_by_t(rounded, rows, m_range):
+            dst, src = walks(rounded, rows)
+            nc.vector.tensor_copy(dst[:, m_range, :, :2], src[:, m_range, :, :2])
+            nc.scalar.copy(dst[:, m_range, :, 2:], src[:, m_range, :, 2:])
+
+        def round_w2(copy, rounded, rows):
+            copy(
+                rounded.rearrange("p (c u) j -> p c j u", u=LINE),
+                rows.rearrange("p j (c u) -> p c j u", u=LINE),
+            )
+
+        def quantize(values, codes, scales):
+            nc.vector.quantize_mx(out=codes[:].bitcast(FP8X4), scales=scales[:], in_=values)
+            return codes[:], scales[:]
+
+        def quantize_weights(rounded, codes, scales):
+            quantize(rounded.rearrange("p t m j -> p (t m j)"), codes, scales)
+            return [
+                (codes[:, t * P : (t + 1) * P], scales[:, t * P : (t + 1) * P])
+                for t in range(rounded.shape[1])
+            ]
+
+        def quantize_behind_rounding(rounded):
+            return quantize_weights(rounded[:], codes_tile([P, H], U32), chained([P, H], U8))
+
+        def quantize_halves(rounded):
+            return [
+                operand
+                for half in range(2)
+                for operand in quantize_weights(
+                    rounded[:, 2 * half : 2 * half + 2],
+                    codes_tile([P, H // 2], U32),
+                    scales_tile(H // 2),
+                )
+            ]
+
+        def add_pass(acc, weights, words, scales, cols, o):
+            for t in range(PACK):
+                nc.tensor.matmul_mx(
+                    out=acc[:, t, :],
+                    lhsT=weights[t][0].bitcast(FP8X4),
+                    lhsT_scale=weights[t][1],
+                    rhs=words[o][:, cols].bitcast(FP8X4),
+                    rhs_scale=scales[4 * o : P, cols],
+                    start=(o == 0 and t == 0),
+                    stop=(o == PASSES - 1 and t == PACK - 1),
+                )
+
+        def second_layer(y_acc, weights2, hidden):
+            nc.tensor.matmul_mx(
+                out=y_acc,
+                lhsT=weights2[0].bitcast(FP8X4),
+                lhsT_scale=weights2[1],
+                rhs=hidden[0].bitcast(FP8X4),
+                rhs_scale=hidden[1],
+                start=True,
+                stop=True,
+            )
+
+        def silu_into(dst, acc):
+            nc.scalar.activation(dst, acc[:].rearrange("p t n -> p n t"), SILU)
+            return dst
+
+        def multiply(h, acc, silu):
+            nc.vector.tensor_tensor(h, acc[:].rearrange("p t n -> p n t"), silu, MULT)
+
+        def spent_row(raw, row):
+            return raw[:, 1, row, :].rearrange("p (n t) -> p n t", t=PACK)
 
         token_scales = keep.tile([P, T], U8, name="token_scales", align_bytes=DMA_ALIGN)
         nc.vector.memset(token_scales[:].bitcast(I32), 0)
@@ -66,222 +177,22 @@ def tile_moe_shr_glu_silu_kernel(
         identity = keep.tile([P, P], F32, name="identity", align_bytes=MX_ALIGN)
         make_identity(nc, identity[:])
         gate_sb = [keep.tile([P, T], F32, name=f"gate_sb{r}") for r in range(2)]
-        for first, per in ((0, 4), (512, 2)):
+        for first, per in ((0, PACK), (P * PACK, 2)):
+            tokens = slice(first, first + P * per)
             column = keep.tile([P, 2, 8], F32, name=f"gate_column{per}")
             nc.scalar.dma_start(
-                column[:, :, :per],
-                gate[:, 0, first : first + P * per].rearrange("r (p c) -> p r c", c=per),
+                column[:, :, :per], gate[:, 0, tokens].rearrange("r (p c) -> p r c", c=per)
             )
             for r in range(2):
-                spread = psum_a1.tile([P, PACK, GROUP], F32, name="acc")
+                spread = bank([P, PACK, GROUP])
                 for c in range(per):
                     nc.tensor.transpose(
                         spread[:, c, :], column[:, r, c : c + 1].to_broadcast([P, P]), identity[:]
                     )
                 nc.scalar.copy(
-                    gate_sb[r][:, first : first + P * per].rearrange("p (n c) -> p n c", c=per),
+                    gate_sb[r][:, tokens].rearrange("p (n c) -> p n c", c=per),
                     spread[:, :per, :].rearrange("p c n -> p n c"),
                 )
-
-        def raw_tile():
-            return raw_pool.tile([P, PASSES, PACK, H], F32, name="raw", align_bytes=DMA_ALIGN)
-
-        def by_pass(matrix):
-            return matrix.rearrange("(o p j) i -> p o j i", o=PASSES, j=PACK)
-
-        def rounded_tile():
-            return rounded_pool.tile([P, PACK, P, PACK], BF16, name="rounded", align_bytes=MX_ALIGN)
-
-        def by_t(codes, scales, count):
-            return [(codes[:, t * P : (t + 1) * P], scales[:, t * P : (t + 1) * P]) for t in range(count)]
-
-        def code_tiles(width):
-            codes = codes_pool.tile([P, width], U32, name="codes", align_bytes=MX_ALIGN)
-            scales = codes_pool.tile([P, width], U8, name="scales", align_bytes=MX_ALIGN)
-            return codes, scales
-
-        def round_columns(rounded, raw_pass, copies, m_range):
-            src = raw_pass.rearrange("p j (m t) -> p m j t", t=PACK)
-            dst = rounded[:].rearrange("p t m j -> p m j t")
-            if isinstance(copies, int):
-                on_vector(dst[:, :copies], src[:, :copies])
-                on_scalar(dst[:, copies:], src[:, copies:])
-                return
-            width = PACK // len(copies)
-            for part, copy in enumerate(copies):
-                pair = slice(width * part, width * (part + 1))
-                copy(dst[:, m_range, :, pair], src[:, m_range, :, pair])
-
-        def round_pass(raw_pass, copies):
-            rounded = rounded_tile()
-            round_columns(rounded, raw_pass, copies, slice(0, P))
-            return rounded
-
-        def quantize_pass(raw_pass, copies):
-            return quantize_rounded(round_pass(raw_pass, copies))
-
-        def quantize_rounded(rounded):
-            codes, scales = code_tiles(H)
-            nc.vector.quantize_mx(
-                out=codes[:].bitcast(FP8X4),
-                scales=scales[:],
-                in_=rounded[:].rearrange("p t m j -> p (t m j)"),
-            )
-            return by_t(codes, scales, PACK)
-
-        def load_whole(matrix):
-            raw = raw_tile()
-            nc.sync.dma_start(raw[:], by_pass(matrix))
-            return raw
-
-        def quantize_loaded(raw, copies):
-            return [quantize_pass(raw[:, o], copies) for o in range(PASSES)]
-
-        def load_and_quantize(matrix, copies, whole, between=None):
-            if whole:
-                raw = load_whole(matrix)
-                return raw, [quantize_pass(raw[:, o], copies[o]) for o in range(PASSES)]
-            raw = raw_tile()
-            quantized = []
-            for o in range(PASSES):
-                nc.sync.dma_start(raw[:, o], by_pass(matrix)[:, o])
-                if o == 0 and between is not None:
-                    between()
-                quantized.append(quantize_pass(raw[:, o], copies[o]))
-            return raw, quantized
-
-        def load_and_quantize_finely(matrix, copies, pieces, last_copies, hold=False):
-            raw = raw_tile()
-            nc.sync.dma_start(raw[:, 0], by_pass(matrix)[:, 0])
-            if hold:
-                first_rounded = rounded_tile()
-                round_columns(first_rounded, raw[:, 0], copies, slice(0, P))
-            else:
-                quantized = [quantize_pass(raw[:, 0], copies)]
-            rounded = rounded_tile()
-            for piece in range(pieces):
-                cols = slice(piece * H // pieces, (piece + 1) * H // pieces)
-                nc.sync.dma_start(raw[:, 1, :, cols], by_pass(matrix)[:, 1, :, cols])
-                m_range = slice(piece * P // pieces, (piece + 1) * P // pieces)
-                round_columns(rounded, raw[:, 1], last_copies, m_range)
-            if hold:
-                codes = rounded_pool.tile([P, H], U32, name="rounded", align_bytes=MX_ALIGN)
-                scales = codes_pool.tile([P, H], U8, name="scales", align_bytes=MX_ALIGN)
-                nc.vector.quantize_mx(
-                    out=codes[:].bitcast(FP8X4),
-                    scales=scales[:],
-                    in_=first_rounded[:].rearrange("p t m j -> p (t m j)"),
-                )
-                quantized = [by_t(codes, scales, PACK)]
-            halves = []
-            for half in range(2):
-                codes, scales = code_tiles(H // 2)
-                nc.vector.quantize_mx(
-                    out=codes[:].bitcast(FP8X4),
-                    scales=scales[:],
-                    in_=rounded[:, 2 * half : 2 * half + 2].rearrange("p t m j -> p (t m j)"),
-                )
-                halves.extend(by_t(codes, scales, 2))
-            quantized.append(halves)
-            return raw, quantized, rounded
-
-        def round_w2(rounded2, raw2, copy):
-            copy(
-                rounded2.rearrange("p (c u) j -> p c j u", u=4),
-                raw2.rearrange("p j (c u) -> p c j u", u=4),
-            )
-
-        def quantize_rounded_w2(rounded2, codes2=None):
-            if codes2 is None:
-                codes2 = small_pool.tile([P, N], U32, name="codes2", align_bytes=MX_ALIGN)
-            scales2 = small_pool.tile([P, N], U8, name="scales2", align_bytes=MX_ALIGN)
-            nc.vector.quantize_mx(
-                out=codes2[:].bitcast(FP8X4),
-                scales=scales2[:],
-                in_=rounded2.rearrange("p n j -> p (n j)"),
-            )
-            return codes2[:], scales2[:]
-
-        def quantize_w2(raw2, copy, rounded2):
-            round_w2(rounded2, raw2, copy)
-            return quantize_rounded_w2(rounded2)
-
-        def multiply_group(acc, silu):
-            h = small_pool.tile([P, GROUP, PACK], BF16, name="h", align_bytes=MX_ALIGN)
-            nc.vector.tensor_tensor(h[:], acc[:].rearrange("p t n -> p n t"), silu, MULT)
-            return h
-
-        def quantize_group(h):
-            h_codes = small_pool.tile([P, GROUP], U32, name="h_codes", align_bytes=MX_ALIGN, bufs=4)
-            h_scales = small_pool.tile([P, GROUP], U8, name="h_scales", align_bytes=MX_ALIGN, bufs=4)
-            nc.vector.quantize_mx(
-                out=h_codes[:].bitcast(FP8X4),
-                scales=h_scales[:],
-                in_=h[:].rearrange("p n t -> p (n t)"),
-            )
-            return h_codes, h_scales
-
-        def w2_tile(pool, name, bufs=None):
-            return pool.tile([P, N, PACK], BF16, name=name, align_bytes=MX_ALIGN, bufs=bufs)[:]
-
-        def first_layer(weights, words, scales, cols, pool):
-            acc = pool.tile([P, PACK, GROUP], F32, name="acc")
-            for o in range(PASSES):
-                for t in range(PACK):
-                    w_codes, w_scales = weights[o][t]
-                    nc.tensor.matmul_mx(
-                        out=acc[:, t, :],
-                        lhsT=w_codes.bitcast(FP8X4),
-                        lhsT_scale=w_scales,
-                        rhs=words[o][:, cols].bitcast(FP8X4),
-                        rhs_scale=scales[4 * o : P, cols],
-                        start=(o == 0 and t == 0),
-                        stop=(o == PASSES - 1 and t == PACK - 1),
-                    )
-            return acc
-
-        def silu_into(dst, acc):
-            nc.scalar.activation(dst, acc[:].rearrange("p t n -> p n t"), SILU)
-            return dst
-
-        def spent_row(raw, row, o=1):
-            return raw[:, o, row, :].rearrange("p (n t) -> p n t", t=PACK)
-
-        def group_cols(first, b):
-            return slice(first + b * GROUP, first + (b + 1) * GROUP)
-
-        def hidden(accs3, silus, pool, name):
-            width = len(silus) * GROUP
-            h = pool.tile([P, width, PACK], BF16, name=name, align_bytes=MX_ALIGN)
-            for b, silu in enumerate(silus):
-                acc = accs3[b]
-                nc.vector.tensor_tensor(
-                    h[:, b * GROUP : (b + 1) * GROUP, :],
-                    acc[:].rearrange("p t n -> p n t"),
-                    silu,
-                    MULT,
-                )
-            h_codes = small_pool.tile([P, width], U32, name="h_codes", align_bytes=MX_ALIGN, bufs=4)
-            h_scales = small_pool.tile([P, width], U8, name="h_scales", align_bytes=MX_ALIGN, bufs=4)
-            nc.vector.quantize_mx(
-                out=h_codes[:].bitcast(FP8X4),
-                scales=h_scales[:],
-                in_=h[:].rearrange("p n t -> p (n t)"),
-            )
-            return h_codes, h_scales
-
-        def second_layer(y_acc, weights2, h_quantized):
-            codes2, scales2 = weights2
-            h_codes, h_scales = h_quantized
-            nc.tensor.matmul_mx(
-                out=y_acc,
-                lhsT=codes2.bitcast(FP8X4),
-                lhsT_scale=scales2,
-                rhs=h_codes[:].bitcast(FP8X4),
-                rhs_scale=h_scales[:],
-                start=True,
-                stop=True,
-            )
 
         y_slots = keep.tile([P, E * C], F32, name="y_slots")
         w2_raw = keep.tile([P, E + 1, PACK, N], F32, name="w2_raw", align_bytes=DMA_ALIGN)
@@ -290,20 +201,13 @@ def tile_moe_shr_glu_silu_kernel(
             keep.tile([P, T // 16], U16, name=f"pos_sb{r}", align_bytes=DMA_ALIGN) for r in range(2)
         ]
 
-        def load_pos():
-            nc.sync.dma_start(pos_sb[0][:], pos1)
-            nc.sync.dma_start(pos_sb[1][:], pos2)
-
-        first_raw = load_whole(w1[0])
+        first_raw = raw_tile()
+        nc.sync.dma_start(first_raw[:], by_pass(w1[0]))
         for q in range(4):
             nc.sync.dma_start(
                 token_scales[32 * q : 32 * q + 4 * PASSES, :].bitcast(I32),
                 x_scales[:, 4 * q : 4 * q + 4, :].bitcast(I32),
             )
-
-        both_engines = (on_scalar, on_vector)
-        scalar_alone = (on_scalar, on_scalar)
-        vector_alone = (on_vector, on_vector)
 
         gathered = []
         for g in range(E * C // GATHER):
@@ -317,238 +221,203 @@ def tile_moe_shr_glu_silu_kernel(
             nc.vector.tensor_copy(slot_scales[:], token_scales[:].indirect(piece))
             gathered.append((slot_words, slot_scales))
 
-        def chained(shape, dtype):
-            return rounded_pool.tile(shape, dtype, name="rounded", align_bytes=MX_ALIGN)
+        groups = range(C // GROUP)
 
-        def quantize_chained(rounded):
-            codes = codes_pool.tile([P, H], U32, name="codes", align_bytes=MX_ALIGN)
-            scales = chained([P, H], U8)
-            nc.vector.quantize_mx(
-                out=codes[:].bitcast(FP8X4),
-                scales=scales[:],
-                in_=rounded[:].rearrange("p t m j -> p (t m j)"),
-            )
-            return by_t(codes, scales, PACK)
-
-        def add_pass(accs, weights, e, o):
+        def add_slot_pass(accs, weights, e, o):
             slot_words, slot_scales = gathered[e * C // GATHER]
-            for b, acc in enumerate(accs):
-                cols = group_cols(e * C % GATHER, b)
-                for t in range(PACK):
-                    nc.tensor.matmul_mx(
-                        out=acc[:, t, :],
-                        lhsT=weights[t][0].bitcast(FP8X4),
-                        lhsT_scale=weights[t][1],
-                        rhs=slot_words[o][:, cols].bitcast(FP8X4),
-                        rhs_scale=slot_scales[4 * o : P, cols],
-                        start=(o == 0 and t == 0),
-                        stop=(o == PASSES - 1 and t == PACK - 1),
-                    )
+            for b in groups:
+                add_pass(accs[b], weights, slot_words, slot_scales, group_cols(e * C % GATHER, b), o)
 
-        def new_banks():
-            return [psum_a1.tile([P, PACK, GROUP], F32, name="acc") for b in range(C // GROUP)]
-
-        def load_and_round(raw, matrix, o, whole, copies):
+        def load(raw, matrix, o, whole):
             if not whole:
                 nc.sync.dma_start(raw[:, o], by_pass(matrix)[:, o])
-            elif o == 0 and matrix is not None:
+            elif o == 0:
                 nc.sync.dma_start(raw[:], by_pass(matrix))
-            return round_pass(raw[:, o], copies)
 
-        waiting = []
         for e in range(E):
-            copies = scalar_alone if e == 0 else 56
-            whole1, whole3 = e < 4, e < WHOLE_LOADS
-            raw1 = first_raw if e == 0 else raw_tile()
-            rounded_a = load_and_round(raw1, None if e == 0 else w1[e], 0, whole1, copies)
+            share = ROUTED_SHARE if e > 0 else 0
+            whole = e < WHOLE_LOADS
+            if e == 0:
+                raw1 = first_raw
+            else:
+                raw1 = raw_tile()
+                load(raw1, w1[e], 0, whole)
+            rounded_a = round_pass(raw1[:, 0], share)
             if e > 0:
-                add_pass(accs3, quantize_chained(rounded_d), e - 1, 1)
-            rounded_b = load_and_round(raw1, w1[e], 1, whole1, copies)
+                add_slot_pass(accs3, quantize_behind_rounding(rounded_d), e - 1, 1)
+
+            load(raw1, w1[e], 1, whole)
+            rounded_b = round_pass(raw1[:, 1], share)
             if e > 0:
                 h = chained([P, C, PACK], BF16)
-                for b in range(C // GROUP):
-                    nc.vector.tensor_tensor(
-                        h[:, group_cols(0, b)], accs3[b][:].rearrange("p t n -> p n t"), silus[b], MULT
-                    )
-            accs = new_banks()
-            add_pass(accs, quantize_chained(rounded_a), e, 0)
+                for b in groups:
+                    multiply(h[:, group_cols(0, b)], accs3[b], silus[b])
+            accs1 = [bank([P, PACK, GROUP]) for b in groups]
+            add_slot_pass(accs1, quantize_behind_rounding(rounded_a), e, 0)
+
             raw3 = raw_tile()
-            rounded_c = load_and_round(raw3, w3[e], 0, whole3, copies)
+            load(raw3, w3[e], 0, whole)
+            rounded_c = round_pass(raw3[:, 0], share)
             if e == 0:
                 nc.sync.dma_start(w2_raw[:, :EARLY_W2], w2_rows[:, :EARLY_W2])
-            if e > 0:
-                h_codes = small_pool.tile([P, C], U32, name="h_codes", align_bytes=MX_ALIGN, bufs=4)
-                h_scales = chained([P, C], U8)
-                nc.vector.quantize_mx(
-                    out=h_codes[:].bitcast(FP8X4),
-                    scales=h_scales[:],
-                    in_=h[:].rearrange("p n t -> p (n t)"),
+            else:
+                hidden = quantize(
+                    h[:].rearrange("p n t -> p (n t)"),
+                    hidden_tile(C, U32, "h_codes"),
+                    chained([P, C], U8),
                 )
                 if e - 1 < EARLY_W2:
-                    y_acc = psum_y.tile([P, C], F32, name="acc")
-                    second_layer(y_acc[:], weights2, (h_codes, h_scales))
-                else:
-                    waiting.append((h_codes, h_scales))
-            add_pass(accs, quantize_chained(rounded_b), e, 1)
-            if e < LAST_ROUTED:
-                rounded_d = load_and_round(raw3, w3[e], 1, whole3, copies)
-                if 0 < e <= EARLY_W2:
-                    on_vector(y_slots[:, (e - 1) * C : e * C], y_acc[:])
+                    y_acc = bank([P, C])
+                    second_layer(y_acc[:], weights2, hidden)
+            add_slot_pass(accs1, quantize_behind_rounding(rounded_b), e, 1)
+
+            if e < LAST:
+                load(raw3, w3[e], 1, whole)
+                rounded_d = round_pass(raw3[:, 1], share)
+                if e > 0:
+                    nc.vector.tensor_copy(y_slots[:, (e - 1) * C : e * C], y_acc[:])
                 if e < EARLY_W2:
-                    rounded2 = chained([P, N, PACK], BF16)[:]
-                    round_w2(rounded2, w2_raw[:, e], on_vector)
-                accs3 = new_banks()
-                add_pass(accs3, quantize_chained(rounded_c), e, 0)
+                    rounded2 = chained([P, N, PACK], BF16)
+                    round_w2(nc.vector.tensor_copy, rounded2[:], w2_raw[:, e])
+                accs3 = [bank([P, PACK, GROUP]) for b in groups]
+                add_slot_pass(accs3, quantize_behind_rounding(rounded_c), e, 0)
                 if e < EARLY_W2:
-                    weights2 = quantize_rounded_w2(rounded2)
-            else:
-                rounded_d = rounded_tile()
-                accs3 = new_banks()
-                for piece in range(FINE_D):
-                    cols = slice(piece * H // FINE_D, (piece + 1) * H // FINE_D)
-                    nc.sync.dma_start(raw3[:, 1, :, cols], by_pass(w3[e])[:, 1, :, cols])
-                    m_range = slice(piece * P // FINE_D, (piece + 1) * P // FINE_D)
-                    round_columns(rounded_d, raw3[:, 1], (on_vector, on_scalar), m_range)
-                    if piece == 0:
-                        add_pass(accs3, quantize_chained(rounded_c), e, 0)
-                nc.sync.dma_start(w2_raw[:, EARLY_W2:E], w2_rows[:, EARLY_W2:E])
-                halves = []
-                for half in range(2):
-                    codes, scales = code_tiles(H // 2)
-                    nc.vector.quantize_mx(
-                        out=codes[:].bitcast(FP8X4),
-                        scales=scales[:],
-                        in_=rounded_d[:, 2 * half : 2 * half + 2].rearrange("p t m j -> p (t m j)"),
+                    weights2 = quantize(
+                        rounded2[:].rearrange("p n j -> p (n j)"),
+                        small([P, N], U32, "codes2"),
+                        small([P, N], U8, "scales2"),
                     )
-                    halves.extend(by_t(codes, scales, 2))
-                add_pass(accs3, halves, e, 1)
-            silus = [silu_into(spent_row(raw3, b, 1), acc) for b, acc in enumerate(accs)]
+            else:
+                rounded_d = chained([P, PACK, P, PACK], BF16)
+                accs3 = [bank([P, PACK, GROUP]) for b in groups]
+                for half in range(2):
+                    cols = slice(half * H // 2, (half + 1) * H // 2)
+                    nc.sync.dma_start(raw3[:, 1, :, cols], by_pass(w3[e])[:, 1, :, cols])
+                    round_by_t(rounded_d, raw3[:, 1], slice(half * P // 2, (half + 1) * P // 2))
+                    if half == 0:
+                        add_slot_pass(accs3, quantize_behind_rounding(rounded_c), e, 0)
+                nc.sync.dma_start(w2_raw[:, EARLY_W2:E], w2_rows[:, EARLY_W2:E])
+                add_slot_pass(accs3, quantize_halves(rounded_d), e, 1)
+            silus = [silu_into(spent_row(raw3, b), accs1[b]) for b in groups]
+
         late = E - EARLY_W2
         rounded2 = (
-            raw3[:, 1, 2:]
-            .rearrange("p j i -> p (j i)")[:, 2 * H - late * 2 * N :]
-            .bitcast(BF16)
-            .rearrange("p (e n j) -> p e n j", e=late, j=PACK)
+            raw3[:, 1, PACK - 1].bitcast(BF16).rearrange("p (e n j) -> p e n j", e=late, j=PACK)
         )
-        for b, copy in zip(reversed(range(late)), (on_vector, on_vector)):
-            round_w2(rounded2[:, b], w2_raw[:, EARLY_W2 + b], copy)
-        h_groups = [multiply_group(accs3[b], silus[b]) for b in range(C // GROUP)]
-        codes2 = small_pool.tile([P, late, N], U32, name="h", align_bytes=MX_ALIGN)
-        scales2 = small_pool.tile([P, late, N], U8, name="scales2", align_bytes=MX_ALIGN)
-        for a, z in ((0, 2),):
-            nc.vector.quantize_mx(
-                out=codes2[:, a:z].rearrange("p e n -> p (e n)").bitcast(FP8X4),
-                scales=scales2[:, a:z].rearrange("p e n -> p (e n)"),
-                in_=rounded2[:, a:z].rearrange("p e n j -> p (e n j)"),
+        for b in reversed(range(late)):
+            round_w2(nc.vector.tensor_copy, rounded2[:, b], w2_raw[:, EARLY_W2 + b])
+        h_groups = []
+        for b in groups:
+            h_groups.append(small([P, GROUP, PACK], BF16, "last_h"))
+            multiply(h_groups[b][:], accs3[b], silus[b])
+        codes2, scales2 = quantize(
+            rounded2.rearrange("p e n j -> p (e n j)"),
+            small([P, late * N], U32, "last_h"),
+            small([P, late * N], U8, "scales2"),
+        )
+        last_hidden = [
+            quantize(
+                h_groups[b][:].rearrange("p n t -> p (n t)"),
+                hidden_tile(GROUP, U32, "h_codes"),
+                hidden_tile(GROUP, U8, "h_scales"),
             )
-        h_quantized = [quantize_group(h) for h in h_groups]
-        y_acc = psum_y.tile([P, len(waiting) * C], F32, name="acc")
-        for b, held in enumerate(waiting):
-            second_layer(y_acc[:, b * C : (b + 1) * C], (codes2[:, b], scales2[:, b]), held)
-        on_vector(y_slots[:, EARLY_W2 * C : LAST_ROUTED * C], y_acc[:])
-        for b in range(C // GROUP):
-            y_acc = psum_y.tile([P, GROUP], F32, name="acc")
-            second_layer(y_acc[:], (codes2[:, late - 1], scales2[:, late - 1]), h_quantized[b])
-            on_vector(y_slots[:, group_cols(LAST_ROUTED * C, b)], y_acc[:])
-
-
-        raw1, weights1 = load_and_quantize(w1[SHARED], ((on_scalar,), (on_scalar,)), False, load_pos)
-        accs = [
-            first_layer(weights1, token_words, token_scales, group_cols(0, b), psum_a1)
-            for b in range(T // GROUP)
+            for b in groups
         ]
-        raw3, weights3, last_rounded = load_and_quantize_finely(w3[SHARED], (on_scalar,), FINE_H, (on_vector, on_scalar), True)
+        y_acc = bank([P, C])
+        second_layer(y_acc[:], (codes2[:, :N], scales2[:, :N]), hidden)
+        nc.vector.tensor_copy(y_slots[:, EARLY_W2 * C : LAST * C], y_acc[:])
+        for b in groups:
+            y_acc = bank([P, GROUP])
+            second_layer(y_acc[:], (codes2[:, N:], scales2[:, N:]), last_hidden[b])
+            nc.vector.tensor_copy(y_slots[:, group_cols(LAST * C, b)], y_acc[:])
 
+        token_groups = range(T // GROUP)
+
+        def shared_products(weights):
+            accs = []
+            for b in token_groups:
+                accs.append(bank([P, PACK, GROUP]))
+                for o in range(PASSES):
+                    add_pass(accs[b], weights[o], token_words, token_scales, group_cols(0, b), o)
+            return accs
+
+        raw1 = raw_tile()
+        weights1 = []
+        for o, share in enumerate((SHARED_W1_SHARE, 0)):
+            load(raw1, w1[SHARED], o, False)
+            if o == 0:
+                nc.sync.dma_start(pos_sb[0][:], pos1)
+                nc.sync.dma_start(pos_sb[1][:], pos2)
+            rounded = round_pass(raw1[:, o], share)
+            weights1.append(quantize_weights(rounded[:], codes_tile([P, H], U32), scales_tile(H)))
+        accs1 = shared_products(weights1)
+
+        raw3 = raw_tile()
+        load(raw3, w3[SHARED], 0, False)
+        rounded_c = round_pass(raw3[:, 0], SHARED_W3_SHARE)
+        rounded_d = chained([P, PACK, P, PACK], BF16)
+        load(raw3, w3[SHARED], 1, False)
+        round_by_t(rounded_d, raw3[:, 1], slice(0, P))
+        weights3 = [
+            quantize_weights(rounded_c[:], chained([P, H], U32), scales_tile(H)),
+            quantize_halves(rounded_d),
+        ]
         nc.sync.dma_start(w2_raw[:, SHARED], w2_rows[:, SHARED])
-        silus = []
-        for b in range(T // GROUP):
-            if b % 2 == 0:
-                pair = rounded_pool.tile([P, 2, GROUP, PACK], F32, name="rounded", align_bytes=MX_ALIGN)
-            silus.append(silu_into(pair[:, b % 2], accs[b]))
-            if b == 2:
-                shared_rounded2 = w2_tile(rounded_pool, "rounded")
-                round_w2(shared_rounded2, w2_raw[:, SHARED], on_scalar)
 
-        accs3 = [
-            first_layer(weights3, token_words, token_scales, group_cols(0, b), psum_a3)
-            for b in range(T // GROUP)
-        ]
-
-        def spent_part(raw, o, index):
-            return raw[:, o, index // 2, index % 2 * C : (index % 2 + 1) * C]
-
-        pick_places = [None, None, spent_part(raw1, 0, 0), spent_part(raw1, 0, 1), spent_part(raw1, 1, 0), codes_pool.tile([P, C], F32, name="codes", align_bytes=MX_ALIGN)[:]]
-        sum_places = [last_rounded[:, 2].rearrange("p m j -> p (m j)").bitcast(F32), last_rounded[:, 3].rearrange("p m j -> p (m j)").bitcast(F32), last_rounded[:, 1].rearrange("p m j -> p (m j)").bitcast(F32)]
+        spent_w1 = [raw1[:, o].rearrange("p j i -> p (j i)") for o in range(PASSES)]
+        places = [small_pool.tile([P, C], F32, name="first_pick", bufs=1)[:]]
+        places.extend(spent_w1[0][:, index * C : (index + 1) * C] for index in range(3))
+        places.append(spent_w1[1][:, :C])
+        places.append(codes_tile([P, C], F32)[:])
         routed = []
         for c in range(T // C):
-            picks = []
             for r in range(2):
-                place = pick_places[2 * c + r]
-                if place is None:
-                    pick = small_pool.tile([P, C], F32, name=f"pick{r}", bufs=1)[:]
-                else:
-                    pick = place
-                looked_up = y_slots[:].indirect(pos_sb[r][:, c * LIST_COLS : (c + 1) * LIST_COLS])
-                gate_part = gate_sb[r][:, c * C : (c + 1) * C]
-                if 2 * c + r in ():
-                    nc.vector.tensor_copy(pick, looked_up)
-                    product = (last_rounded[:, 0].rearrange("p m j -> p (m j)").bitcast(F32) if r == 0 else spent_part(raw1, 1, 2 + r))
-                    nc.gpsimd.tensor_tensor(product, pick, gate_part, MULT)
-                    pick = product
-                else:
-                    nc.vector.tensor_tensor(pick, looked_up, gate_part, MULT)
-                picks.append(pick)
-            combined = sum_places[c]
-            nc.gpsimd.tensor_tensor(combined, picks[0], picks[1], ADD)
-            routed.append(combined)
+                nc.vector.tensor_tensor(
+                    places[2 * c + r],
+                    y_slots[:].indirect(pos_sb[r][:, c * LIST_COLS : (c + 1) * LIST_COLS]),
+                    gate_sb[r][:, c * C : (c + 1) * C],
+                    MULT,
+                )
+            routed.append(rounded_d[:, (2 + c) % PACK].rearrange("p m j -> p (m j)").bitcast(F32))
+            nc.gpsimd.tensor_tensor(routed[c], places[2 * c], places[2 * c + 1], ADD)
 
-        def tail_tile(shape, dtype):
-            return tail_pool.tile(shape, dtype, name="tail", align_bytes=DMA_ALIGN)
+        chunks = T // C
+        silus = []
+        for b in token_groups:
+            if b < chunks:
+                silus.append(silu_into(chained([P, GROUP, PACK], F32)[:], accs1[b]))
+            else:
+                silus.append(silu_into(spent_row(raw3, b - chunks), accs1[b]))
+            if b == chunks - 1:
+                rounded2 = codes_tile([P, N, PACK], BF16)
+                round_w2(nc.scalar.copy, rounded2[:], w2_raw[:, SHARED])
+        accs3 = shared_products(weights3)
 
-        h_tiles, quantized = {}, {}
+        h_chunks, y_accs = [], []
 
-        def multiply(b):
+        def down(c):
+            hidden_chunk = quantize(
+                h_chunks[c][:].rearrange("p n t -> p (n t)"),
+                tail_tile([P, C], U32),
+                hidden_tile(C, U8, "h_scales"),
+            )
+            y_accs.append(bank([P, C]))
+            second_layer(y_accs[c][:], weights2, hidden_chunk)
+
+        for b in token_groups:
             if b % 2 == 0:
-                h_tiles[b // 2] = tail_tile([P, C, PACK], BF16)
-            nc.vector.tensor_tensor(
-                h_tiles[b // 2][:, b % 2 * GROUP : (b % 2 + 1) * GROUP, :],
-                accs3[b][:].rearrange("p t n -> p n t"),
-                silus[b],
-                MULT,
-            )
-
-        shared_w2 = []
-
-        def quantize_shared_w2(c):
-            shared_w2.append(quantize_rounded_w2(shared_rounded2, tail_tile([P, N], U32)))
-
-        def quantize_h(c):
-            h_codes = tail_tile([P, C], U32)
-            h_scales = small_pool.tile([P, C], U8, name="h_scales", align_bytes=MX_ALIGN, bufs=4)
-            nc.vector.quantize_mx(
-                out=h_codes[:].bitcast(FP8X4),
-                scales=h_scales[:],
-                in_=h_tiles[c][:].rearrange("p n t -> p (n t)"),
-            )
-            y_acc = psum_y.tile([P, C], F32, name="acc")
-            second_layer(y_acc[:], shared_w2[0], (h_codes, h_scales))
-            quantized[c] = y_acc
-
-        def finish(c):
+                h_chunks.append(tail_tile([P, C, PACK], BF16))
+            multiply(h_chunks[b // 2][:, group_cols(0, b % 2)], accs3[b], silus[b])
+            if b == chunks:
+                weights2 = quantize(
+                    rounded2[:].rearrange("p n j -> p (n j)"),
+                    tail_tile([P, N], U32),
+                    small([P, N], U8, "scales2"),
+                )
+            if b > chunks:
+                down(b - chunks - 1)
+        down(chunks - 1)
+        for c in range(chunks):
             result = tail_tile([P, C], F32)
-            nc.vector.tensor_tensor(result[:], quantized[c][:], routed[c], ADD)
+            nc.vector.tensor_tensor(result[:], y_accs[c][:], routed[c], ADD)
             nc.sync.dma_start(out[:, c * C : (c + 1) * C], result[:])
-
-        multiply(0)
-        multiply(1)
-        multiply(2)
-        multiply(3)
-        quantize_shared_w2(0)
-        multiply(4)
-        quantize_h(0)
-        multiply(5)
-        quantize_h(1)
-        quantize_h(2)
-        finish(0)
-        finish(1)
-        finish(2)

@@ -32,7 +32,7 @@ DMA_ALIGN = 256
 WHOLE_LOADS = 4
 EARLY_W2 = E - 2
 ROUTED_SHARE = 56
-SHARED_W1_SHARE = 32
+SHARED_W1_SHARE = 16
 SHARED_W3_SHARE = 16
 
 
@@ -290,12 +290,11 @@ def tile_moe_shr_glu_silu_kernel(
             else:
                 rounded_d = chained([P, PACK, P, PACK], BF16)
                 accs3 = [bank([P, PACK, GROUP]) for b in groups]
-                for half in range(2):
-                    cols = slice(half * H // 2, (half + 1) * H // 2)
-                    nc.sync.dma_start(raw3[:, 1, :, cols], by_pass(w3[e])[:, 1, :, cols])
-                    round_by_t(rounded_d, raw3[:, 1], slice(half * P // 2, (half + 1) * P // 2))
-                    if half == 0:
-                        add_slot_pass(accs3, quantize_behind_rounding(rounded_c), e, 0)
+                add_slot_pass(
+                    accs3, quantize_weights(rounded_c[:], codes_tile([P, H], U32), scales_tile(H)), e, 0
+                )
+                load(raw3, w3[e], 1, whole)
+                round_by_t(rounded_d, raw3[:, 1], slice(0, P))
                 nc.sync.dma_start(w2_raw[:, EARLY_W2:E], w2_rows[:, EARLY_W2:E])
                 add_slot_pass(accs3, quantize_halves(rounded_d), e, 1)
             silus = [silu_into(spent_row(raw3, b), accs1[b]) for b in groups]

@@ -290,9 +290,8 @@ def tile_moe_shr_glu_silu_kernel(
             else:
                 rounded_d = chained([P, PACK, P, PACK], BF16)
                 accs3 = [bank([P, PACK, GROUP]) for b in groups]
-                add_slot_pass(
-                    accs3, quantize_weights(rounded_c[:], codes_tile([P, H], U32), scales_tile(H)), e, 0
-                )
+                weights_c = quantize_weights(rounded_c[:], codes_tile([P, H], U32), scales_tile(H))
+                add_slot_pass(accs3, weights_c, e, 0)
                 load(raw3, w3[e], 1, whole)
                 round_by_t(rounded_d, raw3[:, 1], slice(0, P))
                 nc.sync.dma_start(w2_raw[:, EARLY_W2:E], w2_rows[:, EARLY_W2:E])
@@ -303,8 +302,8 @@ def tile_moe_shr_glu_silu_kernel(
         rounded2 = (
             raw3[:, 1, PACK - 1].bitcast(BF16).rearrange("p (e n j) -> p e n j", e=late, j=PACK)
         )
-        for b in reversed(range(late)):
-            round_w2(nc.vector.tensor_copy, rounded2[:, b], w2_raw[:, EARLY_W2 + b])
+        for expert in reversed(range(EARLY_W2, E)):
+            round_w2(nc.vector.tensor_copy, rounded2[:, expert - EARLY_W2], w2_raw[:, expert])
         h_groups = []
         for b in groups:
             h_groups.append(small([P, GROUP, PACK], BF16, "last_h"))
@@ -403,18 +402,19 @@ def tile_moe_shr_glu_silu_kernel(
             y_accs.append(bank([P, C]))
             second_layer(y_accs[c][:], weights2, hidden_chunk)
 
+        last_but_one = T // GROUP - 2
         for b in token_groups:
             if b % 2 == 0:
                 h_chunks.append(tail_tile([P, C, PACK], BF16))
             multiply(h_chunks[b // 2][:, group_cols(0, b % 2)], accs3[b], silus[b])
-            if b == chunks:
+            if b == last_but_one:
                 weights2 = quantize(
                     rounded2[:].rearrange("p n j -> p (n j)"),
                     tail_tile([P, N], U32),
                     small([P, N], U8, "scales2"),
                 )
-            if b > chunks:
-                down(b - chunks - 1)
+            if b >= last_but_one:
+                down(b - last_but_one)
         down(chunks - 1)
         for c in range(chunks):
             result = tail_tile([P, C], F32)

@@ -29,11 +29,11 @@ LAST = E - 1
 MX_ALIGN = 64
 DMA_ALIGN = 256
 
-WHOLE_LOADS = 4
-EARLY_W2 = E - 2
-ROUTED_SHARE = 56
-SHARED_W1_SHARE = 16
-SHARED_W3_SHARE = 16
+EARLY_W2 = 2
+SCALAR_ALONE = 2
+EAGER = 3
+NEXT_SHARE = 24
+LAST_SHARE = 40
 
 
 def tile_moe_shr_glu_silu_kernel(
@@ -43,30 +43,16 @@ def tile_moe_shr_glu_silu_kernel(
 
     with ExitStack() as ctx:
         keep = ctx.enter_context(tc.tile_pool(name="keep", bufs=1))
-        raw_pool = ctx.enter_context(tc.tile_pool(name="raw", bufs=6))
-        chain_pool = ctx.enter_context(tc.tile_pool(name="chain", bufs=10))
-        codes_pool = ctx.enter_context(tc.tile_pool(name="codes", bufs=9))
-        small_pool = ctx.enter_context(tc.tile_pool(name="small", bufs=T // C))
-        tail_pool = ctx.enter_context(tc.tile_pool(name="tail", bufs=7))
+        raw_pool = ctx.enter_context(tc.tile_pool(name="raw", bufs=5))
+        chain_pool = ctx.enter_context(tc.tile_pool(name="chain", bufs=40))
+        codes_pool = ctx.enter_context(tc.tile_pool(name="codes", bufs=14))
         psum = ctx.enter_context(tc.psum_pool(name="psum", bufs=8))
 
         def chained(shape, dtype):
-            return chain_pool.tile(shape, dtype, name="chained", align_bytes=MX_ALIGN)
+            return chain_pool.tile(shape, dtype, name="chained", align_bytes=DMA_ALIGN)
 
-        def codes_tile(shape, dtype):
-            return codes_pool.tile(shape, dtype, name="codes", align_bytes=MX_ALIGN)
-
-        def scales_tile(width):
-            return codes_pool.tile([P, width], U8, name="scales", align_bytes=MX_ALIGN)
-
-        def small(shape, dtype, name):
-            return small_pool.tile(shape, dtype, name=name, align_bytes=MX_ALIGN)
-
-        def hidden_tile(width, dtype, name):
-            return small_pool.tile([P, width], dtype, name=name, align_bytes=MX_ALIGN, bufs=4)
-
-        def tail_tile(shape, dtype):
-            return tail_pool.tile(shape, dtype, name="tail", align_bytes=DMA_ALIGN)
+        def codes_tile(width):
+            return codes_pool.tile([P, width], U32, name="codes", align_bytes=MX_ALIGN)
 
         def bank(shape):
             return psum.tile(shape, F32, name="bank")
@@ -80,24 +66,21 @@ def tile_moe_shr_glu_silu_kernel(
         def group_cols(first, b):
             return slice(first + b * GROUP, first + (b + 1) * GROUP)
 
-        def walks(rounded, rows):
-            return (
-                rounded[:].rearrange("p t m j -> p m j t"),
-                rows.rearrange("p j (m t) -> p m j t", t=PACK),
-            )
+        def round_half(copy, rounded, rows, half, m_range):
+            dst = rounded[:].rearrange("p t m j -> p m j t")
+            src = rows.rearrange("p j (m t) -> p m j t", t=PACK)
+            copy(dst[:, m_range], src[:, m_range, :, 2 * half : 2 * half + 2])
 
-        def round_pass(rows, vector_share):
-            rounded = chained([P, PACK, P, PACK], BF16)
-            dst, src = walks(rounded, rows)
-            if vector_share:
-                nc.vector.tensor_copy(dst[:, :vector_share], src[:, :vector_share])
-            nc.scalar.copy(dst[:, vector_share:], src[:, vector_share:])
+        def rounded_half(copy, rows, half):
+            rounded = chained([P, 2, P, PACK], BF16)
+            round_half(copy, rounded, rows, half, slice(0, P))
             return rounded
 
-        def round_by_t(rounded, rows, m_range):
-            dst, src = walks(rounded, rows)
-            nc.vector.tensor_copy(dst[:, m_range, :, :2], src[:, m_range, :, :2])
-            nc.scalar.copy(dst[:, m_range, :, 2:], src[:, m_range, :, 2:])
+        def shared_half(rows, vector_share):
+            rounded = chained([P, 2, P, PACK], BF16)
+            round_half(nc.scalar.copy, rounded, rows, 1, slice(vector_share, P))
+            round_half(nc.vector.tensor_copy, rounded, rows, 1, slice(0, vector_share))
+            return rounded
 
         def round_w2(copy, rounded, rows):
             copy(
@@ -105,42 +88,40 @@ def tile_moe_shr_glu_silu_kernel(
                 rows.rearrange("p j (c u) -> p c j u", u=LINE),
             )
 
-        def quantize(values, codes, scales):
+        def rounded_w2(copy, rows):
+            rounded = chained([P, N, PACK], BF16)
+            round_w2(copy, rounded[:], rows)
+            return rounded
+
+        def quantize(values, codes):
+            scales = chained([P, codes.shape[1]], U8)
             nc.vector.quantize_mx(out=codes[:].bitcast(FP8X4), scales=scales[:], in_=values)
             return codes[:], scales[:]
 
-        def quantize_weights(rounded, codes, scales):
-            quantize(rounded.rearrange("p t m j -> p (t m j)"), codes, scales)
-            return [
-                (codes[:, t * P : (t + 1) * P], scales[:, t * P : (t + 1) * P])
-                for t in range(rounded.shape[1])
-            ]
+        def quantize_half(rounded):
+            codes, scales = quantize(rounded[:].rearrange("p t m j -> p (t m j)"), codes_tile(2 * P))
+            return [(codes[:, t * P : (t + 1) * P], scales[:, t * P : (t + 1) * P]) for t in range(2)]
 
-        def quantize_behind_rounding(rounded):
-            return quantize_weights(rounded[:], codes_tile([P, H], U32), chained([P, H], U8))
+        def quantize_columns(values, name):
+            codes = keep.tile([P, values.shape[1]], U32, name=name, align_bytes=MX_ALIGN)
+            return quantize(values.rearrange("p n t -> p (n t)"), codes)
 
-        def quantize_halves(rounded):
-            return [
-                operand
-                for half in range(2)
-                for operand in quantize_weights(
-                    rounded[:, 2 * half : 2 * half + 2],
-                    codes_tile([P, H // 2], U32),
-                    scales_tile(H // 2),
-                )
-            ]
-
-        def add_pass(acc, weights, words, scales, cols, o):
-            for t in range(PACK):
-                nc.tensor.matmul_mx(
-                    out=acc[:, t, :],
-                    lhsT=weights[t][0].bitcast(FP8X4),
-                    lhsT_scale=weights[t][1],
-                    rhs=words[o][:, cols].bitcast(FP8X4),
-                    rhs_scale=scales[4 * o : P, cols],
-                    start=(o == 0 and t == 0),
-                    stop=(o == PASSES - 1 and t == PACK - 1),
-                )
+        def add_half(accs, rounded, tokens, o, half):
+            weights = quantize_half(rounded)
+            words, scales, first = tokens
+            for b, acc in enumerate(accs):
+                cols = group_cols(first, b)
+                for u in range(2):
+                    t = 2 * half + u
+                    nc.tensor.matmul_mx(
+                        out=acc[:, t, :],
+                        lhsT=weights[u][0].bitcast(FP8X4),
+                        lhsT_scale=weights[u][1],
+                        rhs=words[o][:, cols].bitcast(FP8X4),
+                        rhs_scale=scales[4 * o : P, cols],
+                        start=(o == 0 and t == 0),
+                        stop=(o == PASSES - 1 and t == PACK - 1),
+                    )
 
         def second_layer(y_acc, weights2, hidden):
             nc.tensor.matmul_mx(
@@ -153,15 +134,24 @@ def tile_moe_shr_glu_silu_kernel(
                 stop=True,
             )
 
-        def silu_into(dst, acc):
-            nc.scalar.activation(dst, acc[:].rearrange("p t n -> p n t"), SILU)
-            return dst
+        def silu_of(acc):
+            silu = chained([P, GROUP, PACK], F32)
+            nc.scalar.activation(silu[:], acc[:].rearrange("p t n -> p n t"), SILU)
+            return silu
 
         def multiply(h, acc, silu):
-            nc.vector.tensor_tensor(h, acc[:].rearrange("p t n -> p n t"), silu, MULT)
+            nc.vector.tensor_tensor(h, acc[:].rearrange("p t n -> p n t"), silu[:], MULT)
 
-        def spent_row(raw, row):
-            return raw[:, 1, row, :].rearrange("p (n t) -> p n t", t=PACK)
+        def multiply_pair(accs, silus):
+            h = chained([P, C, PACK], BF16)
+            for b in range(2):
+                multiply(h[:, group_cols(0, b)], accs[b], silus[b])
+            return h
+
+        def banks(count):
+            return [bank([P, PACK, GROUP]) for b in range(count)]
+
+        vector_copy, scalar_copy = nc.vector.tensor_copy, nc.scalar.copy
 
         token_scales = keep.tile([P, T], U8, name="token_scales", align_bytes=DMA_ALIGN)
         nc.vector.memset(token_scales[:].bitcast(I32), 0)
@@ -176,13 +166,34 @@ def tile_moe_shr_glu_silu_kernel(
 
         identity = keep.tile([P, P], F32, name="identity", align_bytes=MX_ALIGN)
         make_identity(nc, identity[:])
-        gate_sb = [keep.tile([P, T], F32, name=f"gate_sb{r}") for r in range(2)]
-        for first, per in ((0, PACK), (P * PACK, 2)):
-            tokens = slice(first, first + P * per)
-            column = keep.tile([P, 2, 8], F32, name=f"gate_column{per}")
+        pieces = ((0, PACK), (P * PACK, 2))
+        columns = []
+        for first, per in pieces:
+            columns.append(keep.tile([P, 2, 8], F32, name=f"gate_column{per}"))
             nc.scalar.dma_start(
-                column[:, :, :per], gate[:, 0, tokens].rearrange("r (p c) -> p r c", c=per)
+                columns[-1][:, :, :per],
+                gate[:, 0, first : first + P * per].rearrange("r (p c) -> p r c", c=per),
             )
+
+        raw1 = raw_tile()
+        nc.sync.dma_start(raw1[:, 0], by_pass(w1[SHARED])[:, 0])
+        for q in range(4):
+            nc.sync.dma_start(
+                token_scales[32 * q : 32 * q + 4 * PASSES, :].bitcast(I32),
+                x_scales[:, 4 * q : 4 * q + 4, :].bitcast(I32),
+            )
+        nc.sync.dma_start(raw1[:, 1], by_pass(w1[SHARED])[:, 1])
+        raw3 = raw_tile()
+        for o in range(PASSES):
+            nc.sync.dma_start(raw3[:, o], by_pass(w3[SHARED])[:, o])
+        pos_sb = [
+            keep.tile([P, T // 16], U16, name=f"pos_sb{r}", align_bytes=DMA_ALIGN) for r in range(2)
+        ]
+        nc.sync.dma_start(pos_sb[0][:], pos1)
+        nc.sync.dma_start(pos_sb[1][:], pos2)
+
+        gate_sb = [keep.tile([P, T], F32, name=f"gate_sb{r}") for r in range(2)]
+        for (first, per), column in zip(pieces, columns):
             for r in range(2):
                 spread = bank([P, PACK, GROUP])
                 for c in range(per):
@@ -190,233 +201,201 @@ def tile_moe_shr_glu_silu_kernel(
                         spread[:, c, :], column[:, r, c : c + 1].to_broadcast([P, P]), identity[:]
                     )
                 nc.scalar.copy(
-                    gate_sb[r][:, tokens].rearrange("p (n c) -> p n c", c=per),
+                    gate_sb[r][:, first : first + P * per].rearrange("p (n c) -> p n c", c=per),
                     spread[:, :per, :].rearrange("p c n -> p n c"),
                 )
 
-        y_slots = keep.tile([P, E * C], F32, name="y_slots")
-        w2_raw = keep.tile([P, E + 1, PACK, N], F32, name="w2_raw", align_bytes=DMA_ALIGN)
-        w2_rows = w2.rearrange("e (p j) n -> p e j n", j=PACK)
-        pos_sb = [
-            keep.tile([P, T // 16], U16, name=f"pos_sb{r}", align_bytes=DMA_ALIGN) for r in range(2)
-        ]
-
-        first_raw = raw_tile()
-        nc.sync.dma_start(first_raw[:], by_pass(w1[0]))
-        for q in range(4):
-            nc.sync.dma_start(
-                token_scales[32 * q : 32 * q + 4 * PASSES, :].bitcast(I32),
-                x_scales[:, 4 * q : 4 * q + 4, :].bitcast(I32),
-            )
-
-        gathered = []
-        for g in range(E * C // GATHER):
+        def gather(g, source, dtype):
             piece = offs_sb[:, g * GATHER // 16 : (g + 1) * GATHER // 16]
-            slot_words = []
-            for o in range(PASSES):
-                words = keep.tile([P, GATHER], U32, name=f"slot_words{g}_{o}", align_bytes=MX_ALIGN)
-                nc.vector.tensor_copy(words[:], token_words[o].indirect(piece))
-                slot_words.append(words)
-            slot_scales = keep.tile([P, GATHER], U8, name=f"slot_scales{g}", align_bytes=MX_ALIGN)
-            nc.vector.tensor_copy(slot_scales[:], token_scales[:].indirect(piece))
-            gathered.append((slot_words, slot_scales))
+            picked = chained([P, GATHER], dtype)
+            nc.vector.tensor_copy(picked[:], source.indirect(piece))
+            return picked
 
-        groups = range(C // GROUP)
+        sources = [(token_words[0], U32), (token_words[1], U32), (token_scales[:], U8)]
+        gathered = []
 
-        def add_slot_pass(accs, weights, e, o):
-            slot_words, slot_scales = gathered[e * C // GATHER]
-            for b in groups:
-                add_pass(accs[b], weights, slot_words, slot_scales, group_cols(e * C % GATHER, b), o)
+        def gather_next():
+            count = len(gathered)
+            gathered.append(gather(count // 3, *sources[count % 3]))
 
-        def load(raw, matrix, o, whole):
-            if not whole:
-                nc.sync.dma_start(raw[:, o], by_pass(matrix)[:, o])
-            elif o == 0:
-                nc.sync.dma_start(raw[:], by_pass(matrix))
+        def slots_of(e):
+            g = e * C // GATHER
+            return gathered[3 * g : 3 * g + 2], gathered[3 * g + 2], e * C % GATHER
+
+        y_slots = keep.tile([P, E * C], F32, name="y_slots")
+        w2_rows = w2.rearrange("e (p j) n -> p e j n", j=PACK)
+
+        all_tokens = (token_words, token_scales, 0)
+        token_groups = T // GROUP
+        accs1 = banks(token_groups)
+        for index in range(3):
+            gather_next()
+        for o in range(PASSES):
+            for half in range(2):
+                rounded = rounded_half(scalar_copy, raw1[:, o], half)
+                gather_next()
+                add_half(accs1, rounded, all_tokens, o, half)
+        rounded_c = [rounded_half(scalar_copy, raw3[:, 0], half) for half in range(2)]
+        for index in range(2):
+            gather_next()
+        rounded_d = [rounded_half(vector_copy, raw3[:, 1], half) for half in range(2)]
+        silus = [silu_of(acc) for acc in accs1]
+        accs3 = banks(token_groups)
+        for o, rounded in enumerate((rounded_c, rounded_d)):
+            for half in range(2):
+                add_half(accs3, rounded[half], all_tokens, o, half)
+        pending = None
+        waiting = [(accs3[2 * c : 2 * c + 2], silus[2 * c : 2 * c + 2]) for c in range(T // C)]
+        hidden = []
+
+        def quantize_hidden(products):
+            for h in products:
+                hidden.append(quantize_columns(h[:], f"h_codes{len(hidden)}"))
 
         for e in range(E):
-            share = ROUTED_SHARE if e > 0 else 0
-            whole = e < WHOLE_LOADS
+            slots = slots_of(e)
+            eager = e >= EAGER
+            raw1, raw3 = raw_tile(), raw_tile()
+            for raw, matrix in ((raw1, w1[e]), (raw3, w3[e])):
+                if 0 < e < EAGER:
+                    nc.sync.dma_start(raw[:], by_pass(matrix))
+                else:
+                    for o in range(PASSES):
+                        nc.sync.dma_start(raw[:, o], by_pass(matrix)[:, o])
             if e == 0:
-                raw1 = first_raw
-            else:
-                raw1 = raw_tile()
-                load(raw1, w1[e], 0, whole)
-            rounded_a = round_pass(raw1[:, 0], share)
-            if e > 0:
-                add_slot_pass(accs3, quantize_behind_rounding(rounded_d), e - 1, 1)
-
-            load(raw1, w1[e], 1, whole)
-            rounded_b = round_pass(raw1[:, 1], share)
-            if e > 0:
-                h = chained([P, C, PACK], BF16)
-                for b in groups:
-                    multiply(h[:, group_cols(0, b)], accs3[b], silus[b])
-            accs1 = [bank([P, PACK, GROUP]) for b in groups]
-            add_slot_pass(accs1, quantize_behind_rounding(rounded_a), e, 0)
-
-            raw3 = raw_tile()
-            load(raw3, w3[e], 0, whole)
-            rounded_c = round_pass(raw3[:, 0], share)
-            if e == 0:
-                nc.sync.dma_start(w2_raw[:, :EARLY_W2], w2_rows[:, :EARLY_W2])
-            else:
-                hidden = quantize(
-                    h[:].rearrange("p n t -> p (n t)"),
-                    hidden_tile(C, U32, "h_codes"),
-                    chained([P, C], U8),
-                )
-                if e - 1 < EARLY_W2:
+                early_w2 = keep.tile([P, EARLY_W2, PACK, N], F32, name="early_w2", align_bytes=DMA_ALIGN)
+                nc.sync.dma_start(early_w2[:], w2_rows[:, :EARLY_W2])
+            early = 0 < e <= EARLY_W2
+            multiply_step = 0 if (e == 0 or e > EAGER) else 1
+            for step in range(2 * PASSES):
+                rows = (raw1, raw3)[step // PASSES][:, step % PASSES]
+                o = step % PASSES
+                if e == LAST and step == 3:
+                    break
+                alone = 4 * e + step < SCALAR_ALONE
+                first = rounded_half(scalar_copy if alone else vector_copy, rows, 0)
+                if e == LAST and step == 2:
+                    second = shared_half(rows, NEXT_SHARE)
+                else:
+                    second = rounded_half(scalar_copy, rows, 1)
+                if step == 0 and early:
+                    rounded2 = rounded_w2(scalar_copy, early_w2[:, e - 1])
+                if step == multiply_step:
+                    products = [multiply_pair(*pair) for pair in waiting]
+                if step == multiply_step + 1:
+                    quantize_hidden(products)
+                if step == 2 and early:
                     y_acc = bank([P, C])
-                    second_layer(y_acc[:], weights2, hidden)
-            add_slot_pass(accs1, quantize_behind_rounding(rounded_b), e, 1)
+                    second_layer(y_acc[:], quantize_columns(rounded2[:], f"codes2_{e}"), hidden[e + 2])
+                if pending:
+                    add_half(*pending)
+                if o == 0:
+                    accs = banks(2)
+                    if step == 0:
+                        accs1 = accs
+                    else:
+                        accs3 = accs
+                add_half(accs, first, slots, o, 0)
+                pending = (accs, second, slots, o, 1)
+                if eager:
+                    add_half(*pending)
+                    pending = None
+                if step == (2 if e == LAST else 3):
+                    silus = [silu_of(acc) for acc in accs1]
+                if step == 3 and early:
+                    nc.scalar.copy(y_slots[:, (e - 1) * C : e * C], y_acc[:])
+            waiting = [(accs3, silus)]
 
-            if e < LAST:
-                load(raw3, w3[e], 1, whole)
-                rounded_d = round_pass(raw3[:, 1], share)
-                if e > 0:
-                    nc.vector.tensor_copy(y_slots[:, (e - 1) * C : e * C], y_acc[:])
-                if e < EARLY_W2:
-                    rounded2 = chained([P, N, PACK], BF16)
-                    round_w2(nc.vector.tensor_copy, rounded2[:], w2_raw[:, e])
-                accs3 = [bank([P, PACK, GROUP]) for b in groups]
-                add_slot_pass(accs3, quantize_behind_rounding(rounded_c), e, 0)
-                if e < EARLY_W2:
-                    weights2 = quantize(
-                        rounded2[:].rearrange("p n j -> p (n j)"),
-                        small([P, N], U32, "codes2"),
-                        small([P, N], U8, "scales2"),
-                    )
-            else:
-                rounded_d = chained([P, PACK, P, PACK], BF16)
-                accs3 = [bank([P, PACK, GROUP]) for b in groups]
-                weights_c = quantize_weights(rounded_c[:], codes_tile([P, H], U32), scales_tile(H))
-                add_slot_pass(accs3, weights_c, e, 0)
-                load(raw3, w3[e], 1, whole)
-                round_by_t(rounded_d, raw3[:, 1], slice(0, P))
-                nc.sync.dma_start(w2_raw[:, EARLY_W2:E], w2_rows[:, EARLY_W2:E])
-                add_slot_pass(accs3, quantize_halves(rounded_d), e, 1)
-            silus = [silu_into(spent_row(raw3, b), accs1[b]) for b in groups]
+        late = list(range(EARLY_W2, E + 1))
+        late_raw = raw_tile()[:].rearrange("p o j i -> p (o j i)")
+        late_rows = {}
+        for index, expert in enumerate(late):
+            rows = late_raw[:, index * PACK * N : (index + 1) * PACK * N]
+            late_rows[expert] = rows.rearrange("p (j n) -> p j n", j=PACK)
+            nc.sync.dma_start(late_rows[expert], w2_rows[:, expert])
+        first = rounded_half(vector_copy, raw3[:, 1], 0)
+        second = shared_half(raw3[:, 1], LAST_SHARE)
+        add_half(accs3, first, slots, 1, 0)
+        add_half(accs3, second, slots, 1, 1)
 
-        late = E - EARLY_W2
-        rounded2 = (
-            raw3[:, 1, PACK - 1].bitcast(BF16).rearrange("p (e n j) -> p e n j", e=late, j=PACK)
-        )
-        for expert in reversed(range(EARLY_W2, E)):
-            round_w2(nc.vector.tensor_copy, rounded2[:, expert - EARLY_W2], w2_raw[:, expert])
+        def quantize_pair(rounded, name):
+            codes, scales = quantize_columns(rounded[:].rearrange("p e n j -> p (e n) j"), name)
+            return [(codes[:, u * N : (u + 1) * N], scales[:, u * N : (u + 1) * N]) for u in range(2)]
+
+        pair_a = chained([P, 2, N, PACK], BF16)
+        round_w2(scalar_copy, pair_a[:, 0], late_rows[LAST - 3])
+        round_w2(vector_copy, pair_a[:, 1], late_rows[LAST - 2])
+        pair_b = chained([P, 2, N, PACK], BF16)
+        round_w2(scalar_copy, pair_b[:, 0], late_rows[LAST - 1])
+        round_w2(scalar_copy, pair_b[:, 1], late_rows[LAST])
+        weights_a = quantize_pair(pair_a, "codes2_a")
+        y_a = bank([P, 2, C])
+        for u in range(2):
+            second_layer(y_a[:, u], weights_a[u], hidden[LAST + u])
         h_groups = []
-        for b in groups:
-            h_groups.append(small([P, GROUP, PACK], BF16, "last_h"))
+        for b in range(2):
+            h_groups.append(chained([P, GROUP, PACK], BF16))
             multiply(h_groups[b][:], accs3[b], silus[b])
-        codes2, scales2 = quantize(
-            rounded2.rearrange("p e n j -> p (e n j)"),
-            small([P, late * N], U32, "last_h"),
-            small([P, late * N], U8, "scales2"),
-        )
-        last_hidden = [
-            quantize(
-                h_groups[b][:].rearrange("p n t -> p (n t)"),
-                hidden_tile(GROUP, U32, "h_codes"),
-                hidden_tile(GROUP, U8, "h_scales"),
-            )
-            for b in groups
-        ]
-        y_acc = bank([P, C])
-        second_layer(y_acc[:], (codes2[:, :N], scales2[:, :N]), hidden)
-        nc.vector.tensor_copy(y_slots[:, EARLY_W2 * C : LAST * C], y_acc[:])
-        for b in groups:
-            y_acc = bank([P, GROUP])
-            second_layer(y_acc[:], (codes2[:, N:], scales2[:, N:]), last_hidden[b])
-            nc.vector.tensor_copy(y_slots[:, group_cols(LAST * C, b)], y_acc[:])
-
-        token_groups = range(T // GROUP)
-
-        def shared_products(weights):
-            accs = []
-            for b in token_groups:
-                accs.append(bank([P, PACK, GROUP]))
-                for o in range(PASSES):
-                    add_pass(accs[b], weights[o], token_words, token_scales, group_cols(0, b), o)
-            return accs
-
-        raw1 = raw_tile()
-        weights1 = []
-        for o, share in enumerate((SHARED_W1_SHARE, 0)):
-            load(raw1, w1[SHARED], o, False)
-            if o == 0:
-                nc.sync.dma_start(pos_sb[0][:], pos1)
-                nc.sync.dma_start(pos_sb[1][:], pos2)
-            rounded = round_pass(raw1[:, o], share)
-            weights1.append(quantize_weights(rounded[:], codes_tile([P, H], U32), scales_tile(H)))
-        accs1 = shared_products(weights1)
-
-        raw3 = raw_tile()
-        load(raw3, w3[SHARED], 0, False)
-        rounded_c = round_pass(raw3[:, 0], SHARED_W3_SHARE)
-        rounded_d = chained([P, PACK, P, PACK], BF16)
-        load(raw3, w3[SHARED], 1, False)
-        round_by_t(rounded_d, raw3[:, 1], slice(0, P))
-        weights3 = [
-            quantize_weights(rounded_c[:], chained([P, H], U32), scales_tile(H)),
-            quantize_halves(rounded_d),
-        ]
-        nc.sync.dma_start(w2_raw[:, SHARED], w2_rows[:, SHARED])
-
-        spent_w1 = [raw1[:, o].rearrange("p j i -> p (j i)") for o in range(PASSES)]
-        places = [small_pool.tile([P, C], F32, name="first_pick", bufs=1)[:]]
-        places.extend(spent_w1[0][:, index * C : (index + 1) * C] for index in range(3))
-        places.append(spent_w1[1][:, :C])
-        places.append(codes_tile([P, C], F32)[:])
-        routed = []
+        nc.scalar.copy(y_slots[:, (LAST - 3) * C : (LAST - 1) * C], y_a[:].rearrange("p e n -> p (e n)"))
+        weights_b = quantize_pair(pair_b, "codes2_b")
+        y_b = bank([P, C])
+        second_layer(y_b[:], weights_b[0], hidden[LAST + 2])
+        rounded_shared = rounded_w2(scalar_copy, late_rows[SHARED])
+        y_last = []
+        for b in range(2):
+            last_hidden = quantize_columns(h_groups[b][:], f"last_h{b}")
+            y_last.append(bank([P, GROUP]))
+            second_layer(y_last[b][:], weights_b[1], last_hidden)
+        nc.scalar.copy(y_slots[:, (LAST - 1) * C : LAST * C], y_b[:])
+        for b in range(2):
+            nc.vector.tensor_copy(y_slots[:, group_cols(LAST * C, b)], y_last[b][:])
+        weights_shared = quantize_columns(rounded_shared[:], "codes2_shared")
+        shared_turned = []
         for c in range(T // C):
-            for r in range(2):
-                nc.vector.tensor_tensor(
-                    places[2 * c + r],
-                    y_slots[:].indirect(pos_sb[r][:, c * LIST_COLS : (c + 1) * LIST_COLS]),
-                    gate_sb[r][:, c * C : (c + 1) * C],
-                    MULT,
-                )
-            routed.append(rounded_d[:, (2 + c) % PACK].rearrange("p m j -> p (m j)").bitcast(F32))
-            nc.gpsimd.tensor_tensor(routed[c], places[2 * c], places[2 * c + 1], ADD)
+            acc = bank([P, 2, N])
+            for b in range(2):
+                tokens = [plane[:, group_cols(0, b)] for plane in hidden[c]]
+                second_layer(acc[:, b], tokens, weights_shared)
+            shared_turned.append(chained([P, 2, N], F32))
+            nc.scalar.copy(shared_turned[c][:], acc[:])
+
+        def pick(r, c):
+            picked = chained([P, C], F32)
+            nc.vector.tensor_tensor(
+                picked[:],
+                y_slots[:].indirect(pos_sb[r][:, c * LIST_COLS : (c + 1) * LIST_COLS]),
+                gate_sb[r][:, c * C : (c + 1) * C],
+                MULT,
+            )
+            return picked
+
+        def add(a, b):
+            total = chained([P, C], F32)
+            nc.vector.tensor_tensor(total[:], a[:], b[:], ADD)
+            return total
+
+        def turn(acc, block, start, stop):
+            nc.tensor.matmul(acc, block, identity[:], start=start, stop=stop, is_transpose=True)
 
         chunks = T // C
-        silus = []
-        for b in token_groups:
-            if b < chunks:
-                silus.append(silu_into(chained([P, GROUP, PACK], F32)[:], accs1[b]))
-            else:
-                silus.append(silu_into(spent_row(raw3, b - chunks), accs1[b]))
-            if b == chunks - 1:
-                rounded2 = codes_tile([P, N, PACK], BF16)
-                round_w2(nc.scalar.copy, rounded2[:], w2_raw[:, SHARED])
-        accs3 = shared_products(weights3)
-
-        h_chunks, y_accs = [], []
-
-        def down(c):
-            hidden_chunk = quantize(
-                h_chunks[c][:].rearrange("p n t -> p (n t)"),
-                tail_tile([P, C], U32),
-                hidden_tile(C, U8, "h_scales"),
-            )
-            y_accs.append(bank([P, C]))
-            second_layer(y_accs[c][:], weights2, hidden_chunk)
-
-        last_but_one = T // GROUP - 2
-        for b in token_groups:
-            if b % 2 == 0:
-                h_chunks.append(tail_tile([P, C, PACK], BF16))
-            multiply(h_chunks[b // 2][:, group_cols(0, b % 2)], accs3[b], silus[b])
-            if b == last_but_one:
-                weights2 = quantize(
-                    rounded2[:].rearrange("p n j -> p (n j)"),
-                    tail_tile([P, N], U32),
-                    small([P, N], U8, "scales2"),
-                )
-            if b >= last_but_one:
-                down(b - last_but_one)
-        down(chunks - 1)
-        for c in range(chunks):
-            result = tail_tile([P, C], F32)
-            nc.vector.tensor_tensor(result[:], y_accs[c][:], routed[c], ADD)
+        first_turned, partials = [], []
+        for c in range(chunks + 1):
+            if c < chunks:
+                first_pick = pick(0, c)
+                acc = bank([P, 2, N])
+                for b in range(2):
+                    turn(acc[:, b], first_pick[:, group_cols(0, b)], True, True)
+                first_turned.append(chained([P, 2, N], F32))
+                nc.scalar.copy(first_turned[c][:], acc[:])
+            if c > 0:
+                partials.append(bank([P, C]))
+                for b in range(2):
+                    block = partials[c - 1][:, group_cols(0, b)]
+                    turn(block, shared_turned[c - 1][:, b], True, False)
+                    turn(block, first_turned[c - 1][:, b], False, True)
+        second_picks = [pick(1, c) for c in range(2)]
+        for c in range(T // C):
+            result = add(partials[c], second_picks[c])
             nc.sync.dma_start(out[:, c * C : (c + 1) * C], result[:])
+            if c == 0:
+                second_picks.append(pick(1, 2))

@@ -15,6 +15,7 @@ U8 = mybir.dt.uint8
 FP8X4 = mybir.dt.float8_e4m3fn_x4
 MULT = mybir.AluOpType.mult
 ADD = mybir.AluOpType.add
+COPY = mybir.ActivationFunctionType.Copy
 SILU = mybir.ActivationFunctionType.Silu
 
 P = 128
@@ -106,22 +107,26 @@ def tile_moe_shr_glu_silu_kernel(
             codes = keep.tile([P, values.shape[1]], U32, name=name, align_bytes=MX_ALIGN)
             return quantize(values.rearrange("p n t -> p (n t)"), codes)
 
+        def product(acc, weights, tokens, b, o, t, start, stop):
+            words, scales, first = tokens
+            cols = group_cols(first, b)
+            nc.tensor.matmul_mx(
+                out=acc[:, t, :],
+                lhsT=weights[0].bitcast(FP8X4),
+                lhsT_scale=weights[1],
+                rhs=words[o][:, cols].bitcast(FP8X4),
+                rhs_scale=scales[4 * o : P, cols],
+                start=start,
+                stop=stop,
+            )
+
         def add_half(accs, rounded, tokens, o, half):
             weights = quantize_half(rounded)
-            words, scales, first = tokens
             for b, acc in enumerate(accs):
-                cols = group_cols(first, b)
                 for u in range(2):
                     t = 2 * half + u
-                    nc.tensor.matmul_mx(
-                        out=acc[:, t, :],
-                        lhsT=weights[u][0].bitcast(FP8X4),
-                        lhsT_scale=weights[u][1],
-                        rhs=words[o][:, cols].bitcast(FP8X4),
-                        rhs_scale=scales[4 * o : P, cols],
-                        start=(o == 0 and t == 0),
-                        stop=(o == PASSES - 1 and t == PACK - 1),
-                    )
+                    last = o == PASSES - 1 and t == PACK - 1
+                    product(acc, weights[u], tokens, b, o, t, o == 0 and t == 0, last)
 
         def second_layer(y_acc, weights2, hidden):
             nc.tensor.matmul_mx(
@@ -166,14 +171,12 @@ def tile_moe_shr_glu_silu_kernel(
 
         identity = keep.tile([P, P], F32, name="identity", align_bytes=MX_ALIGN)
         make_identity(nc, identity[:])
-        pieces = ((0, PACK), (P * PACK, 2))
-        columns = []
-        for first, per in pieces:
-            columns.append(keep.tile([P, 2, 8], F32, name=f"gate_column{per}"))
-            nc.scalar.dma_start(
-                columns[-1][:, :, :per],
-                gate[:, 0, first : first + P * per].rearrange("r (p c) -> p r c", c=per),
-            )
+        token_groups = T // GROUP
+        gate_rows = keep.tile([P, 2, GROUP], F32, name="gate_rows", align_bytes=DMA_ALIGN)
+        nc.gpsimd.memset(gate_rows[:], 0.0)
+        nc.scalar.dma_start(
+            gate_rows[:token_groups], gate[:, 0, :].rearrange("r (b c) -> b r c", c=GROUP)
+        )
 
         raw1 = raw_tile()
         nc.sync.dma_start(raw1[:, 0], by_pass(w1[SHARED])[:, 0])
@@ -192,18 +195,22 @@ def tile_moe_shr_glu_silu_kernel(
         nc.sync.dma_start(pos_sb[0][:], pos1)
         nc.sync.dma_start(pos_sb[1][:], pos2)
 
-        gate_sb = [keep.tile([P, T], F32, name=f"gate_sb{r}") for r in range(2)]
-        for (first, per), column in zip(pieces, columns):
-            for r in range(2):
-                spread = bank([P, PACK, GROUP])
-                for c in range(per):
-                    nc.tensor.transpose(
-                        spread[:, c, :], column[:, r, c : c + 1].to_broadcast([P, P]), identity[:]
-                    )
-                nc.scalar.copy(
-                    gate_sb[r][:, first : first + P * per].rearrange("p (n c) -> p n c", c=per),
-                    spread[:, :per, :].rearrange("p c n -> p n c"),
-                )
+        turned = bank([P, 2, P])
+        for r in range(2):
+            nc.tensor.transpose(turned[:, r], gate_rows[:, r], identity[:])
+        gate_columns = keep.tile([P, 2, token_groups], F32, name="gate_columns")
+        nc.scalar.copy(gate_columns[:], turned[:, :, :token_groups])
+        second_gate = keep.tile([P, T], F32, name="second_gate")
+        for first in range(0, token_groups, PACK):
+            count = min(PACK, token_groups - first)
+            spread = bank([P, count, GROUP])
+            for b in range(count):
+                column = gate_columns[:, 1, first + b : first + b + 1]
+                nc.tensor.transpose(spread[:, b], column.to_broadcast([P, P]), identity[:])
+            nc.scalar.copy(
+                second_gate[:, first * GROUP : (first + count) * GROUP],
+                spread[:].rearrange("p b n -> p (b n)"),
+            )
 
         def gather(g, source, dtype):
             piece = offs_sb[:, g * GATHER // 16 : (g + 1) * GATHER // 16]
@@ -226,7 +233,6 @@ def tile_moe_shr_glu_silu_kernel(
         w2_rows = w2.rearrange("e (p j) n -> p e j n", j=PACK)
 
         all_tokens = (token_words, token_scales, 0)
-        token_groups = T // GROUP
         accs1 = banks(token_groups)
         for index in range(3):
             gather_next()
@@ -315,8 +321,10 @@ def tile_moe_shr_glu_silu_kernel(
             nc.sync.dma_start(late_rows[expert], w2_rows[:, expert])
         first = rounded_half(vector_copy, raw3[:, 1], 0)
         second = shared_half(raw3[:, 1], LAST_SHARE)
-        add_half(accs3, first, slots, 1, 0)
-        add_half(accs3, second, slots, 1, 1)
+        weights = quantize_half(first) + quantize_half(second)
+        for b, order in enumerate(((0, 1, 2, 3), (2, 3, 0, 1))):
+            for t in order:
+                product(accs3[b], weights[t], slots, b, 1, t, False, t == order[-1])
 
         def quantize_pair(rounded, name):
             codes, scales = quantize_columns(rounded[:].rearrange("p e n j -> p (e n) j"), name)
@@ -359,13 +367,13 @@ def tile_moe_shr_glu_silu_kernel(
             shared_turned.append(chained([P, 2, N], F32))
             nc.scalar.copy(shared_turned[c][:], acc[:])
 
-        def pick(r, c):
+        def results_at(r, c):
+            return y_slots[:].indirect(pos_sb[r][:, c * LIST_COLS : (c + 1) * LIST_COLS])
+
+        def pick(c):
             picked = chained([P, C], F32)
             nc.vector.tensor_tensor(
-                picked[:],
-                y_slots[:].indirect(pos_sb[r][:, c * LIST_COLS : (c + 1) * LIST_COLS]),
-                gate_sb[r][:, c * C : (c + 1) * C],
-                MULT,
+                picked[:], results_at(1, c), second_gate[:, c * C : (c + 1) * C], MULT
             )
             return picked
 
@@ -379,23 +387,25 @@ def tile_moe_shr_glu_silu_kernel(
 
         chunks = T // C
         first_turned, partials = [], []
-        for c in range(chunks + 1):
-            if c < chunks:
-                first_pick = pick(0, c)
-                acc = bank([P, 2, N])
-                for b in range(2):
-                    turn(acc[:, b], first_pick[:, group_cols(0, b)], True, True)
-                first_turned.append(chained([P, 2, N], F32))
-                nc.scalar.copy(first_turned[c][:], acc[:])
-            if c > 0:
-                partials.append(bank([P, C]))
-                for b in range(2):
-                    block = partials[c - 1][:, group_cols(0, b)]
-                    turn(block, shared_turned[c - 1][:, b], True, False)
-                    turn(block, first_turned[c - 1][:, b], False, True)
-        second_picks = [pick(1, c) for c in range(2)]
+        for c in range(chunks):
+            first_pick = chained([P, C], F32)
+            nc.vector.tensor_copy(first_pick[:], results_at(0, c))
+            acc = bank([P, 2, N])
+            for b in range(2):
+                turn(acc[:, b], first_pick[:, group_cols(0, b)], True, True)
+            first_turned.append(chained([P, 2, N], F32))
+            for b in range(2):
+                weight = gate_columns[:, 0, 2 * c + b : 2 * c + b + 1]
+                nc.scalar.activation(first_turned[c][:, b], acc[:, b], COPY, scale=weight)
+            partials.append(bank([P, C]))
+            for b in range(2):
+                turn(partials[c][:, group_cols(0, b)], shared_turned[c][:, b], b == 0, False)
+        for c in range(chunks):
+            for b in range(2):
+                turn(partials[c][:, group_cols(0, b)], first_turned[c][:, b], False, b == 1)
+        second_picks = [pick(c) for c in range(2)]
         for c in range(T // C):
             result = add(partials[c], second_picks[c])
             nc.sync.dma_start(out[:, c * C : (c + 1) * C], result[:])
             if c == 0:
-                second_picks.append(pick(1, 2))
+                second_picks.append(pick(2))

@@ -32,7 +32,7 @@ DMA_ALIGN = 256
 
 EARLY_W2 = 2
 SCALAR_ALONE = 2
-EAGER = 3
+EAGER = 4
 NEXT_SHARE = 24
 LAST_SHARE = 40
 
@@ -174,43 +174,36 @@ def tile_moe_shr_glu_silu_kernel(
         token_groups = T // GROUP
         gate_rows = keep.tile([P, 2, GROUP], F32, name="gate_rows", align_bytes=DMA_ALIGN)
         nc.gpsimd.memset(gate_rows[:], 0.0)
-        nc.scalar.dma_start(
-            gate_rows[:token_groups], gate[:, 0, :].rearrange("r (b c) -> b r c", c=GROUP)
-        )
 
         raw1 = raw_tile()
-        nc.sync.dma_start(raw1[:, 0], by_pass(w1[SHARED])[:, 0])
+        for o in range(PASSES):
+            nc.sync.dma_start(raw1[:, o], by_pass(w1[SHARED])[:, o])
         for q in range(4):
             nc.sync.dma_start(
                 token_scales[32 * q : 32 * q + 4 * PASSES, :].bitcast(I32),
                 x_scales[:, 4 * q : 4 * q + 4, :].bitcast(I32),
             )
-        nc.sync.dma_start(raw1[:, 1], by_pass(w1[SHARED])[:, 1])
         raw3 = raw_tile()
-        for o in range(PASSES):
-            nc.sync.dma_start(raw3[:, o], by_pass(w3[SHARED])[:, o])
+        nc.sync.dma_start(raw3[:], by_pass(w3[SHARED]))
         pos_sb = [
             keep.tile([P, T // 16], U16, name=f"pos_sb{r}", align_bytes=DMA_ALIGN) for r in range(2)
         ]
         nc.sync.dma_start(pos_sb[0][:], pos1)
         nc.sync.dma_start(pos_sb[1][:], pos2)
 
-        turned = bank([P, 2, P])
-        for r in range(2):
-            nc.tensor.transpose(turned[:, r], gate_rows[:, r], identity[:])
         gate_columns = keep.tile([P, 2, token_groups], F32, name="gate_columns")
-        nc.scalar.copy(gate_columns[:], turned[:, :, :token_groups])
-        second_gate = keep.tile([P, T], F32, name="second_gate")
-        for first in range(0, token_groups, PACK):
-            count = min(PACK, token_groups - first)
-            spread = bank([P, count, GROUP])
-            for b in range(count):
-                column = gate_columns[:, 1, first + b : first + b + 1]
-                nc.tensor.transpose(spread[:, b], column.to_broadcast([P, P]), identity[:])
-            nc.scalar.copy(
-                second_gate[:, first * GROUP : (first + count) * GROUP],
-                spread[:].rearrange("p b n -> p (b n)"),
-            )
+        second_gate = keep.tile([P, T - C], F32, name="second_gate")
+
+        def spread_gate():
+            turned = bank([P, 2, P])
+            for r in range(2):
+                nc.tensor.transpose(turned[:, r], gate_rows[:, r], identity[:])
+            nc.scalar.copy(gate_columns[:], turned[:, :, :token_groups])
+            spread = bank([P, T - C])
+            for b in range(2, token_groups):
+                column = gate_columns[:, 1, b : b + 1].to_broadcast([P, P])
+                nc.tensor.transpose(spread[:, group_cols(0, b - 2)], column, identity[:])
+            nc.scalar.copy(second_gate[:], spread[:])
 
         def gather(g, source, dtype):
             piece = offs_sb[:, g * GATHER // 16 : (g + 1) * GATHER // 16]
@@ -219,15 +212,18 @@ def tile_moe_shr_glu_silu_kernel(
             return picked
 
         sources = [(token_words[0], U32), (token_words[1], U32), (token_scales[:], U8)]
-        gathered = []
+        gathered = {}
+
+        pieces = E * C // GATHER
+        to_gather = [(g, kind) for kind in range(3) for g in range(pieces)]
 
         def gather_next():
-            count = len(gathered)
-            gathered.append(gather(count // 3, *sources[count % 3]))
+            g, kind = to_gather[len(gathered)]
+            gathered[g, kind] = gather(g, *sources[kind])
 
         def slots_of(e):
             g = e * C // GATHER
-            return gathered[3 * g : 3 * g + 2], gathered[3 * g + 2], e * C % GATHER
+            return [gathered[g, o] for o in range(PASSES)], gathered[g, PASSES], e * C % GATHER
 
         y_slots = keep.tile([P, E * C], F32, name="y_slots")
         w2_rows = w2.rearrange("e (p j) n -> p e j n", j=PACK)
@@ -241,15 +237,19 @@ def tile_moe_shr_glu_silu_kernel(
                 rounded = rounded_half(scalar_copy, raw1[:, o], half)
                 gather_next()
                 add_half(accs1, rounded, all_tokens, o, half)
-        rounded_c = [rounded_half(scalar_copy, raw3[:, 0], half) for half in range(2)]
+        rounded = [rounded_half(scalar_copy, raw3[:, 0], half) for half in range(2)]
+        rounded.extend(rounded_half(vector_copy, raw3[:, 1], half) for half in range(2))
+        silus = [silu_of(acc) for acc in accs1]
+        weights = [operand for half in rounded for operand in quantize_half(half)]
+        accs3 = []
+        for b in range(token_groups):
+            accs3.append(bank([P, PACK, GROUP]))
+            for o in range(PASSES):
+                for t in range(PACK):
+                    index = PACK * o + t
+                    product(accs3[b], weights[index], all_tokens, b, o, t, index == 0, index == 7)
         for index in range(2):
             gather_next()
-        rounded_d = [rounded_half(vector_copy, raw3[:, 1], half) for half in range(2)]
-        silus = [silu_of(acc) for acc in accs1]
-        accs3 = banks(token_groups)
-        for o, rounded in enumerate((rounded_c, rounded_d)):
-            for half in range(2):
-                add_half(accs3, rounded[half], all_tokens, o, half)
         pending = None
         waiting = [(accs3[2 * c : 2 * c + 2], silus[2 * c : 2 * c + 2]) for c in range(T // C)]
         hidden = []
@@ -263,7 +263,7 @@ def tile_moe_shr_glu_silu_kernel(
             eager = e >= EAGER
             raw1, raw3 = raw_tile(), raw_tile()
             for raw, matrix in ((raw1, w1[e]), (raw3, w3[e])):
-                if 0 < e < EAGER:
+                if e < EAGER:
                     nc.sync.dma_start(raw[:], by_pass(matrix))
                 else:
                     for o in range(PASSES):
@@ -271,6 +271,11 @@ def tile_moe_shr_glu_silu_kernel(
             if e == 0:
                 early_w2 = keep.tile([P, EARLY_W2, PACK, N], F32, name="early_w2", align_bytes=DMA_ALIGN)
                 nc.sync.dma_start(early_w2[:], w2_rows[:, :EARLY_W2])
+                nc.sync.dma_start(
+                    gate_rows[:token_groups], gate[:, 0, :].rearrange("r (b c) -> b r c", c=GROUP)
+                )
+            if e == 3:
+                spread_gate()
             early = 0 < e <= EARLY_W2
             multiply_step = 0 if (e == 0 or e > EAGER) else 1
             for step in range(2 * PASSES):
@@ -330,13 +335,15 @@ def tile_moe_shr_glu_silu_kernel(
             codes, scales = quantize_columns(rounded[:].rearrange("p e n j -> p (e n) j"), name)
             return [(codes[:, u * N : (u + 1) * N], scales[:, u * N : (u + 1) * N]) for u in range(2)]
 
-        pair_a = chained([P, 2, N, PACK], BF16)
-        round_w2(scalar_copy, pair_a[:, 0], late_rows[LAST - 3])
-        round_w2(vector_copy, pair_a[:, 1], late_rows[LAST - 2])
+        pair_a = [
+            rounded_w2(scalar_copy, late_rows[LAST - 3]),
+            rounded_w2(vector_copy, late_rows[LAST - 2]),
+        ]
         pair_b = chained([P, 2, N, PACK], BF16)
         round_w2(scalar_copy, pair_b[:, 0], late_rows[LAST - 1])
         round_w2(scalar_copy, pair_b[:, 1], late_rows[LAST])
-        weights_a = quantize_pair(pair_a, "codes2_a")
+        rounded_shared = rounded_w2(scalar_copy, late_rows[SHARED])
+        weights_a = [quantize_columns(pair_a[u][:], f"codes2_a{u}") for u in range(2)]
         y_a = bank([P, 2, C])
         for u in range(2):
             second_layer(y_a[:, u], weights_a[u], hidden[LAST + u])
@@ -348,16 +355,15 @@ def tile_moe_shr_glu_silu_kernel(
         weights_b = quantize_pair(pair_b, "codes2_b")
         y_b = bank([P, C])
         second_layer(y_b[:], weights_b[0], hidden[LAST + 2])
-        rounded_shared = rounded_w2(scalar_copy, late_rows[SHARED])
         y_last = []
         for b in range(2):
             last_hidden = quantize_columns(h_groups[b][:], f"last_h{b}")
             y_last.append(bank([P, GROUP]))
             second_layer(y_last[b][:], weights_b[1], last_hidden)
+        weights_shared = quantize_columns(rounded_shared[:], "codes2_shared")
         nc.scalar.copy(y_slots[:, (LAST - 1) * C : LAST * C], y_b[:])
         for b in range(2):
             nc.vector.tensor_copy(y_slots[:, group_cols(LAST * C, b)], y_last[b][:])
-        weights_shared = quantize_columns(rounded_shared[:], "codes2_shared")
         shared_turned = []
         for c in range(T // C):
             acc = bank([P, 2, N])
@@ -373,39 +379,50 @@ def tile_moe_shr_glu_silu_kernel(
         def pick(c):
             picked = chained([P, C], F32)
             nc.vector.tensor_tensor(
-                picked[:], results_at(1, c), second_gate[:, c * C : (c + 1) * C], MULT
+                picked[:], results_at(1, c), second_gate[:, (c - 1) * C : c * C], MULT
             )
             return picked
-
-        def add(a, b):
-            total = chained([P, C], F32)
-            nc.vector.tensor_tensor(total[:], a[:], b[:], ADD)
-            return total
 
         def turn(acc, block, start, stop):
             nc.tensor.matmul(acc, block, identity[:], start=start, stop=stop, is_transpose=True)
 
         chunks = T // C
-        first_turned, partials = [], []
+        def turned_pick(r, c):
+            picked = chained([P, C], F32)
+            nc.vector.tensor_copy(picked[:], results_at(r, c))
+            weighted = chained([P, 2, N], F32)
+            for b in range(2):
+                acc = bank([P, N])
+                turn(acc[:], picked[:, group_cols(0, b)], True, True)
+                weight = gate_columns[:, r, 2 * c + b : 2 * c + b + 1]
+                nc.scalar.activation(weighted[:, b], acc[:], COPY, scale=weight)
+            return weighted
+
+        ranges = [(0, 2), (2, 4), (4, 5), (5, 6)]
+        sums = [None] * token_groups
+
+        def turn_back(c, term, first, last):
+            for b in range(2 * c, 2 * c + 2):
+                start, stop = [r for r in ranges if r[0] <= b < r[1]][0]
+                if first and b == start:
+                    acc = bank([P, (stop - start) * GROUP])
+                    sums[start:stop] = [acc] * (stop - start)
+                block = sums[b][:, group_cols(0, b - start)]
+                turn(block, term[:, b % 2], first and b == start, last and b == stop - 1)
+
         for c in range(chunks):
-            first_pick = chained([P, C], F32)
-            nc.vector.tensor_copy(first_pick[:], results_at(0, c))
-            acc = bank([P, 2, N])
-            for b in range(2):
-                turn(acc[:, b], first_pick[:, group_cols(0, b)], True, True)
-            first_turned.append(chained([P, 2, N], F32))
-            for b in range(2):
-                weight = gate_columns[:, 0, 2 * c + b : 2 * c + b + 1]
-                nc.scalar.activation(first_turned[c][:, b], acc[:, b], COPY, scale=weight)
-            partials.append(bank([P, C]))
-            for b in range(2):
-                turn(partials[c][:, group_cols(0, b)], shared_turned[c][:, b], b == 0, False)
-        for c in range(chunks):
-            for b in range(2):
-                turn(partials[c][:, group_cols(0, b)], first_turned[c][:, b], False, b == 1)
-        second_picks = [pick(c) for c in range(2)]
-        for c in range(T // C):
-            result = add(partials[c], second_picks[c])
-            nc.sync.dma_start(out[:, c * C : (c + 1) * C], result[:])
-            if c == 0:
-                second_picks.append(pick(2))
+            turn_back(c, shared_turned[c], True, False)
+        picks = [(0, 0), (1, 0)] + [(0, c) for c in range(1, chunks)]
+        terms = [turned_pick(r, c) for r, c in picks]
+        for index, (r, c) in enumerate(picks):
+            turn_back(c, terms[index], False, index > 0)
+        second_picks = [None] + [pick(c) for c in range(1, chunks)]
+        for start, stop in ranges:
+            result = chained([P, (stop - start) * GROUP], F32)
+            if start == 0:
+                nc.scalar.copy(result[:], sums[start][:])
+            else:
+                first = start % 2 * GROUP
+                other = second_picks[start // 2][:, first : first + (stop - start) * GROUP]
+                nc.vector.tensor_tensor(result[:], sums[start][:], other, ADD)
+            nc.sync.dma_start(out[:, start * GROUP : stop * GROUP], result[:])

@@ -30,7 +30,7 @@ LAST = E - 1
 MX_ALIGN = 64
 DMA_ALIGN = 256
 
-EARLY_W2 = 2
+EARLY_W2 = 1
 SCALAR_ALONE = 2
 EAGER = 4
 NEXT_SHARE = 24
@@ -157,6 +157,9 @@ def tile_moe_shr_glu_silu_kernel(
             return [bank([P, PACK, GROUP]) for b in range(count)]
 
         vector_copy, scalar_copy = nc.vector.tensor_copy, nc.scalar.copy
+
+        def gpsimd_round(dst, src):
+            nc.gpsimd.tensor_scalar(dst, src, 1.0, 0.0, MULT, ADD)
 
         token_scales = keep.tile([P, T], U8, name="token_scales", align_bytes=DMA_ALIGN)
         nc.vector.memset(token_scales[:].bitcast(I32), 0)
@@ -335,33 +338,37 @@ def tile_moe_shr_glu_silu_kernel(
             codes, scales = quantize_columns(rounded[:].rearrange("p e n j -> p (e n) j"), name)
             return [(codes[:, u * N : (u + 1) * N], scales[:, u * N : (u + 1) * N]) for u in range(2)]
 
-        pair_a = [
-            rounded_w2(scalar_copy, late_rows[LAST - 3]),
-            rounded_w2(vector_copy, late_rows[LAST - 2]),
-        ]
-        pair_b = chained([P, 2, N, PACK], BF16)
-        round_w2(scalar_copy, pair_b[:, 0], late_rows[LAST - 1])
-        round_w2(scalar_copy, pair_b[:, 1], late_rows[LAST])
+        pair = chained([P, 2, N, PACK], BF16)
+        round_w2(scalar_copy, pair[:, 1], late_rows[1])
+        rounded_b = rounded_w2(vector_copy, late_rows[2])
+        round_w2(scalar_copy, pair[:, 0], late_rows[3])
+        rounded_last = rounded_w2(scalar_copy, late_rows[LAST])
         rounded_shared = rounded_w2(scalar_copy, late_rows[SHARED])
-        weights_a = [quantize_columns(pair_a[u][:], f"codes2_a{u}") for u in range(2)]
+        weights_a = [quantize_columns(pair[:, 1], "codes2_a"), quantize_columns(rounded_b[:], "codes2_b")]
+        gpsimd_round(pair[:, 1], late_rows[4].rearrange("p j n -> p n j"))
         y_a = bank([P, 2, C])
         for u in range(2):
-            second_layer(y_a[:, u], weights_a[u], hidden[LAST + u])
+            second_layer(y_a[:, u], weights_a[u], hidden[4 + u])
         h_groups = []
         for b in range(2):
             h_groups.append(chained([P, GROUP, PACK], BF16))
             multiply(h_groups[b][:], accs3[b], silus[b])
-        nc.scalar.copy(y_slots[:, (LAST - 3) * C : (LAST - 1) * C], y_a[:].rearrange("p e n -> p (e n)"))
-        weights_b = quantize_pair(pair_b, "codes2_b")
-        y_b = bank([P, C])
-        second_layer(y_b[:], weights_b[0], hidden[LAST + 2])
+        nc.scalar.copy(y_slots[:, C : 3 * C], y_a[:].rearrange("p e n -> p (e n)"))
+        weights_b = quantize_pair(pair, "codes2_pair")
+        y_b = []
+        for u in range(2):
+            y_b.append(bank([P, C]))
+            second_layer(y_b[u][:], weights_b[u], hidden[6 + u])
+        last_hidden = [quantize_columns(h_groups[0][:], "last_h0")]
+        weights_last = quantize_columns(rounded_last[:], "codes2_last")
+        last_hidden.append(quantize_columns(h_groups[1][:], "last_h1"))
         y_last = []
         for b in range(2):
-            last_hidden = quantize_columns(h_groups[b][:], f"last_h{b}")
             y_last.append(bank([P, GROUP]))
-            second_layer(y_last[b][:], weights_b[1], last_hidden)
+            second_layer(y_last[b][:], weights_last, last_hidden[b])
         weights_shared = quantize_columns(rounded_shared[:], "codes2_shared")
-        nc.scalar.copy(y_slots[:, (LAST - 1) * C : LAST * C], y_b[:])
+        nc.vector.tensor_copy(y_slots[:, 3 * C : 4 * C], y_b[0][:])
+        nc.scalar.copy(y_slots[:, 4 * C : 5 * C], y_b[1][:])
         for b in range(2):
             nc.vector.tensor_copy(y_slots[:, group_cols(LAST * C, b)], y_last[b][:])
         shared_turned = []
@@ -413,8 +420,10 @@ def tile_moe_shr_glu_silu_kernel(
         for c in range(chunks):
             turn_back(c, shared_turned[c], True, False)
         picks = [(0, 0), (1, 0)] + [(0, c) for c in range(1, chunks)]
-        terms = [turned_pick(r, c) for r, c in picks]
+        terms = [turned_pick(*picks[0])]
         for index, (r, c) in enumerate(picks):
+            if index + 1 < len(picks):
+                terms.append(turned_pick(*picks[index + 1]))
             turn_back(c, terms[index], False, index > 0)
         second_picks = [None] + [pick(c) for c in range(1, chunks)]
         for start, stop in ranges:

@@ -32,6 +32,7 @@ DMA_ALIGN = 256
 
 EARLY_W2 = 1
 SCALAR_ALONE = 2
+SHARED_OUT = 2
 EAGER = 4
 NEXT_SHARE = 24
 LAST_SHARE = 40
@@ -195,18 +196,22 @@ def tile_moe_shr_glu_silu_kernel(
         nc.sync.dma_start(pos_sb[1][:], pos2)
 
         gate_columns = keep.tile([P, 2, token_groups], F32, name="gate_columns")
-        second_gate = keep.tile([P, T - C], F32, name="second_gate")
+        spread_gates = keep.tile([P, T + GROUP], F32, name="spread_gates")
+        to_spread = [(0, b) for b in range(token_groups)] + [(1, token_groups - 1)]
 
-        def spread_gate():
+        def turn_gate():
             turned = bank([P, 2, P])
             for r in range(2):
                 nc.tensor.transpose(turned[:, r], gate_rows[:, r], identity[:])
             nc.scalar.copy(gate_columns[:], turned[:, :, :token_groups])
-            spread = bank([P, T - C])
-            for b in range(2, token_groups):
-                column = gate_columns[:, 1, b : b + 1].to_broadcast([P, P])
-                nc.tensor.transpose(spread[:, group_cols(0, b - 2)], column, identity[:])
-            nc.scalar.copy(second_gate[:], spread[:])
+
+        def spread_gate(start, stop):
+            spread = bank([P, (stop - start) * GROUP])
+            for b in range(start, stop):
+                r, group = to_spread[b]
+                column = gate_columns[:, r, group : group + 1].to_broadcast([P, P])
+                nc.tensor.transpose(spread[:, group_cols(0, b - start)], column, identity[:])
+            nc.scalar.copy(spread_gates[:, start * GROUP : stop * GROUP], spread[:])
 
         def gather(g, source, dtype):
             piece = offs_sb[:, g * GATHER // 16 : (g + 1) * GATHER // 16]
@@ -229,6 +234,7 @@ def tile_moe_shr_glu_silu_kernel(
             return [gathered[g, o] for o in range(PASSES)], gathered[g, PASSES], e * C % GATHER
 
         y_slots = keep.tile([P, E * C], F32, name="y_slots")
+        shared_turned = keep.tile([P, token_groups, N], F32, name="shared_turned")
         w2_rows = w2.rearrange("e (p j) n -> p e j n", j=PACK)
 
         all_tokens = (token_words, token_scales, 0)
@@ -274,11 +280,17 @@ def tile_moe_shr_glu_silu_kernel(
             if e == 0:
                 early_w2 = keep.tile([P, EARLY_W2, PACK, N], F32, name="early_w2", align_bytes=DMA_ALIGN)
                 nc.sync.dma_start(early_w2[:], w2_rows[:, :EARLY_W2])
+                shared_w2 = keep.tile([P, PACK, N], F32, name="shared_w2", align_bytes=DMA_ALIGN)
+                nc.sync.dma_start(shared_w2[:], w2_rows[:, SHARED])
                 nc.sync.dma_start(
                     gate_rows[:token_groups], gate[:, 0, :].rearrange("r (b c) -> b r c", c=GROUP)
                 )
+            if e == 2:
+                turn_gate()
             if e == 3:
-                spread_gate()
+                spread_gate(0, PACK)
+            if e == 4:
+                spread_gate(PACK, len(to_spread))
             early = 0 < e <= EARLY_W2
             multiply_step = 0 if (e == 0 or e > EAGER) else 1
             for step in range(2 * PASSES):
@@ -294,6 +306,8 @@ def tile_moe_shr_glu_silu_kernel(
                     second = rounded_half(scalar_copy, rows, 1)
                 if step == 0 and early:
                     rounded2 = rounded_w2(scalar_copy, early_w2[:, e - 1])
+                if step == 0 and e == SHARED_OUT:
+                    rounded2 = rounded_w2(scalar_copy, shared_w2[:])
                 if step == multiply_step:
                     products = [multiply_pair(*pair) for pair in waiting]
                 if step == multiply_step + 1:
@@ -301,6 +315,17 @@ def tile_moe_shr_glu_silu_kernel(
                 if step == 2 and early:
                     y_acc = bank([P, C])
                     second_layer(y_acc[:], quantize_columns(rounded2[:], f"codes2_{e}"), hidden[e + 2])
+                if step == 2 and e == SHARED_OUT:
+                    weights_shared = quantize_columns(rounded2[:], "codes2_shared")
+                    shared_accs = []
+                    for start, stop in ((0, PACK), (PACK, token_groups)):
+                        shared_accs.append(bank([P, stop - start, N]))
+                        for b in range(start, stop):
+                            tokens = [plane[:, group_cols(0, b % 2)] for plane in hidden[b // 2]]
+                            if b < token_groups - 1:
+                                second_layer(shared_accs[-1][:, b - start], tokens, weights_shared)
+                            else:
+                                second_layer(shared_accs[-1][:, b - start], weights_shared, tokens)
                 if pending:
                     add_half(*pending)
                 if o == 0:
@@ -318,9 +343,12 @@ def tile_moe_shr_glu_silu_kernel(
                     silus = [silu_of(acc) for acc in accs1]
                 if step == 3 and early:
                     nc.scalar.copy(y_slots[:, (e - 1) * C : e * C], y_acc[:])
+                if step == 3 and e == SHARED_OUT:
+                    nc.scalar.copy(shared_turned[:, :PACK], shared_accs[0][:])
+                    nc.scalar.copy(shared_turned[:, PACK:], shared_accs[1][:])
             waiting = [(accs3, silus)]
 
-        late = list(range(EARLY_W2, E + 1))
+        late = list(range(EARLY_W2, E))
         late_raw = raw_tile()[:].rearrange("p o j i -> p (o j i)")
         late_rows = {}
         for index, expert in enumerate(late):
@@ -343,7 +371,6 @@ def tile_moe_shr_glu_silu_kernel(
         rounded_b = rounded_w2(vector_copy, late_rows[2])
         round_w2(scalar_copy, pair[:, 0], late_rows[3])
         rounded_last = rounded_w2(scalar_copy, late_rows[LAST])
-        rounded_shared = rounded_w2(scalar_copy, late_rows[SHARED])
         weights_a = [quantize_columns(pair[:, 1], "codes2_a"), quantize_columns(rounded_b[:], "codes2_b")]
         gpsimd_round(pair[:, 1], late_rows[4].rearrange("p j n -> p n j"))
         y_a = bank([P, 2, C])
@@ -366,72 +393,69 @@ def tile_moe_shr_glu_silu_kernel(
         for b in range(2):
             y_last.append(bank([P, GROUP]))
             second_layer(y_last[b][:], weights_last, last_hidden[b])
-        weights_shared = quantize_columns(rounded_shared[:], "codes2_shared")
-        nc.vector.tensor_copy(y_slots[:, 3 * C : 4 * C], y_b[0][:])
-        nc.scalar.copy(y_slots[:, 4 * C : 5 * C], y_b[1][:])
+        for u in range(2):
+            nc.scalar.copy(y_slots[:, (3 + u) * C : (4 + u) * C], y_b[u][:])
         for b in range(2):
             nc.vector.tensor_copy(y_slots[:, group_cols(LAST * C, b)], y_last[b][:])
-        shared_turned = []
-        for c in range(T // C):
-            acc = bank([P, 2, N])
-            for b in range(2):
-                tokens = [plane[:, group_cols(0, b)] for plane in hidden[c]]
-                second_layer(acc[:, b], tokens, weights_shared)
-            shared_turned.append(chained([P, 2, N], F32))
-            nc.scalar.copy(shared_turned[c][:], acc[:])
 
-        def results_at(r, c):
-            return y_slots[:].indirect(pos_sb[r][:, c * LIST_COLS : (c + 1) * LIST_COLS])
+        def tokens_of(start, stop):
+            return slice(start * GROUP, stop * GROUP)
 
-        def pick(c):
-            picked = chained([P, C], F32)
-            nc.vector.tensor_tensor(
-                picked[:], results_at(1, c), second_gate[:, (c - 1) * C : c * C], MULT
-            )
-            return picked
+        def results_at(r, start, stop):
+            return y_slots[:].indirect(pos_sb[r][:, start * GROUP // 16 : stop * GROUP // 16])
 
         def turn(acc, block, start, stop):
             nc.tensor.matmul(acc, block, identity[:], start=start, stop=stop, is_transpose=True)
 
-        chunks = T // C
-        def turned_pick(r, c):
-            picked = chained([P, C], F32)
-            nc.vector.tensor_copy(picked[:], results_at(r, c))
-            weighted = chained([P, 2, N], F32)
-            for b in range(2):
-                acc = bank([P, N])
-                turn(acc[:], picked[:, group_cols(0, b)], True, True)
-                weight = gate_columns[:, r, 2 * c + b : 2 * c + b + 1]
-                nc.scalar.activation(weighted[:, b], acc[:], COPY, scale=weight)
-            return weighted
+        def gated_pick(r, start, stop, gates):
+            picked = chained([P, (stop - start) * GROUP], F32)
+            nc.vector.tensor_tensor(picked[:], results_at(r, start, stop), gates, MULT)
+            return picked
 
-        ranges = [(0, 2), (2, 4), (4, 5), (5, 6)]
-        sums = [None] * token_groups
+        def turned_pick(start, stop):
+            picked = chained([P, (stop - start) * GROUP], F32)
+            nc.scalar.activation(picked[:], results_at(1, start, stop), COPY)
+            turned = []
+            for u in range(stop - start):
+                turned.append(bank([P, N]))
+                turn(turned[u][:], picked[:, group_cols(0, u)], True, True)
+            return turned
 
-        def turn_back(c, term, first, last):
-            for b in range(2 * c, 2 * c + 2):
-                start, stop = [r for r in ranges if r[0] <= b < r[1]][0]
-                if first and b == start:
-                    acc = bank([P, (stop - start) * GROUP])
-                    sums[start:stop] = [acc] * (stop - start)
-                block = sums[b][:, group_cols(0, b - start)]
-                turn(block, term[:, b % 2], first and b == start, last and b == stop - 1)
-
-        for c in range(chunks):
-            turn_back(c, shared_turned[c], True, False)
-        picks = [(0, 0), (1, 0)] + [(0, c) for c in range(1, chunks)]
-        terms = [turned_pick(*picks[0])]
-        for index, (r, c) in enumerate(picks):
-            if index + 1 < len(picks):
-                terms.append(turned_pick(*picks[index + 1]))
-            turn_back(c, terms[index], False, index > 0)
-        second_picks = [None] + [pick(c) for c in range(1, chunks)]
+        ranges = [(0, 2), (2, 4), (4, 5)]
+        sums = []
         for start, stop in ranges:
-            result = chained([P, (stop - start) * GROUP], F32)
-            if start == 0:
-                nc.scalar.copy(result[:], sums[start][:])
-            else:
-                first = start % 2 * GROUP
-                other = second_picks[start // 2][:, first : first + (stop - start) * GROUP]
-                nc.vector.tensor_tensor(result[:], sums[start][:], other, ADD)
-            nc.sync.dma_start(out[:, start * GROUP : stop * GROUP], result[:])
+            sums.append(bank([P, stop - start, GROUP]))
+            for b in range(start, stop):
+                turn(sums[-1][:, b - start], shared_turned[:, b], b == start, False)
+
+        def weigh(index, turned):
+            start, stop = ranges[index]
+            weighted = chained([P, stop - start, N], F32)
+            for b in range(start, stop):
+                weight = gate_columns[:, 1, b : b + 1]
+                nc.scalar.activation(weighted[:, b - start], turned[b - start][:], COPY, scale=weight)
+                turn(sums[index][:, b - start], weighted[:, b - start], False, b == stop - 1)
+
+        def add(first, second):
+            total = chained([P, second.shape[1]], F32)
+            nc.vector.tensor_tensor(total[:], first, second, ADD)
+            return total
+
+        def finish(index, picked):
+            total = add(sums[index][:].rearrange("p b n -> p (b n)"), picked)
+            nc.sync.dma_start(out[:, tokens_of(*ranges[index])], total[:])
+
+        turned = [turned_pick(*ranges[0])]
+        front = gated_pick(0, 0, 4, spread_gates[:, tokens_of(0, 4)])
+        turned.append(turned_pick(*ranges[1]))
+        back = gated_pick(0, 4, 6, spread_gates[:, tokens_of(4, 6)])
+        turned.append(turned_pick(*ranges[2]))
+        weigh(0, turned[0])
+        last_second = gated_pick(1, 5, 6, spread_gates[:, tokens_of(6, 7)])
+        weigh(1, turned[1])
+        last_first = add(shared_turned[:, 5], back[:, tokens_of(1, 2)])
+        weigh(2, turned[2])
+        finish(0, front[:, tokens_of(0, 2)])
+        nc.sync.dma_start(out[:, tokens_of(5, 6)], add(last_first[:], last_second[:])[:])
+        finish(1, front[:, tokens_of(2, 4)])
+        finish(2, back[:, tokens_of(0, 1)])

@@ -33,7 +33,9 @@ DMA_ALIGN = 256
 EARLY_W2 = 1
 SCALAR_ALONE = 2
 SHARED_OUT = 2
+WHOLE_LOADS = 3
 EAGER = 4
+STREAM_SHARE = 112
 NEXT_SHARE = 24
 LAST_SHARE = 40
 
@@ -78,10 +80,11 @@ def tile_moe_shr_glu_silu_kernel(
             round_half(copy, rounded, rows, half, slice(0, P))
             return rounded
 
-        def shared_half(rows, vector_share):
+        def shared_half(rows, half, vector_share):
             rounded = chained([P, 2, P, PACK], BF16)
-            round_half(nc.scalar.copy, rounded, rows, 1, slice(vector_share, P))
-            round_half(nc.vector.tensor_copy, rounded, rows, 1, slice(0, vector_share))
+            copies = [(nc.vector.tensor_copy, slice(0, vector_share)), (nc.scalar.copy, slice(vector_share, P))]
+            for copy, m_range in copies[:: 1 - 2 * half]:
+                round_half(copy, rounded, rows, half, m_range)
             return rounded
 
         def round_w2(copy, rounded, rows):
@@ -272,16 +275,14 @@ def tile_moe_shr_glu_silu_kernel(
             eager = e >= EAGER
             raw1, raw3 = raw_tile(), raw_tile()
             for raw, matrix in ((raw1, w1[e]), (raw3, w3[e])):
-                if e < EAGER:
+                if e < WHOLE_LOADS:
                     nc.sync.dma_start(raw[:], by_pass(matrix))
                 else:
                     for o in range(PASSES):
                         nc.sync.dma_start(raw[:, o], by_pass(matrix)[:, o])
             if e == 0:
-                early_w2 = keep.tile([P, EARLY_W2, PACK, N], F32, name="early_w2", align_bytes=DMA_ALIGN)
-                nc.sync.dma_start(early_w2[:], w2_rows[:, :EARLY_W2])
-                shared_w2 = keep.tile([P, PACK, N], F32, name="shared_w2", align_bytes=DMA_ALIGN)
-                nc.sync.dma_start(shared_w2[:], w2_rows[:, SHARED])
+                early_w2 = keep.tile([P, 2, PACK, N], F32, name="early_w2", align_bytes=DMA_ALIGN)
+                nc.sync.dma_start(early_w2[:], w2_rows[:, 0 : SHARED + 1 : SHARED])
                 nc.sync.dma_start(
                     gate_rows[:token_groups], gate[:, 0, :].rearrange("r (b c) -> b r c", c=GROUP)
                 )
@@ -299,15 +300,20 @@ def tile_moe_shr_glu_silu_kernel(
                 if e == LAST and step == 3:
                     break
                 alone = 4 * e + step < SCALAR_ALONE
-                first = rounded_half(scalar_copy if alone else vector_copy, rows, 0)
+                if alone:
+                    first = rounded_half(scalar_copy, rows, 0)
+                elif e == LAST and step == 2:
+                    first = rounded_half(vector_copy, rows, 0)
+                else:
+                    first = shared_half(rows, 0, STREAM_SHARE)
                 if e == LAST and step == 2:
-                    second = shared_half(rows, NEXT_SHARE)
+                    second = shared_half(rows, 1, NEXT_SHARE)
                 else:
                     second = rounded_half(scalar_copy, rows, 1)
                 if step == 0 and early:
                     rounded2 = rounded_w2(scalar_copy, early_w2[:, e - 1])
                 if step == 0 and e == SHARED_OUT:
-                    rounded2 = rounded_w2(scalar_copy, shared_w2[:])
+                    rounded2 = rounded_w2(scalar_copy, early_w2[:, 1])
                 if step == multiply_step:
                     products = [multiply_pair(*pair) for pair in waiting]
                 if step == multiply_step + 1:
@@ -356,7 +362,7 @@ def tile_moe_shr_glu_silu_kernel(
             late_rows[expert] = rows.rearrange("p (j n) -> p j n", j=PACK)
             nc.sync.dma_start(late_rows[expert], w2_rows[:, expert])
         first = rounded_half(vector_copy, raw3[:, 1], 0)
-        second = shared_half(raw3[:, 1], LAST_SHARE)
+        second = shared_half(raw3[:, 1], 1, LAST_SHARE)
         weights = quantize_half(first) + quantize_half(second)
         for b, order in enumerate(((0, 1, 2, 3), (2, 3, 0, 1))):
             for t in order:

@@ -35,7 +35,7 @@ SCALAR_ALONE = 2
 SHARED_OUT = 2
 WHOLE_LOADS = 3
 EAGER = 4
-STREAM_SHARE = 112
+STREAM_SHARE = 16
 NEXT_SHARE = 24
 LAST_SHARE = 40
 
@@ -286,11 +286,11 @@ def tile_moe_shr_glu_silu_kernel(
                 nc.sync.dma_start(
                     gate_rows[:token_groups], gate[:, 0, :].rearrange("r (b c) -> b r c", c=GROUP)
                 )
-            if e == 2:
+            if e == 1:
                 turn_gate()
-            if e == 3:
+            if e == 2:
                 spread_gate(0, PACK)
-            if e == 4:
+            if e == 3:
                 spread_gate(PACK, len(to_spread))
             early = 0 < e <= EARLY_W2
             multiply_step = 0 if (e == 0 or e > EAGER) else 1
@@ -302,12 +302,12 @@ def tile_moe_shr_glu_silu_kernel(
                 alone = 4 * e + step < SCALAR_ALONE
                 if alone:
                     first = rounded_half(scalar_copy, rows, 0)
-                elif e == LAST and step == 2:
-                    first = rounded_half(vector_copy, rows, 0)
                 else:
-                    first = shared_half(rows, 0, STREAM_SHARE)
+                    first = rounded_half(vector_copy, rows, 0)
                 if e == LAST and step == 2:
                     second = shared_half(rows, 1, NEXT_SHARE)
+                elif e > 0:
+                    second = shared_half(rows, 1, STREAM_SHARE)
                 else:
                     second = rounded_half(scalar_copy, rows, 1)
                 if step == 0 and early:

@@ -452,16 +452,16 @@ def tile_moe_shr_glu_silu_kernel(
             nc.sync.dma_start(out[:, tokens_of(*ranges[index])], total[:])
 
         turned = [turned_pick(*ranges[0])]
-        front = gated_pick(0, 0, 4, spread_gates[:, tokens_of(0, 4)])
+        last_picks = [gated_pick(r, 5, 6, spread_gates[:, tokens_of(5 + r, 6 + r)]) for r in range(2)]
         turned.append(turned_pick(*ranges[1]))
-        back = gated_pick(0, 4, 6, spread_gates[:, tokens_of(4, 6)])
+        front = gated_pick(0, 0, 4, spread_gates[:, tokens_of(0, 4)])
         turned.append(turned_pick(*ranges[2]))
         weigh(0, turned[0])
-        last_second = gated_pick(1, 5, 6, spread_gates[:, tokens_of(6, 7)])
+        partial = add(shared_turned[:, 5], last_picks[0][:])
+        back = gated_pick(0, 4, 5, spread_gates[:, tokens_of(4, 5)])
         weigh(1, turned[1])
-        last_first = add(shared_turned[:, 5], back[:, tokens_of(1, 2)])
+        nc.sync.dma_start(out[:, tokens_of(5, 6)], add(partial[:], last_picks[1][:])[:])
         weigh(2, turned[2])
         finish(0, front[:, tokens_of(0, 2)])
-        nc.sync.dma_start(out[:, tokens_of(5, 6)], add(last_first[:], last_second[:])[:])
         finish(1, front[:, tokens_of(2, 4)])
-        finish(2, back[:, tokens_of(0, 1)])
+        finish(2, back[:])

@@ -266,9 +266,23 @@ def tile_moe_shr_glu_silu_kernel(
         waiting = [(accs3[2 * c : 2 * c + 2], silus[2 * c : 2 * c + 2]) for c in range(T // C)]
         hidden = []
 
+        wide = []
+
         def quantize_hidden(products):
             for h in products:
-                hidden.append(quantize_columns(h[:], f"h_codes{len(hidden)}"))
+                if len(hidden) < 2:
+                    if not wide:
+                        wide.append(keep.tile([P, 2 * C], U32, name="wide_codes", align_bytes=MX_ALIGN))
+                        wide.append(chained([P, 2 * C], U8))
+                    codes, scales = [plane[:, len(hidden) * C : (len(hidden) + 1) * C] for plane in wide]
+                    values = h[:].rearrange("p n t -> p (n t)")
+                    nc.vector.quantize_mx(out=codes.bitcast(FP8X4), scales=scales, in_=values)
+                    hidden.append((codes, scales))
+                else:
+                    hidden.append(quantize_columns(h[:], f"h_codes{len(hidden)}"))
+
+        def warm_up(spent):
+            second_layer(spent, weights_shared, (wide[0][:], wide[1][:]))
 
         for e in range(E):
             slots = slots_of(e)
@@ -361,6 +375,7 @@ def tile_moe_shr_glu_silu_kernel(
             rows = late_raw[:, index * PACK * N : (index + 1) * PACK * N]
             late_rows[expert] = rows.rearrange("p (j n) -> p j n", j=PACK)
             nc.sync.dma_start(late_rows[expert], w2_rows[:, expert])
+        warm_up(accs1[1][:].rearrange("p t n -> p (t n)"))
         first = rounded_half(vector_copy, raw3[:, 1], 0)
         second = shared_half(raw3[:, 1], 1, LAST_SHARE)
         weights = quantize_half(first) + quantize_half(second)
@@ -386,12 +401,13 @@ def tile_moe_shr_glu_silu_kernel(
         for b in range(2):
             h_groups.append(chained([P, GROUP, PACK], BF16))
             multiply(h_groups[b][:], accs3[b], silus[b])
+        warm_up(accs3[0][:].rearrange("p t n -> p (t n)"))
         nc.scalar.copy(y_slots[:, C : 3 * C], y_a[:].rearrange("p e n -> p (e n)"))
         weights_b = quantize_pair(pair, "codes2_pair")
         y_b = []
         for u in range(2):
-            y_b.append(bank([P, C]))
-            second_layer(y_b[u][:], weights_b[u], hidden[6 + u])
+            y_b.append(bank([P, 2 * C]))
+            second_layer(y_b[u][:, :C], weights_b[u], hidden[6 + u])
         last_hidden = [quantize_columns(h_groups[0][:], "last_h0")]
         weights_last = quantize_columns(rounded_last[:], "codes2_last")
         last_hidden.append(quantize_columns(h_groups[1][:], "last_h1"))
@@ -400,9 +416,12 @@ def tile_moe_shr_glu_silu_kernel(
             y_last.append(bank([P, GROUP]))
             second_layer(y_last[b][:], weights_last, last_hidden[b])
         for u in range(2):
-            nc.scalar.copy(y_slots[:, (3 + u) * C : (4 + u) * C], y_b[u][:])
+            nc.scalar.copy(y_slots[:, (3 + u) * C : (4 + u) * C], y_b[u][:, :C])
         for b in range(2):
             nc.vector.tensor_copy(y_slots[:, group_cols(LAST * C, b)], y_last[b][:])
+
+        for repeat in range(2):
+            warm_up(y_b[0][:])
 
         def tokens_of(start, stop):
             return slice(start * GROUP, stop * GROUP)

@@ -195,8 +195,6 @@ def tile_moe_shr_glu_silu_kernel(
         pos_sb = [
             keep.tile([P, T // 16], U16, name=f"pos_sb{r}", align_bytes=DMA_ALIGN) for r in range(2)
         ]
-        nc.sync.dma_start(pos_sb[0][:], pos1)
-        nc.sync.dma_start(pos_sb[1][:], pos2)
 
         gate_columns = keep.tile([P, 2, token_groups], F32, name="gate_columns")
         spread_gates = keep.tile([P, T + GROUP], F32, name="spread_gates")
@@ -375,6 +373,8 @@ def tile_moe_shr_glu_silu_kernel(
             rows = late_raw[:, index * PACK * N : (index + 1) * PACK * N]
             late_rows[expert] = rows.rearrange("p (j n) -> p j n", j=PACK)
             nc.sync.dma_start(late_rows[expert], w2_rows[:, expert])
+        nc.sync.dma_start(pos_sb[0][:], pos1)
+        nc.sync.dma_start(pos_sb[1][:], pos2)
         warm_up(accs1[1][:].rearrange("p t n -> p (t n)"))
         first = rounded_half(vector_copy, raw3[:, 1], 0)
         second = shared_half(raw3[:, 1], 1, LAST_SHARE)

@@ -279,9 +279,6 @@ def tile_moe_shr_glu_silu_kernel(
                 else:
                     hidden.append(quantize_columns(h[:], f"h_codes{len(hidden)}"))
 
-        def warm_up(spent):
-            second_layer(spent, weights_shared, (wide[0][:], wide[1][:]))
-
         for e in range(E):
             slots = slots_of(e)
             eager = e >= EAGER
@@ -375,7 +372,6 @@ def tile_moe_shr_glu_silu_kernel(
             nc.sync.dma_start(late_rows[expert], w2_rows[:, expert])
         nc.sync.dma_start(pos_sb[0][:], pos1)
         nc.sync.dma_start(pos_sb[1][:], pos2)
-        warm_up(accs1[1][:].rearrange("p t n -> p (t n)"))
         first = rounded_half(vector_copy, raw3[:, 1], 0)
         second = shared_half(raw3[:, 1], 1, LAST_SHARE)
         weights = quantize_half(first) + quantize_half(second)
@@ -401,7 +397,6 @@ def tile_moe_shr_glu_silu_kernel(
         for b in range(2):
             h_groups.append(chained([P, GROUP, PACK], BF16))
             multiply(h_groups[b][:], accs3[b], silus[b])
-        warm_up(accs3[0][:].rearrange("p t n -> p (t n)"))
         nc.scalar.copy(y_slots[:, C : 3 * C], y_a[:].rearrange("p e n -> p (e n)"))
         weights_b = quantize_pair(pair, "codes2_pair")
         y_b = []
@@ -419,9 +414,6 @@ def tile_moe_shr_glu_silu_kernel(
             nc.scalar.copy(y_slots[:, (3 + u) * C : (4 + u) * C], y_b[u][:, :C])
         for b in range(2):
             nc.vector.tensor_copy(y_slots[:, group_cols(LAST * C, b)], y_last[b][:])
-
-        for repeat in range(2):
-            warm_up(y_b[0][:])
 
         def tokens_of(start, stop):
             return slice(start * GROUP, stop * GROUP)

from contextlib import ExitStack

import concourse.mybir as mybir
from concourse.masks import make_identity

K, T, E, C, H, N = 1024, 768, 6, 256, 512, 128
FLOPS = 2 * (E * C + T) * (2 * K * H + H * N)

F32 = mybir.dt.float32
BF16 = mybir.dt.bfloat16
I32 = mybir.dt.int32
U32 = mybir.dt.uint32
U16 = mybir.dt.uint16
U8 = mybir.dt.uint8
FP8X4 = mybir.dt.float8_e4m3fn_x4
MULT = mybir.AluOpType.mult
ADD = mybir.AluOpType.add
COPY = mybir.ActivationFunctionType.Copy
SILU = mybir.ActivationFunctionType.Silu

P = 128
PACK = 4
PASSES = K // (P * PACK)
GROUP = 128
LINE = 4
LIST_COLS = C // 16
GATHER = 2 * C
SHARED = E
LAST = E - 1
MX_ALIGN = 64
DMA_ALIGN = 256

EARLY_W2 = 1
SCALAR_ALONE = 2
SHARED_OUT = 2
WHOLE_LOADS = 3
EAGER = 4
STREAM_SHARE = 16
NEXT_SHARE = 24
LAST_SHARE = 40


def tile_moe_shr_glu_silu_kernel(
    tc, x_words, x_scales, w1, w3, w2, gate, offs, pos1, pos2, out
):
    nc = tc.nc

    with ExitStack() as ctx:
        keep = ctx.enter_context(tc.tile_pool(name="keep", bufs=1))
        raw_pool = ctx.enter_context(tc.tile_pool(name="raw", bufs=5))
        chain_pool = ctx.enter_context(tc.tile_pool(name="chain", bufs=40))
        codes_pool = ctx.enter_context(tc.tile_pool(name="codes", bufs=14))
        psum = ctx.enter_context(tc.psum_pool(name="psum", bufs=8))

        def chained(shape, dtype):
            return chain_pool.tile(shape, dtype, name="chained", align_bytes=DMA_ALIGN)

        def codes_tile(width):
            return codes_pool.tile([P, width], U32, name="codes", align_bytes=MX_ALIGN)

        def bank(shape):
            return psum.tile(shape, F32, name="bank")

        def raw_tile():
            return raw_pool.tile([P, PASSES, PACK, H], F32, name="raw", align_bytes=DMA_ALIGN)

        def by_pass(matrix):
            return matrix.rearrange("(o p j) i -> p o j i", o=PASSES, j=PACK)

        def group_cols(first, b):
            return slice(first + b * GROUP, first + (b + 1) * GROUP)

        def round_half(copy, rounded, rows, half, m_range):
            dst = rounded[:].rearrange("p t m j -> p m j t")
            src = rows.rearrange("p j (m t) -> p m j t", t=PACK)
            copy(dst[:, m_range], src[:, m_range, :, 2 * half : 2 * half + 2])

        def rounded_half(copy, rows, half):
            rounded = chained([P, 2, P, PACK], BF16)
            round_half(copy, rounded, rows, half, slice(0, P))
            return rounded

        def shared_half(rows, half, vector_share):
            rounded = chained([P, 2, P, PACK], BF16)
            copies = [(nc.vector.tensor_copy, slice(0, vector_share)), (nc.scalar.copy, slice(vector_share, P))]
            for copy, m_range in copies[:: 1 - 2 * half]:
                round_half(copy, rounded, rows, half, m_range)
            return rounded

        def round_w2(copy, rounded, rows):
            copy(
                rounded.rearrange("p (c u) j -> p c j u", u=LINE),
                rows.rearrange("p j (c u) -> p c j u", u=LINE),
            )

        def rounded_w2(copy, rows):
            rounded = chained([P, N, PACK], BF16)
            round_w2(copy, rounded[:], rows)
            return rounded

        def quantize(values, codes):
            scales = chained([P, codes.shape[1]], U8)
            nc.vector.quantize_mx(out=codes[:].bitcast(FP8X4), scales=scales[:], in_=values)
            return codes[:], scales[:]

        def quantize_half(rounded):
            codes, scales = quantize(rounded[:].rearrange("p t m j -> p (t m j)"), codes_tile(2 * P))
            return [(codes[:, t * P : (t + 1) * P], scales[:, t * P : (t + 1) * P]) for t in range(2)]

        def quantize_columns(values, name):
            codes = keep.tile([P, values.shape[1]], U32, name=name, align_bytes=MX_ALIGN)
            return quantize(values.rearrange("p n t -> p (n t)"), codes)

        def product(acc, weights, tokens, b, o, t, start, stop):
            words, scales, first = tokens
            cols = group_cols(first, b)
            nc.tensor.matmul_mx(
                out=acc[:, t, :],
                lhsT=weights[0].bitcast(FP8X4),
                lhsT_scale=weights[1],
                rhs=words[o][:, cols].bitcast(FP8X4),
                rhs_scale=scales[4 * o : P, cols],
                start=start,
                stop=stop,
            )

        def add_half(accs, rounded, tokens, o, half):
            weights = quantize_half(rounded)
            for b, acc in enumerate(accs):
                for u in range(2):
                    t = 2 * half + u
                    last = o == PASSES - 1 and t == PACK - 1
                    product(acc, weights[u], tokens, b, o, t, o == 0 and t == 0, last)

        def second_layer(y_acc, weights2, hidden):
            nc.tensor.matmul_mx(
                out=y_acc,
                lhsT=weights2[0].bitcast(FP8X4),
                lhsT_scale=weights2[1],
                rhs=hidden[0].bitcast(FP8X4),
                rhs_scale=hidden[1],
                start=True,
                stop=True,
            )

        def silu_of(acc):
            silu = chained([P, GROUP, PACK], F32)
            nc.scalar.activation(silu[:], acc[:].rearrange("p t n -> p n t"), SILU)
            return silu

        def multiply(h, acc, silu):
            nc.vector.tensor_tensor(h, acc[:].rearrange("p t n -> p n t"), silu[:], MULT)

        def multiply_pair(accs, silus):
            h = chained([P, C, PACK], BF16)
            for b in range(2):
                multiply(h[:, group_cols(0, b)], accs[b], silus[b])
            return h

        def banks(count):
            return [bank([P, PACK, GROUP]) for b in range(count)]

        vector_copy, scalar_copy = nc.vector.tensor_copy, nc.scalar.copy

        def gpsimd_round(dst, src):
            nc.gpsimd.tensor_scalar(dst, src, 1.0, 0.0, MULT, ADD)

        token_scales = keep.tile([P, T], U8, name="token_scales", align_bytes=DMA_ALIGN)
        nc.vector.memset(token_scales[:].bitcast(I32), 0)
        all_words = keep.tile([P, PASSES, T], U32, name="all_words", align_bytes=DMA_ALIGN)
        nc.sync.dma_start(
            all_words[:].bitcast(I32),
            x_words.rearrange("o p t r -> p o (t r)").bitcast(I32),
        )
        token_words = [all_words[:, o, :] for o in range(PASSES)]
        offs_sb = keep.tile([P, E * LIST_COLS], U16, name="offs_sb", align_bytes=DMA_ALIGN)
        nc.sync.dma_start(offs_sb[:], offs)

        identity = keep.tile([P, P], F32, name="identity", align_bytes=MX_ALIGN)
        make_identity(nc, identity[:])
        token_groups = T // GROUP
        gate_rows = keep.tile([P, 2, GROUP], F32, name="gate_rows", align_bytes=DMA_ALIGN)
        nc.gpsimd.memset(gate_rows[:], 0.0)

        raw1 = raw_tile()
        for o in range(PASSES):
            nc.sync.dma_start(raw1[:, o], by_pass(w1[SHARED])[:, o])
        for q in range(4):
            nc.sync.dma_start(
                token_scales[32 * q : 32 * q + 4 * PASSES, :].bitcast(I32),
                x_scales[:, 4 * q : 4 * q + 4, :].bitcast(I32),
            )
        raw3 = raw_tile()
        nc.sync.dma_start(raw3[:], by_pass(w3[SHARED]))
        pos_sb = [
            keep.tile([P, T // 16], U16, name=f"pos_sb{r}", align_bytes=DMA_ALIGN) for r in range(2)
        ]

        gate_columns = keep.tile([P, 2, token_groups], F32, name="gate_columns")
        spread_gates = keep.tile([P, T + GROUP], F32, name="spread_gates")
        to_spread = [(0, b) for b in range(token_groups)] + [(1, token_groups - 1)]

        def turn_gate():
            turned = bank([P, 2, P])
            for r in range(2):
                nc.tensor.transpose(turned[:, r], gate_rows[:, r], identity[:])
            nc.scalar.copy(gate_columns[:], turned[:, :, :token_groups])

        def spread_gate(start, stop):
            spread = bank([P, (stop - start) * GROUP])
            for b in range(start, stop):
                r, group = to_spread[b]
                column = gate_columns[:, r, group : group + 1].to_broadcast([P, P])
                nc.tensor.transpose(spread[:, group_cols(0, b - start)], column, identity[:])
            nc.scalar.copy(spread_gates[:, start * GROUP : stop * GROUP], spread[:])

        def gather(g, source, dtype):
            piece = offs_sb[:, g * GATHER // 16 : (g + 1) * GATHER // 16]
            picked = chained([P, GATHER], dtype)
            nc.vector.tensor_copy(picked[:], source.indirect(piece))
            return picked

        sources = [(token_words[0], U32), (token_words[1], U32), (token_scales[:], U8)]
        gathered = {}

        pieces = E * C // GATHER
        to_gather = [(g, kind) for kind in range(3) for g in range(pieces)]

        def gather_next():
            g, kind = to_gather[len(gathered)]
            gathered[g, kind] = gather(g, *sources[kind])

        def slots_of(e):
            g = e * C // GATHER
            return [gathered[g, o] for o in range(PASSES)], gathered[g, PASSES], e * C % GATHER

        y_slots = keep.tile([P, E * C], F32, name="y_slots")
        shared_turned = keep.tile([P, token_groups, N], F32, name="shared_turned")
        w2_rows = w2.rearrange("e (p j) n -> p e j n", j=PACK)

        all_tokens = (token_words, token_scales, 0)
        accs1 = banks(token_groups)
        for index in range(3):
            gather_next()
        for o in range(PASSES):
            for half in range(2):
                rounded = rounded_half(scalar_copy, raw1[:, o], half)
                gather_next()
                add_half(accs1, rounded, all_tokens, o, half)
        rounded = [rounded_half(scalar_copy, raw3[:, 0], half) for half in range(2)]
        rounded.extend(rounded_half(vector_copy, raw3[:, 1], half) for half in range(2))
        silus = [silu_of(acc) for acc in accs1]
        weights = [operand for half in rounded for operand in quantize_half(half)]
        accs3 = []
        for b in range(token_groups):
            accs3.append(bank([P, PACK, GROUP]))
            for o in range(PASSES):
                for t in range(PACK):
                    index = PACK * o + t
                    product(accs3[b], weights[index], all_tokens, b, o, t, index == 0, index == 7)
        for index in range(2):
            gather_next()
        pending = None
        waiting = [(accs3[2 * c : 2 * c + 2], silus[2 * c : 2 * c + 2]) for c in range(T // C)]
        hidden = []

        wide = []

        def quantize_hidden(products):
            for h in products:
                if len(hidden) < 2:
                    if not wide:
                        wide.append(keep.tile([P, 2 * C], U32, name="wide_codes", align_bytes=MX_ALIGN))
                        wide.append(chained([P, 2 * C], U8))
                    codes, scales = [plane[:, len(hidden) * C : (len(hidden) + 1) * C] for plane in wide]
                    values = h[:].rearrange("p n t -> p (n t)")
                    nc.vector.quantize_mx(out=codes.bitcast(FP8X4), scales=scales, in_=values)
                    hidden.append((codes, scales))
                else:
                    hidden.append(quantize_columns(h[:], f"h_codes{len(hidden)}"))

        for e in range(E):
            slots = slots_of(e)
            eager = e >= EAGER
            raw1, raw3 = raw_tile(), raw_tile()
            for raw, matrix in ((raw1, w1[e]), (raw3, w3[e])):
                if e < WHOLE_LOADS:
                    nc.sync.dma_start(raw[:], by_pass(matrix))
                else:
                    for o in range(PASSES):
                        nc.sync.dma_start(raw[:, o], by_pass(matrix)[:, o])
            if e == 0:
                early_w2 = keep.tile([P, 2, PACK, N], F32, name="early_w2", align_bytes=DMA_ALIGN)
                nc.sync.dma_start(early_w2[:], w2_rows[:, 0 : SHARED + 1 : SHARED])
                nc.sync.dma_start(
                    gate_rows[:token_groups], gate[:, 0, :].rearrange("r (b c) -> b r c", c=GROUP)
                )
            if e == 1:
                turn_gate()
            if e == 2:
                spread_gate(0, PACK)
            if e == 3:
                spread_gate(PACK, len(to_spread))
            early = 0 < e <= EARLY_W2
            multiply_step = 0 if (e == 0 or e > EAGER) else 1
            for step in range(2 * PASSES):
                rows = (raw1, raw3)[step // PASSES][:, step % PASSES]
                o = step % PASSES
                if e == LAST and step == 3:
                    break
                alone = 4 * e + step < SCALAR_ALONE
                if alone:
                    first = rounded_half(scalar_copy, rows, 0)
                else:
                    first = rounded_half(vector_copy, rows, 0)
                if e == LAST and step == 2:
                    second = shared_half(rows, 1, NEXT_SHARE)
                elif e > 0:
                    second = shared_half(rows, 1, STREAM_SHARE)
                else:
                    second = rounded_half(scalar_copy, rows, 1)
                if step == 0 and early:
                    rounded2 = rounded_w2(scalar_copy, early_w2[:, e - 1])
                if step == 0 and e == SHARED_OUT:
                    rounded2 = rounded_w2(scalar_copy, early_w2[:, 1])
                if step == multiply_step:
                    products = [multiply_pair(*pair) for pair in waiting]
                if step == multiply_step + 1:
                    quantize_hidden(products)
                if step == 2 and early:
                    y_acc = bank([P, C])
                    second_layer(y_acc[:], quantize_columns(rounded2[:], f"codes2_{e}"), hidden[e + 2])
                if step == 2 and e == SHARED_OUT:
                    weights_shared = quantize_columns(rounded2[:], "codes2_shared")
                    shared_accs = []
                    for start, stop in ((0, PACK), (PACK, token_groups)):
                        shared_accs.append(bank([P, stop - start, N]))
                        for b in range(start, stop):
                            tokens = [plane[:, group_cols(0, b % 2)] for plane in hidden[b // 2]]
                            if b < token_groups - 1:
                                second_layer(shared_accs[-1][:, b - start], tokens, weights_shared)
                            else:
                                second_layer(shared_accs[-1][:, b - start], weights_shared, tokens)
                if pending:
                    add_half(*pending)
                if o == 0:
                    accs = banks(2)
                    if step == 0:
                        accs1 = accs
                    else:
                        accs3 = accs
                add_half(accs, first, slots, o, 0)
                pending = (accs, second, slots, o, 1)
                if eager:
                    add_half(*pending)
                    pending = None
                if step == (2 if e == LAST else 3):
                    silus = [silu_of(acc) for acc in accs1]
                if step == 3 and early:
                    nc.scalar.copy(y_slots[:, (e - 1) * C : e * C], y_acc[:])
                if step == 3 and e == SHARED_OUT:
                    nc.scalar.copy(shared_turned[:, :PACK], shared_accs[0][:])
                    nc.scalar.copy(shared_turned[:, PACK:], shared_accs[1][:])
            waiting = [(accs3, silus)]

        late = list(range(EARLY_W2, E))
        late_raw = raw_tile()[:].rearrange("p o j i -> p (o j i)")
        late_rows = {}
        for index, expert in enumerate(late):
            rows = late_raw[:, index * PACK * N : (index + 1) * PACK * N]
            late_rows[expert] = rows.rearrange("p (j n) -> p j n", j=PACK)
            nc.sync.dma_start(late_rows[expert], w2_rows[:, expert])
        nc.sync.dma_start(pos_sb[0][:], pos1)
        nc.sync.dma_start(pos_sb[1][:], pos2)
        first = rounded_half(vector_copy, raw3[:, 1], 0)
        second = shared_half(raw3[:, 1], 1, LAST_SHARE)
        weights = quantize_half(first) + quantize_half(second)
        for b, order in enumerate(((0, 1, 2, 3), (2, 3, 0, 1))):
            for t in order:
                product(accs3[b], weights[t], slots, b, 1, t, False, t == order[-1])

        def quantize_pair(rounded, name):
            codes, scales = quantize_columns(rounded[:].rearrange("p e n j -> p (e n) j"), name)
            return [(codes[:, u * N : (u + 1) * N], scales[:, u * N : (u + 1) * N]) for u in range(2)]

        pair = chained([P, 2, N, PACK], BF16)
        round_w2(scalar_copy, pair[:, 1], late_rows[1])
        rounded_b = rounded_w2(vector_copy, late_rows[2])
        round_w2(scalar_copy, pair[:, 0], late_rows[3])
        rounded_last = rounded_w2(scalar_copy, late_rows[LAST])
        weights_a = [quantize_columns(pair[:, 1], "codes2_a"), quantize_columns(rounded_b[:], "codes2_b")]
        gpsimd_round(pair[:, 1], late_rows[4].rearrange("p j n -> p n j"))
        y_a = bank([P, 2, C])
        for u in range(2):
            second_layer(y_a[:, u], weights_a[u], hidden[4 + u])
        h_groups = []
        for b in range(2):
            h_groups.append(chained([P, GROUP, PACK], BF16))
            multiply(h_groups[b][:], accs3[b], silus[b])
        nc.scalar.copy(y_slots[:, C : 3 * C], y_a[:].rearrange("p e n -> p (e n)"))
        weights_b = quantize_pair(pair, "codes2_pair")
        y_b = []
        for u in range(2):
            y_b.append(bank([P, 2 * C]))
            second_layer(y_b[u][:, :C], weights_b[u], hidden[6 + u])
        last_hidden = [quantize_columns(h_groups[0][:], "last_h0")]
        weights_last = quantize_columns(rounded_last[:], "codes2_last")
        last_hidden.append(quantize_columns(h_groups[1][:], "last_h1"))
        y_last = []
        for b in range(2):
            y_last.append(bank([P, GROUP]))
            second_layer(y_last[b][:], weights_last, last_hidden[b])
        for u in range(2):
            nc.scalar.copy(y_slots[:, (3 + u) * C : (4 + u) * C], y_b[u][:, :C])
        for b in range(2):
            nc.vector.tensor_copy(y_slots[:, group_cols(LAST * C, b)], y_last[b][:])

        def tokens_of(start, stop):
            return slice(start * GROUP, stop * GROUP)

        def results_at(r, start, stop):
            return y_slots[:].indirect(pos_sb[r][:, start * GROUP // 16 : stop * GROUP // 16])

        def turn(acc, block, start, stop):
            nc.tensor.matmul(acc, block, identity[:], start=start, stop=stop, is_transpose=True)

        def gated_pick(r, start, stop, gates):
            picked = chained([P, (stop - start) * GROUP], F32)
            nc.vector.tensor_tensor(picked[:], results_at(r, start, stop), gates, MULT)
            return picked

        def turned_pick(start, stop):
            picked = chained([P, (stop - start) * GROUP], F32)
            nc.scalar.activation(picked[:], results_at(1, start, stop), COPY)
            turned = []
            for u in range(stop - start):
                turned.append(bank([P, N]))
                turn(turned[u][:], picked[:, group_cols(0, u)], True, True)
            return turned

        ranges = [(0, 2), (2, 4), (4, 5)]
        sums = []
        for start, stop in ranges:
            sums.append(bank([P, stop - start, GROUP]))
            for b in range(start, stop):
                turn(sums[-1][:, b - start], shared_turned[:, b], b == start, False)

        def weigh(index, turned):
            start, stop = ranges[index]
            weighted = chained([P, stop - start, N], F32)
            for b in range(start, stop):
                weight = gate_columns[:, 1, b : b + 1]
                nc.scalar.activation(weighted[:, b - start], turned[b - start][:], COPY, scale=weight)
                turn(sums[index][:, b - start], weighted[:, b - start], False, b == stop - 1)

        def add(first, second):
            total = chained([P, second.shape[1]], F32)
            nc.vector.tensor_tensor(total[:], first, second, ADD)
            return total

        def finish(index, picked):
            total = add(sums[index][:].rearrange("p b n -> p (b n)"), picked)
            nc.sync.dma_start(out[:, tokens_of(*ranges[index])], total[:])

        turned = [turned_pick(*ranges[0])]
        last_picks = [gated_pick(r, 5, 6, spread_gates[:, tokens_of(5 + r, 6 + r)]) for r in range(2)]
        turned.append(turned_pick(*ranges[1]))
        front = gated_pick(0, 0, 4, spread_gates[:, tokens_of(0, 4)])
        turned.append(turned_pick(*ranges[2]))
        weigh(0, turned[0])
        partial = add(shared_turned[:, 5], last_picks[0][:])
        back = gated_pick(0, 4, 5, spread_gates[:, tokens_of(4, 5)])
        weigh(1, turned[1])
        nc.sync.dma_start(out[:, tokens_of(5, 6)], add(partial[:], last_picks[1][:])[:])
        weigh(2, turned[2])
        finish(0, front[:, tokens_of(0, 2)])
        finish(1, front[:, tokens_of(2, 4)])
        finish(2, back[:])
